import numpy as np, ml_dtypes
CORES = [5,29,101,125,133,157,229,253]
N = 8
BF = ml_dtypes.bfloat16
def gentries(a):
    return np.ascontiguousarray(a.reshape(8, 16, -1).transpose(0, 2, 1)).reshape(8, -1)
def gtable(e):
    e = np.asarray(e); return np.ascontiguousarray(e.reshape(8, -1, 16).transpose(0, 2, 1)).reshape(128, -1).astype(np.int32)
C, I, P, R, S, VM, DM = 1280, 128, 24, 4, 2, 40, 15014400
V, W, B = 2 * C, 2 * C + I, I // S
def walk(nx):
    lead = nx.shape[:-1]; full = np.concatenate([nx, np.broadcast_to(V + np.arange(I), lead + (I,))], axis=-1)
    q = [np.broadcast_to(np.arange(I), lead + (I,))]
    for k in range(1, P): q.append(np.take_along_axis(full, q[-1], -1))
    return np.stack(q, axis=-2)
def parts(rng):
    x = np.minimum((256 * rng.random((N, 8, 1, W)) * rng.random((N, 8, 16, W))).astype(np.int64), 255)
    nu = rng.integers(0, 5, (N, 8, 16)); nu[:, :, 5] = np.maximum(nu[:, :, 5], 1)
    nx = I + np.argsort(rng.random((N, 8, V)), axis=-1)
    le = rng.integers(0, 512, (N, 8, 4, C)); vol = rng.integers(1, VM + 1, (N, 8, V))
    lag = np.minimum(np.exp2(13 + 7 * rng.random((N, 8, I))).astype(np.int64), DM)
    return x, nu, nx, le, vol, lag
def pack(x, nu, nx, le, vol, lag):
    return {"x": np.ascontiguousarray(x.reshape(N, 128, W)).astype(np.float32).astype(BF), "nu": np.ascontiguousarray(nu.reshape(N, 128, 1)).astype(np.int32),
            "nx": np.stack([gtable(a) for a in nx]), "le": np.stack([gtable(a.reshape(8, -1)) for a in le]),
            "vol": np.stack([gtable(a) for a in vol]), "lag": np.stack([gtable(a) for a in lag])}
def chains(rng, lens, out, fix, own=()):
    own = np.array(own, np.int64); pool = I + rng.permutation(V - I); pool = pool[~np.isin(pool, own)]; end = np.add.accumulate(lens - 1)
    for i, p in fix:
        e = int(end[i]) - 1; j = int(np.nonzero(pool == p)[0][0]); pool[j] = pool[e]; pool[e] = p
    nx = np.zeros(V, np.int64); nx[own] = own
    for i in range(I):
        s = np.concatenate([[i], pool[end[i] - lens[i] + 1:end[i]], [V + out[i]]]).astype(np.int64); nx[s[:-1]] = s[1:]
    rest = pool[end[-1]:]; nx[rest] = rest[rng.permutation(len(rest))]
    return nx
def setup_inputs(rng):
    return pack(*parts(rng))
def setup_inputs_spread(rng):
    x, nu, nx, le, vol, lag = parts(rng)
    x = np.minimum((np.exp2(8 * rng.random((N, 8, 1, W))) * rng.random((N, 8, 16, W))).astype(np.int64), 255)
    nu = rng.choice(np.array([0, 0, 1, 4]), (N, 8, 16)); nu[:, :, 3] = 4
    le = np.minimum(np.exp2(9 * rng.random((N, 8, 4, C))).astype(np.int64) - 1, 511)
    vol = np.maximum(np.minimum(np.power(float(VM), rng.random((N, 8, V))).astype(np.int64), VM), 1)
    lag = np.maximum(np.minimum(np.power(float(DM), rng.random((N, 8, I))).astype(np.int64), DM), 1)
    return pack(x, nu, nx, le, vol, lag)
def setup_inputs_ends(rng):
    A = np.array([0, 1, I // 2, I - 2, I - 1]); D = np.array([2, 3, I // 2 + 1, I - 4, I - 3])
    o = np.setdiff1d(np.arange(I), np.concatenate([A, D])); row = np.arange(16)[:, None]
    kind = rng.choice(4, (N, 8, 1, W), p=[0.35, 0.15, 0.25, 0.25]); lane = rng.integers(0, 16, (N, 8, 1, W))
    x = np.where(kind == 0, 255, np.where(kind == 1, np.where(row == lane, 254, 255), np.where(kind == 2, 0, 255 * rng.integers(0, 2, (N, 8, 16, W)))))
    nu = 4 * rng.integers(0, 2, (N, 8, 16)); nu[:, :, 0] = 4; nu[:, 0] = 4; nu[:, 7] = 4; nu[:, 1] = 0; nu[:, 2] = 4; nu[:, 2, 15] = 0
    hi = np.array([511, 511, 510, 510])[:, None]; u = rng.random((N, 8, 1, C))
    le = np.where(u < 0.1, hi, np.where(u < 0.2, hi[::-1], np.where(u < 0.3, 511, 511 * rng.integers(0, 2, (N, 8, 4, C)))))
    vol = np.where(rng.random((N, 8, V)) < 0.5, 1, VM); lag = np.where(rng.random((N, 8, I)) < 0.5, 1, DM); nx = np.zeros((N, 8, V), np.int64)
    for r in range(N):
        for g in range(8):
            lens = np.zeros(I, np.int64); lens[A] = P; lens[D] = R + 1; lens[o] = rng.permutation(np.resize(np.array([1, P // 2, P - 1, P, P + 1]), len(o)))
            out = np.zeros(I, np.int64); out[A] = D; out[D] = A; out[o] = rng.permutation(o)
            nx[r, g] = chains(rng, lens, out, [(0, I), (1, I + 1), (I - 2, V - 2), (I - 1, V - 1)])
            q = walk(nx[r, g]); a = q[:, A]; d = q[:R + 1, D]; both = np.concatenate([a.reshape(-1), d.reshape(-1)])
            le[r, g][:, both % C] = 511
            x[r, g][:, both] = 255; x[r, g][:, V + A] = 255; x[r, g][:, V + D] = 255
            mix = 255 * rng.integers(0, 2, (16, 5)); mix[0] = 255; mix[15] = 0; x[r, g][:, d[1]] = mix
            vol[r, g, a] = VM; vol[r, g, a[1, 1]] = VM - 1
            vol[r, g, a[1:, 2:4]] = np.where(rng.random((P - 1, 2)) < 0.5, 1, VM); vol[r, g, a[1, 2:4]] = 1
            tot = 255 * int(np.sum(nu[r, g])) * np.sum(vol[r, g, a[1:]], axis=0)
            lag[r, g, D] = 1; lag[r, g, A] = DM; lag[r, g, A[2]] = max(int(tot[2]), 1); lag[r, g, A[3]] = min(max(int(tot[3]) + 1, 1), DM)
    return pack(x, nu, nx, le, vol, lag)
def setup_inputs_corners(rng):
    x, nu, nx, le, vol, lag = parts(rng); ar = np.arange(I); m = V // I
    vol = rng.choice(np.array([1, 2, VM - 1, VM]), (N, 8, V)); stay = np.array([0, 511, 511, 0])[:, None]
    for r in range(N):
        for g in range(8):
            t = (g + r) % 8; lens = None
            if t == 0: le[r, g] = stay; lens = rng.permutation(np.resize(np.array([1, 2, P - 1, P, P + 1]), I))
            if t == 1: le[r, g] = 511 - stay
            if t == 2: le[r, g] = 0; lens = np.ones(I, np.int64); lens[rng.integers(0, I)] = V - I + 1
            if t == 3: le[r, g] = stay; lens = rng.permutation(np.resize(np.array([1, P - 1]), I))
            if t == 4: le[r, g] = 511; lens = rng.permutation(np.resize(np.array([m - 1, m + 1]), I))
            if t == 5: lag[r, g] = DM; vol[r, g] = 1
            if t == 6: lag[r, g] = 1; vol[r, g] = VM; nu[r, g] = 0; nu[r, g, rng.integers(0, 16)] = 4
            if t == 7:
                e = rng.integers(-100, 101, (7, W)); nu[r, g] = 4; nu[r, g, 0] = 1
                x[r, g, 0] = 128 + rng.integers(0, 2, W); x[r, g, 1:15:2] = 100 + e; x[r, g, 2:15:2] = 100 - e; x[r, g, 15] = 100
                le[r, g] = np.array([511, 511, 510, 510])[:, None]
            if lens is not None:
                nx[r, g] = chains(rng, lens, rng.permutation(I), []); q = walk(nx[r, g])
                if t == 3:
                    off = np.ones(W, bool); off[q.reshape(-1)] = False; p = np.nonzero(off[:V])[0]; nx[r, g, p] = p
                c = np.sum(nu[r, g][:, None] * x[r, g], axis=0); c[:V] = c[:V] * vol[r, g]; c[V:] = 0
                T = np.add.accumulate(c[q], axis=0); k = rng.integers(1, P, I); j = (rng.random(I) * k).astype(np.int64)
                lag[r, g] = np.maximum(np.minimum(T[k, ar] - T[j, ar] + rng.choice(np.array([0, 0, 0, 1]), I), DM), 1)
    return pack(x, nu, nx, le, vol, lag)
def setup_inputs_calm(rng):
    x, nu, nx, le, vol, lag = parts(rng)
    x = (np.argsort(rng.random((N, 8, 16, W)), axis=2) < rng.integers(0, 4, (N, 8, 1, W))).astype(np.int64)
    nu = rng.integers(0, 3, (N, 8, 16)); nu[:, ::2] = 1; nu[:, :, 7] = 1
    le = rng.integers(0, 4, (N, 8, 4, C)); vol = rng.integers(1, 3, (N, 8, V)); vol[:, 0] = 1; vol[:, 5] = 1
    lag = rng.integers(1, 7, (N, 8, I)); t = (np.arange(N)[:, None] + np.arange(8)[None, :]) % 4
    lag = np.where(t[:, :, None] < 3, t[:, :, None] + 1, lag)
    return pack(x, nu, nx, le, vol, lag)
def setup_inputs_fine(rng):
    x, nu, nx, le, vol, lag = parts(rng); ar = np.arange(I); stay = np.array([0, 511, 511, 0])[:, None]; turn = int(rng.integers(0, 4))
    forms = np.array([[255] * 16, [255] * 13 + [182, 0, 0], [255] * 8 + [0] * 8])
    pats = np.array([[511, 511, 510, 511], [511, 510, 511, 511], [511, 511, 505, 504], [504, 505, 511, 511], [510, 509, 511, 511], [511, 511, 509, 510]]).T
    for g in range(8):
        t = (g + turn) % 4; lane = int(rng.integers(0, 16)); others = np.delete(np.arange(16), lane); nu[:, g] = 4
        if t == 0 or t == 2: nu[:, g, lane] = 1
        far = np.append(rng.permutation(I - 1)[:I // 2 - 1], I - 1); near = np.setdiff1d(ar, far); n = len(far)
        for r in range(N):
            if t == 0 or t == 2: x[r, g][others] = 255 - np.argsort(rng.random((15, W)), axis=0)
            if t == 0:
                x[r, g, lane] = 255; le[r, g] = stay; vol[r, g] = rng.integers(VM - 3, VM + 1, V)
                c = np.zeros(W, np.int64); c[:V] = 15135 * vol[r, g]; q = walk(nx[r, g]); T = np.add.accumulate(c[q], axis=0)
                k = np.maximum(np.argmax(rng.random((P, I)) * ((T >= 2 ** 23) & (q < V)), axis=0), 1); j = np.maximum(k - 1 - rng.integers(0, 3, I), 0)
                lag[r, g] = np.maximum(np.minimum(T[k, ar] - T[j, ar] + rng.integers(0, 2, I), DM), 1)
            if t == 1:
                lens = rng.integers(1, 4, I); lens[far] = P; out = np.zeros(I, np.int64); out[far] = rng.permutation(far); out[near] = rng.permutation(near)
                nx[r, g] = chains(rng, lens, out, [], C + far); a = walk(nx[r, g])[:, far]
                le[r, g] = stay; le[r, g][:, far] = np.array([0, 0, 511, 511])[:, None]
                x[r, g][:, a[1:].reshape(-1)] = 255; x[r, g][:, far] = rng.integers(100, 255, (16, n)); x[r, g][:, C + far] = rng.integers(100, 255, (16, n))
                x[r, g][:, V + far] = rng.integers(0, 61, (16, n)); vol[r, g, a[1:]] = VM
                less = rng.random(n) < 0.5; less[0] = True; e = a[rng.integers(1, P, n), np.arange(n)]; x[r, g][rng.integers(0, 16, n)[less], e[less]] = 254
                c = 4 * np.sum(x[r, g], axis=0); tot = VM * np.sum(c[a[1:]], axis=0); u = rng.random(n); u[0] = 0
                lag[r, g, far] = np.where(u < 0.5, DM, np.minimum(tot + (u < 0.75), DM))
            if t == 2:
                x[r, g, lane] = 254 + rng.integers(0, 2, W); a = rng.integers(501, 512, C); b = rng.integers(501, 512, C)
                le[r, g] = np.where(rng.random(C) < 0.5, np.stack([a, b, a - 1, b - 1]), np.stack([a - 1, b - 1, a, b]))
            if t == 3:
                z = rng.choice(3, W, p=[0.45, 0.3, 0.25]); x[r, g] = np.take_along_axis(forms[z].T, np.argsort(rng.random((16, W)), axis=0), 0)
                le[r, g] = pats[:, rng.integers(0, 6, C)]; shut = I + rng.permutation(C - I)[:(C - I) // 4]; le[r, g][:, shut] = np.array([511, 511, 0, 0])[:, None]
                both = np.concatenate([shut, C + shut]); nx[r, g, np.setdiff1d(np.arange(V), both)] = rng.permutation(np.setdiff1d(I + np.arange(V), both))
                sw = rng.random(len(shut)) < 0.5; nx[r, g, shut] = np.where(sw, C + shut, shut); nx[r, g, C + shut] = np.where(sw, shut, C + shut)
    return pack(x, nu, nx, le, vol, lag)
def check_inputs(d):
    bad = []
    for k, lo, hi in (("x", 0, 255), ("nu", 0, 4), ("nx", I, W - 1), ("le", 0, 511), ("vol", 1, VM), ("lag", 1, DM)):
        v = np.asarray(d[k]).astype(np.float64)
        if not bool(np.all((v >= lo) & (v <= hi))): bad.append("range of " + k)
    v = np.asarray(d["x"]).astype(np.float64)
    if not bool(np.all(v == np.floor(v))): bad.append("whole numbers of x")
    if not all(bool(np.all(np.sort(gentries(a), axis=1) == np.arange(I, W))) for a in d["nx"]): bad.append("nx: each number once in each group")
    return bad
def reference(x, nu, nx, le, vol, lag):
    X = x.astype(np.float32).astype(np.int64).reshape(N, 8, 16, W); w = nu.astype(np.int64).reshape(N, 8, 16, 1)
    nxt = np.stack([gentries(a) for a in nx]).astype(np.int64); ln = np.stack([gentries(a) for a in le]).astype(np.int64).reshape(N, 8, 4, C)
    vo = np.stack([gentries(a) for a in vol]).astype(np.int64); vo = np.concatenate([vo, np.zeros((N, 8, I), np.int64)], axis=2)
    de = np.stack([gentries(a) for a in lag]).astype(np.int64)
    for rnd in range(R):
        mu = np.add.reduce(w * X, axis=2)
        ex = mu.copy(); come = np.zeros((N, 8, 16, I), np.int64)
        for r in range(N):
            for s in range(S):
                ex[r, :, V + s * B:V + (s + 1) * B] = mu[(r + 1 + s) % N, :, s * B:(s + 1) * B]
                come[r, :, :, s * B:(s + 1) * B] = X[(r - 1 - s) % N, :, :, V + s * B:V + (s + 1) * B]
        m = np.take_along_axis(ex, nxt, 2); m0, m1 = m[:, :, :C], m[:, :, C:]
        cross = ln[:, :, 1] * m1 + ln[:, :, 2] * m0 < ln[:, :, 0] * m0 + ln[:, :, 3] * m1
        a, b = nxt[:, :, :C], nxt[:, :, C:]
        nxt = np.concatenate([np.where(cross, b, a), np.where(cross, a, b)], axis=2)
        q = walk(nxt)
        T = np.add.accumulate(np.take_along_axis(vo * mu, q.reshape(N, 8, P * I), 2).reshape(N, 8, P, I), axis=2)
        src = np.zeros((N, 8, P, I), np.int64) + (W + np.arange(I))
        for k in range(1, P):
            for j in range(k):
                src[:, :, k] = np.where(T[:, :, k] - T[:, :, j] >= de, q[:, :, j], src[:, :, k])
            src[:, :, k] = np.where(q[:, :, k] >= V, src[:, :, k - 1], src[:, :, k])
        new = np.take_along_axis(np.concatenate([X, come], axis=3), src.reshape(N, 8, 1, P * I), 3)
        np.put_along_axis(X, q.reshape(N, 8, 1, P * I), new, 3)
    return {"y": X.reshape(N, 128, W).astype(np.float32).astype(BF), "yn": np.stack([gtable(a) for a in nxt]).astype(np.float32)}

@@ -1,0 +1,537 @@
+from concourse.bass import DstId, RemoteDMATransfer
+from concourse.mybir import AluOpType as Op
+from concourse.mybir import ActivationFunctionType as Act
+
+R = 4
+PW = 168
+ROW = 32 * PW
+XP0 = 2816
+XW = XP0 + 23 * 128
+CB = 8192
+SV = 68
+PK = 3072
+SMALL = 2624
+
+F, H, I, U = "float32", "bfloat16", "int32", "uint16"
+SCRATCH = {
+    "xn": ("sbuf", [128, 2688], H), "xa": ("sbuf", [128, XW], H), "xb": ("sbuf", [128, XW], H),
+    "aw": ("sbuf", [128, 128 + 23 * 128], H), "arr": ("sbuf", [128, R * 128], H),
+    "ew": ("sbuf", [128, 144], H), "pk": ("sbuf", [128, 144], H), "gb": ("sbuf", [128, 2560], H), "gb2": ("sbuf", [128, 2560], H),
+    "rl": ("sbuf", [128, R * 64], H), "rb": ("sbuf", [128, 72], H),
+    "win": ("sbuf", [128, ROW], F), "pos": ("sbuf", [128, ROW], F), "pos2": ("sbuf", [128, ROW], F),
+    "vh": ("sbuf", [128, 14 * 128], F), "vs": ("sbuf", [128, 11 * 128], F), "dfl": ("sbuf", [128, 2560], F),
+    "rep": ("sbuf", [128, 256], F), "tte": ("sbuf", [128, 44, 32], F), "tto": ("sbuf", [128, 88, 16], F),
+    "ql": ("sbuf", [128, 192], U), "xl": ("sbuf", [128, 184], U), "sp": ("sbuf", [128, 184], U), "piu": ("sbuf", [128, PW], U),
+    "nxu": ("sbuf", [128, 160], U), "npu": ("sbuf", [128, 160], U), "eiu": ("sbuf", [128, 160], U),
+    "nui": ("sbuf", [128, 4], I), "nxi": ("sbuf", [128, 160], I), "lei": ("sbuf", [128, 320], I),
+    "voi": ("sbuf", [128, 160], I), "lgi": ("sbuf", [128, 8], I), "ti1": ("sbuf", [128, 160], I), "ti2": ("sbuf", [128, 160], I),
+    "pci": ("sbuf", [128, 8], I), "col": ("sbuf", [128, 24], F), "ci": ("sbuf", [128, PW], F), "mg": ("sbuf", [128, 128], F),
+    "oti": ("sbuf", [128, 184], F), "ot": ("sbuf", [128, 184], H),
+    "z": ("sbuf", [128, 144], H), "znu": ("sbuf", [128, 144], H), "z1": ("sbuf", [128, 144], H), "zd": ("sbuf", [128, 144], H),
+    "zs": ("sbuf", [128, 144], H), "bnu": ("sbuf", [128, 128], H), "ib": ("sbuf", [128, 128], H), "i128": ("sbuf", [128, 128], H),
+    "am": ("sbuf", [128, 5 * 128], F),
+    "nxl": ("sbuf", [128, PW], F), "wl": ("sbuf", [128, PW], F), "bs": ("sbuf", [128, 160], F), "idc": ("sbuf", [128, 160], F),
+    "sn": ("sbuf", [128, 184], I), "sm": ("sbuf", [128, 184], F), "pg": ("psum", [128, 64, 4, 2], F), "vl": ("sbuf", [128, PW], F),
+    "rs": ("sbuf", [128, PW], F), "idn": ("sbuf", [128, 160], F), "p1": ("sbuf", [128, PW], F), "p2": ("sbuf", [128, PW], F),
+    "pm": ("sbuf", [128, PW], F), "dd": ("sbuf", [128, 160], F), "d1": ("sbuf", [128, 160], F), "vv": ("sbuf", [128, 160], F),
+    "vp": ("sbuf", [128, 160], F), "pp": ("sbuf", [128, 160], F), "wv": ("sbuf", [128, 160], F), "dfp": ("sbuf", [128, 160], F),
+    "ea": ("sbuf", [128, 160], F), "eb": ("sbuf", [128, 160], F), "m1": ("sbuf", [128, 160], F), "m2": ("sbuf", [128, 160], F),
+    "h": ("sbuf", [128, 10 * 80], F), "e01": ("sbuf", [128, 16, 2], F), "lgx": ("sbuf", [128, 192], F), "uu": ("sbuf", [128, 192], F),
+    "one": ("sbuf", [128, 24], F), "cnd": ("sbuf", [128, 23 * 184], H), "tb": ("sbuf", [128, 128], H), "tf": ("sbuf", [128, 128], F),
+    "yo": ("sbuf", [128, 160], F),
+    "mu": ("psum", [128, 512], F), "mu1": ("psum", [128, 512], F), "mud": ("psum", [128, 512], F),
+    "pf": ("psum", [128, 32, 4, 2, 2], F), "pt": ("psum", [128, 512], F), "cnt": ("psum", [128, 512], F),
+}
+SEMAPHORES = (["cv", "ca", "cp", "cg", "ld0", "ld1", "ld2", "ld3", "ld4", "dw", "dp", "dr", "dr2", "dy", "back", "sb", "rback", "rsb"]
+              + ["a%d" % t for t in range(R)] + ["s%d" % t for t in range(R)]
+              + ["ra%d" % t for t in range(R)] + ["rs%d" % t for t in range(R)])
+
+
+def _bits(engines):
+    m = 0
+    for e in engines:
+        m |= 1 << e
+    return m
+
+
+def _relay(src, dst, T, topo, nth):
+    if topo.may_write(src, dst):
+        return None
+    c = [k for k in topo.cores_of(src) if T.rank_of(k) is None and topo.may_write(k, dst)]
+    c.sort(key=lambda k: (topo.die(k) != topo.die(src), k))
+    return c[nth]
+
+
+def _relay_program(g, core, T, topo):
+    n = len(T.cores)
+    for r in range(n):
+        src = T.cores[r]
+        for step in (1, 2):
+            dst = T.cores[(r - step) % n]
+            if _relay(src, dst, T, topo, 1) == core:
+                eng = topo.engines(core, dst)[:8]
+                rid, pid = topo.addr(dst, core)
+                g.wait_ge(T.sem.rback, 8)
+                g.remote_dma(T.ew[:, 72 * (step - 1):72 * step], T.rb[:, :], T.sem.back, T.sem.rsb, pid, rid, _bits(eng))
+                g.wait_ge(T.sem.rsb, 8)
+            dst = T.cores[(r + step) % n]
+            if _relay(src, dst, T, topo, 0) == core:
+                eng = topo.engines(core, dst)[:8]
+                rid, pid = topo.addr(dst, core)
+                for t in range(R):
+                    g.wait_ge(T.sem["ra%d" % t], 8)
+                    c0 = 128 * t + 64 * (step - 1)
+                    g.remote_dma(T.arr[:, c0:c0 + 64], T.rl[:, 64 * t:64 * t + 64], T.sem["a%d" % t], T.sem["rs%d" % t], pid, rid, _bits(eng))
+                for t in range(R):
+                    g.wait_ge(T.sem["rs%d" % t], 8)
+
+
+def rank_program(g, core, T, topo):
+    rank = T.rank_of(core)
+    if rank is None:
+        _relay_program(g, core, T, topo)
+        return
+    n = len(T.cores)
+    Q = {"v": g.vector, "a": g.scalar, "p": g.tensor, "g": g, "s": g.sync}
+    V, A, P = g.vector, g.scalar, g.tensor
+    CS = {"v": "cv", "a": "ca", "p": "cp", "g": "cg"}
+    cnt, know, lastw, readers, batch = {}, {q: {} for q in Q}, {}, {}, {}
+
+    def need(q, ev, raw):
+        sem, val, clock, eng = ev
+        if eng == q == "p" and not raw:
+            return
+        if isinstance(val, list):
+            if not val:
+                val.append(cnt[sem])
+            val = val[0]
+        if know[q].get(sem, 0) < val:
+            Q[q].wait_ge(T.sem[sem], val)
+            know[q][sem] = val
+        for s, v in clock.items():
+            if know[q].get(s, 0) < v:
+                know[q][s] = v
+
+    def before(q, rd, wr, compute):
+        for x in rd:
+            if x in lastw:
+                need(q, lastw[x], True)
+        for x in wr:
+            if x in lastw:
+                need(q, lastw[x], not compute)
+            for ev in readers.get(x, []):
+                need(q, ev, not compute)
+
+    def after(ev, rd, wr):
+        for x in rd:
+            readers.setdefault(x, []).append(ev)
+        for x in wr:
+            lastw[x] = ev
+            readers[x] = []
+
+    def op(q, fns, rd, wr):
+        rd, wr = rd.split(), wr.split()
+        before(q, rd, wr, True)
+        ins = None
+        for f in (fns if isinstance(fns, list) else [fns]):
+            ins = f()
+        s = CS[q]
+        cnt[s] = cnt.get(s, 0) + 1
+        ins.then_inc(T.sem[s], 1)
+        after((s, cnt[s], dict(know[q]), q), rd, wr)
+
+    def dma(q, out, in_, sem, rd, wr):
+        rd, wr = rd.split(), wr.split()
+        before(q, rd, wr, False)
+        Q[q].dma_start(out, in_).then_inc(T.sem[sem], 16)
+        cnt[sem] = cnt.get(sem, 0) + 16
+        if batch.get(sem, [0]):
+            batch[sem] = []
+        after((sem, batch[sem], dict(know[q]), None), rd, wr)
+
+    def landed(sem, regions):
+        cnt[sem] = 16
+        for x in regions.split():
+            lastw[x] = (sem, 16, {}, None)
+
+    def send(dsts, nth, srcs, outs, relay_out, rsem, relay_sem, lsem, rd):
+        rd = rd.split()
+        before("g", rd, [], False)
+        used, trs = [], []
+        order = sorted(range(2), key=lambda j: _relay(core, dsts[j], T, topo, nth) is not None)
+        for j in order:
+            rel = _relay(core, dsts[j], T, topo, nth)
+            to = dsts[j] if rel is None else rel
+            eng = [e for e in topo.engines(core, to) if e not in used][:8]
+            used += eng
+            rid, pid = topo.addr(to, core)
+            trs.append(RemoteDMATransfer(dst_ids=[DstId(rid=rid, pnc=pid)], dma_engine_mask=_bits(eng),
+                                         remote_sem=T.sem[rsem if rel is None else relay_sem],
+                                         src=srcs[j], dst=outs[j] if rel is None else relay_out))
+        g.remote_dma_fused(trs, local_sem=T.sem[lsem])
+        cnt[lsem] = 16
+        after((lsem, 16, dict(know["g"]), None), rd, [])
+
+    def tt(out, a, b, o, rd, wr):
+        op("v", lambda: V.tensor_tensor(out, a, b, o), rd, wr)
+
+    def ts(out, a, s1, o1, rd, wr, s2=None, o2=None):
+        if o2 is None:
+            op("v", lambda: V.tensor_scalar(out, a, s1, None, o1), rd, wr)
+        else:
+            op("v", lambda: V.tensor_scalar(out, a, s1, s2, o1, o2), rd, wr)
+
+    def cp(q, out, in_, rd, wr):
+        if q == "v":
+            op("v", lambda: V.tensor_copy(out, in_), rd, wr)
+        else:
+            op("a", lambda: A.activation(out, in_, Act.Copy), rd, wr)
+
+    def fill(ap, c, wr):
+        op("v", lambda: V.memset(ap, c), "", wr)
+
+    def iota(out, pattern, base, cm, wr):
+        op("g", lambda: g.iota(out, pattern, base, cm, allow_small_or_imprecise_dtypes=True), "", wr)
+
+    def spread(out, zt, src, c0, c1, rd, wr):
+        op("p", [(lambda i=i: P.matmul(out[:, c0:c1], zt[:, 15 - i:143 - i], src[:, 16 * c0 + i:16 * c1:16], i == 0, i == 15))
+                 for i in range(16)], rd, wr)
+
+    def col(j):
+        return T.col[:, j:j + 1]
+
+    def half(j):
+        return T.h[:, 80 * j:80 * j + 80]
+
+    a_, b_ = slice(0, 80), slice(80, 160)
+    X = [T.xa, T.xb]
+    XN = ["xa", "xb"]
+    fwd = [T.cores[(rank + 1) % n], T.cores[(rank + 2) % n]]
+    bwd = [T.cores[(rank - 1) % n], T.cores[(rank - 2) % n]]
+    landed("back", "ew")
+    for t in range(R):
+        landed("a%d" % t, "arr%d" % t)
+
+    dma("s", T.nui[:, 0:1], T.nu[:, :], "ld0", "", "nui")
+    dma("a", T.xa[:, 2560:2688], T.x[:, 0:128], "ld0", "", "xai")
+    dma("s", T.voi[:, :], T.vol[:, :], "ld1", "", "voi")
+    dma("a", T.nxi[:, :], T.nx[:, :], "ld1", "", "nxi")
+    dma("a", T.xa[:, 2688:2816], T.x[:, 2560:2688], "ld4", "", "xao")
+    dma("s", T.xn[:, :], T.x[:, :], "ld2", "", "xn0 xn1")
+    dma("a", T.lei[:, :], T.le[:, :], "ld3", "", "lei")
+    dma("s", T.lgi[:, :], T.lag[:, :], "ld3", "", "lgi")
+
+    op("g", lambda: g.iota(T.pci[:, 0:1], [[1, 1]], 0, 1), "", "pci0")
+    iota(T.mg[:, :], [[1, 8], [0, 16]], 0, 0, "mg")
+    iota(T.ci[:, :], [[1, PW]], 0, 0, "ci")
+    iota(T.win[:, 4200:ROW], [[0, ROW - 4200]], 0, 0, "win3")
+    fill(T.win[:, 0:1400], 0.0, "win0")
+    cp("a", T.win[:, 1400:2800], T.win[:, 0:1400], "win0", "win1")
+    cp("a", T.win[:, 2800:4200], T.win[:, 0:1400], "win0", "win2")
+    fill(T.pk[:, :], 0.0, "pk")
+    fill(T.z[:, :], 0.0, "z")
+    ts(T.pci[:, 1:2], T.pci[:, 0:1], 15, Op.bitwise_and, "pci0", "pci1")
+    ts(T.pci[:, 2:3], T.pci[:, 0:1], 4, Op.logical_shift_right, "pci0", "pci2")
+    ts(T.pci[:, 3:4], T.pci[:, 0:1], 16, Op.bitwise_and, "pci0", "pci3")
+    ts(T.pci[:, 4:5], T.pci[:, 0:1], 31, Op.bitwise_and, "pci0", "pci4")
+    cP, cI, cG, cH16, cI32, cOD, cS0, cSG, cNU, cH, cNH, cPP, cPM, cPI, cHO, cND = range(16)
+    cp("v", T.col[:, 0:5], T.pci[:, 0:5], "pci0 pci1 pci2 pci3 pci4", "c0")
+    ts(col(cOD), col(cI), 1.0, Op.is_equal, "c0", "cod")
+    ts(col(cS0), col(cI), 0.0, Op.is_equal, "c0", "cs0")
+    tt(col(cSG), col(cS0), col(cOD), Op.subtract, "cod cs0", "csg")
+
+    cp("v", col(cNU), T.nui[:, 0:1], "nui", "cnu")
+    ts(T.bnu[:, :], T.mg[:, :], col(cG), Op.is_equal, "mg c0 cnu", "bnu", col(cNU), Op.mult)
+    cp("v", T.pk[:, 0:1], col(cNU), "cnu pk", "pk0")
+    cp("v", T.pk[:, 136:137], col(cNU), "cnu pk", "pk1")
+    op("p", lambda: P.matmul(T.cnt[:, 0:128], T.bnu[:, :], T.xa[:, 2560:2688], True, True), "bnu xai", "cnt")
+    ts(T.tb[:, :], T.cnt[:, 0:128], col(cSG), Op.mult, "cnt csg", "tb")
+    ts(T.tf[:, :], T.cnt[:, 0:128], col(cOD), Op.mult, "cnt cod", "tf")
+    tt(T.pk[:, 8:136], T.tf[:, :], T.tb[:, :], Op.add, "tb tf pk", "pk2")
+    send(bwd, 1, [T.pk[:, 0:72], T.pk[:, 72:144]], [T.ew[:, 0:72], T.ew[:, 72:144]], T.rb[:, :], "back", "rback", "sb", "pk pk0 pk1 pk2")
+
+    def send_fwd(t):
+        x = X[t % 2]
+        send(fwd, 0, [x[:, 2688:2752], x[:, 2752:2816]], [T.arr[:, 128 * t:128 * t + 64], T.arr[:, 128 * t + 64:128 * t + 128]],
+             T.rl[:, 64 * t:64 * t + 64], "a%d" % t, "ra%d" % t, "s%d" % t, XN[t % 2] + "o")
+    send_fwd(0)
+    iota(T.vh[:, 0:128], [[1, 128]], XP0 + CB, 0, "vh0")
+    iota(T.oti[:, :], [[0, 23], [16, 8]], 0, 0, "oti")
+    iota(T.vh[:, 128:13 * 128], [[256, 12], [1, 128]], XP0 + CB + 128, 0, "vh1")
+    iota(T.vh[:, 13 * 128:14 * 128], [[1, 128]], XP0 + 22 * 128 - SMALL, 0, "vh2")
+    for j in range(11):
+        iota(T.vs[:, 128 * j:128 * j + 128], [[32, 4], [0, 2], [1, 16]], XP0 + CB + 256 * (j + 1), 0, "vs%d" % j)
+    iota(T.dfl[:, :], [[1, 2560]], CB + 128, 0, "dfl")
+
+    fill(T.vl[:, 160:164], 0.0, "vl1")
+    fill(T.vl[:, 164:168], -1.0, "vl2")
+    cp("v", T.vl[:, 0:160], T.voi[:, :], "voi", "vl0")
+    dma("s", T.win[0::32, :], T.vl[:, :], "dw", "vl0 vl1 vl2", "win0 win1 win2 win3 wf0")
+    dma("s", T.win[16::32, :], T.vl[:, :], "dw", "vl0 vl1 vl2", "wf1")
+    cp("v", T.nxu[:, :], T.nxi[:, :], "nxi", "nxu")
+    ts(T.z[:, 15:143:16], T.ci[:, 0:8], col(cG), Op.is_equal, "ci c0 z", "z")
+    ts(T.ti1[:, :], T.nxi[:, :], 4, Op.logical_shift_right, "nxi", "ti1")
+    ts(T.ti2[:, :], T.nxi[:, :], 15, Op.bitwise_and, "nxi", "ti2")
+    ts(col(cHO), col(cH16), float(PW), Op.mult, "c0", "cho")
+    ts(col(cPI), col(cI32), float(PW), Op.mult, "c0", "cpi")
+    ts(T.znu[:, :], T.z[:, :], col(cNU), Op.mult, "z cnu", "znu")
+    ts(T.zs[:, :], T.z[:, :], col(cS0), Op.mult, "z cs0", "zs")
+    ts(T.pm[:, 0:160], T.ti2[:, :], float(PW), Op.mult, "ti2 cho", "pm", col(cHO), Op.add)
+    tt(T.p1[:, 0:160], T.pm[:, 0:160], T.ti1[:, :], Op.add, "pm ti1", "p1")
+    cp("v", T.npu[:, :], T.p1[:, 0:160], "p1", "npu")
+    ts(T.eiu[:, :], T.nxi[:, :], 2552.0, Op.subtract, "nxi", "eiu", 7.0, Op.max)
+
+    def four(out, name, window, offs, rd):
+        for j in range(4):
+            cp("va"[j % 2], out[:, 640 * j:640 * j + 640], window.indirect(offs[:, 40 * j:40 * j + 40]), rd, "%s%d" % (name, j))
+    four(T.xa, "xas", T.xn[:, :], T.nxu, "xn0 xn1 nxu")
+    spread(T.mu, T.znu, T.xa, 0, 80, "znu xas0 xas1", "mu")
+    spread(T.mu, T.znu, T.xa, 80, 168, "znu xas2 xas3 xai", "mu")
+    tt(T.dd[:, a_], T.lei[:, 160:240], T.lei[:, 0:80], Op.subtract, "lei", "dd")
+    tt(T.dd[:, b_], T.lei[:, 240:320], T.lei[:, 80:160], Op.subtract, "lei", "dd")
+    ts(T.idn[:, :], T.ci[:, 0:160], 16.0, Op.mult, "ci c0", "idn", col(cI), Op.add)
+    ts(T.nxl[:, 160:168], T.ci[:, 160:168], col(cPI), Op.add, "ci cpi", "nxo", float(PK), Op.mult)
+    ts(T.p1[:, 0:160], T.p1[:, 0:160], float(PK), Op.mult, "p1", "p1")
+    ts(T.idc[:, :], T.idn[:, :], float(CB), Op.add, "idn", "idc")
+    tt(T.bs[:, :], T.p1[:, 0:160], T.idn[:, :], Op.add, "p1 idn", "ba bb")
+    ts(T.ql[:, 0:8], T.ci[:, 0:8], col(cPI), Op.add, "ci cpi", "ql0")
+    fill(T.wl[:, 160:168], 0.0, "wo")
+    fill(T.rs[:, 0:160], 0.0, "rs0")
+    ts(T.rs[:, 160:168], T.idn[:, 0:8], float(2688 - SMALL), Op.add, "idn", "rs1")
+    WALL = "win0 win1 win2 win3 wf0 wf1 wf2 wf3"
+    four(T.gb, "gb", T.win[:, :], T.npu, WALL + " npu")
+    spread(T.mu1, T.zs, T.gb, 0, 80, "zs gb0 gb1", "mu1")
+    spread(T.mu1, T.zs, T.gb, 80, 160, "zs gb2 gb3", "mu1")
+    for buf, nm, sem in ((T.pos, "pos", "dr"), (T.pos2, "pos2", "dr2")):
+        dma("s", buf[0::32, :], T.rs[:, :], sem, "rs0 rs1", nm + "r0")
+        dma("s", buf[16::32, :], T.rs[:, :], sem, "rs0 rs1", nm + "r1")
+    ts(col(cH), col(cH16), 1.0 / 16, Op.mult, "c0", "ch")
+    ts(col(cNH), col(cH16), 0.0, Op.is_equal, "c0", "cnh")
+    ts(col(cPP), col(cP), 16.0, Op.add, "c0", "cpp")
+    ts(col(cPM), col(cP), -16.0, Op.add, "c0", "cpm")
+    cp("v", T.lgx[:, 0:8], T.lgi[:, :], "lgi", "lgx")
+    for w0, w1 in ((8, 16), (16, 32), (32, 64), (64, 128), (128, 192)):
+        cp("a", T.lgx[:, w0:w1], T.lgx[:, 0:w1 - w0], "lgx", "lgx")
+    fill(T.one[:, :], 1.0, "one")
+    ts(T.e01[:, 0:8, 0], T.idn[:, 0:8], 2560.0, Op.add, "idn", "e0s")
+    ts(T.ot[:, :], T.oti[:, :], col(cI), Op.add, "oti c0", "ot")
+    am = [T.am[:, 128 * j:128 * j + 128] for j in range(5)]
+    c128 = T.ci[:, 0:128]
+    ts(am[0], c128, col(cP), Op.is_equal, "ci c0 cnh", "am0", col(cNH), Op.mult)
+    ts(am[1], c128, col(cPP), Op.is_equal, "ci cpp cnh", "am1", col(cNH), Op.mult)
+    ts(am[2], c128, col(cPM), Op.is_equal, "ci cpm ch", "am2", col(cH), Op.mult)
+    ts(am[3], c128, col(cP), Op.is_equal, "ci c0 ch", "am3", col(cH), Op.mult)
+    ts(am[4], c128, col(cP), Op.is_equal, "ci c0", "am4")
+    ts(T.ib[:, :], c128, col(cP), Op.is_equal, "ci c0", "ib")
+    ts(T.i128[:, :], c128, col(cP), Op.is_equal, "ci c0", "i128", 128.0, Op.mult)
+    cp("v", T.vv[:, :], T.mu1[:, 0:160], "mu1", "va vb")
+
+    def masks():
+        ts(T.m1[:, :], T.vv[:, :], 0.0, Op.is_gt, "va vb", "m1")
+        ts(T.vp[:, :], T.vv[:, :], 0.0, Op.max, "va vb", "vp")
+        tt(T.d1[:, :], T.m1[:, :], T.dd[:, :], Op.mult, "m1 dd", "d1")
+        tt(half(0), T.bs[:, b_], T.bs[:, a_], Op.subtract, "ba bb", "dn")
+    masks()
+
+    def cross_a():
+        tt(T.pp[:, :], T.mu[:, 0:160], T.d1[:, :], Op.mult, "mu d1", "pp")
+        tt(T.wv[:, :], T.mu[:, 0:160], T.vp[:, :], Op.mult, "mu vp", "wv")
+        tt(half(1), T.pp[:, a_], T.pp[:, b_], Op.subtract, "pp", "qq")
+        tt(half(2), T.wv[:, b_], T.wv[:, a_], Op.subtract, "wv", "dwv")
+
+    def bound(e, rd):
+        tt(T.eb[:, :], e, T.dd[:, :], Op.mult, rd + " dd", "eb")
+        tt(half(3), T.eb[:, b_], T.eb[:, a_], Op.subtract, "eb", "rr")
+
+    S = T.pt[:, 256:336]
+
+    def swap(dst, src, d, j, rd, wa, wb):
+        tt(half(j), d, S, Op.mult, rd + " ss", "t%d" % j)
+        tt(dst[:, a_], src[:, a_], half(j), Op.add, rd + " t%d" % j, wa)
+        tt(dst[:, b_], src[:, b_], half(j), Op.subtract, rd + " t%d" % j, wb)
+
+    def rows(f, src, q2, rd):
+        dma("s", T.win[f::32, :], src[:, :], "dw", rd, "wf%d" % (2 * f))
+        dma(q2, T.win[16 + f::32, :], src[:, :], "dw", rd, "wf%d" % (2 * f + 1))
+
+    def unpack(out, in_, rd, wr):
+        ts(out, in_, 1.0 / PK, Op.mult, rd, wr, -0.4165, Op.add)
+
+    def slots(src, nm, x, k0, k1, rd):
+        c = slice(8 * k0, 8 * k1)
+        unpack(T.sn[:, c], src, nm, "sn%d" % k0)
+        ts(T.sm[:, c], T.sn[:, c], -float(PK), Op.mult, "sn%d" % k0, "sm%d" % k0)
+        tt(T.sm[:, c], src, T.sm[:, c], Op.add, nm + " sm%d" % k0, "sm%d" % k0)
+        cp("v", T.xl[:, c], T.sm[:, c], "sm%d" % k0, "xl%d" % k0)
+        cp("a", T.aw[:, 128 * (k0 + 1):128 * (k1 + 1)], x[:, 0:2688].indirect(T.xl[:, c]), rd + " xl%d" % k0, "xo%d" % k0)
+
+    def scatter(buf, nm, offs, vals, rd):
+        op("a", lambda: A.activation(buf[:, :].indirect(offs), vals, Act.Silu), rd, nm + "r0 " + nm + "r1")
+
+    def entry(k):
+        j = (k - 2) // 2
+        return T.tte[:, 4 * j:4 * j + 4, :] if k % 2 == 0 else T.tto[:, 8 * j:8 * j + 8, :]
+
+    def entry_q(k):
+        j = (k - 2) // 2
+        return T.tte[:, 4 * j:4 * j + 4, 0::16] if k % 2 == 0 else T.tto[:, 8 * j:8 * j + 8, 0]
+
+    def home_even(k0, k1):
+        j0, j1 = (k0 - 2) // 2, (k1 - 2) // 2 + 1
+        rd = " ".join("tt%d" % k for k in range(k0, k1 + 1, 2)) + " am0 am1 am2 am3"
+        op("p", [(lambda hc=hc, hh=hh: P.matmul(T.pf[:, k0:k1 + 1:2, :, hc, :], am[2 * hc + hh],
+                                                T.tte[:, 4 * j0:4 * j1, 16 * hh:16 * hh + 2], hh == 0, hh == 1))
+                 for hc in range(2) for hh in range(2)], rd, "pf")
+        if k1 <= 16:
+            op("p", [(lambda hc=hc, hh=hh: P.matmul(T.pg[:, k0:k1 + 1:2, :, hc], am[2 * hc + hh],
+                                                    T.tte[:, 4 * j0:4 * j1, 16 * hh], hh == 0, hh == 1))
+                     for hc in range(2) for hh in range(2)], rd, "pg")
+
+    def home_odd(k0, k1):
+        j0, j1 = (k0 - 2) // 2, (k1 - 2) // 2 + 1
+        rd = " ".join("tt%d" % k for k in range(k0, k1 + 1, 2)) + " am4"
+        op("p", lambda: P.matmul(T.pf[:, k0:k1 + 1:2, :, :, :], am[4], T.tto[:, 8 * j0:8 * j1, 0:2], True, True), rd, "pf")
+        if k1 <= 16:
+            op("p", lambda: P.matmul(T.pg[:, k0:k1 + 1:2, :, :], am[4], T.tto[:, 8 * j0:8 * j1, 0], True, True), rd, "pg")
+
+    cross_a()
+    scatter(T.pos, "pos", T.ql[:, 0:8], T.vh[:, 0:128], "ql0 vh0")
+    four(T.gb2, "gc", T.ew[:, :], T.eiu, "ew eiu")
+    spread(T.mud, T.z, T.gb2, 0, 80, "z gc0 gc1", "mud")
+    spread(T.mud, T.z, T.gb2, 80, 160, "z gc2 gc3", "mud")
+    ts(T.z1[:, :], T.z[:, :], T.ew[:, 0:1], Op.mult, "z ew", "z1")
+    tt(col(cND), T.ew[:, 136:137], T.ew[:, 0:1], Op.subtract, "ew", "cnd")
+    ts(T.zd[:, :], T.z[:, :], col(cND), Op.mult, "z cnd", "zd")
+    bound(T.mud[:, 0:160], "mud")
+
+    for t in range(R):
+        last = t == R - 1
+        x, xn, y, yn = X[t % 2], XN[t % 2], X[1 - t % 2], XN[1 - t % 2]
+        xs = " ".join("%ss%d" % (xn, j) for j in range(4))
+        pos, pn = (T.pos2, "pos2") if last else (T.pos, "pos")
+        if t > 0:
+            cross_a()
+        tt(S, half(1), half(3), Op.is_lt, "qq rr", "ss")
+        if not last:
+            spread(T.mu1, T.z1, x, 0, 160, "z1 " + xs, "mu1")
+            spread(T.mud, T.zd, x, 0, 160, "zd " + xs, "mud")
+        q2 = "s" if last else "a"
+        tt(half(5), half(0), S, Op.mult, "dn ss", "t5")
+        tt(half(6), half(2), S, Op.mult, "dwv ss", "t6")
+        tt(T.nxl[:, a_], T.bs[:, a_], half(5), Op.add, "ba t5", "nxa")
+        tt(T.nxl[:, b_], T.bs[:, b_], half(5), Op.subtract, "bb t5", "nxb")
+        rows(0, T.nxl, q2, "nxa nxb nxo")
+        tt(T.wl[:, a_], T.wv[:, a_], half(6), Op.add, "wv t6", "wa")
+        tt(T.wl[:, b_], T.wv[:, b_], half(6), Op.subtract, "wv t6", "wb")
+        rows(1, T.wl, q2, "wa wb wo")
+        unpack(T.ql[:, 8:16], T.nxl[:, 0:8], "nxa", "ql1")
+        scatter(pos, pn, T.ql[:, 8:16], T.vh[:, 128:256], "ql1 vh1")
+        if t == 0:
+            op("a", lambda: A.activation(T.vs[:, :], T.vs[:, :], Act.Identity, bias=col(cH16)),
+               "c0 " + " ".join("vs%d" % j for j in range(11)), "vs")
+        if t == R - 2:
+            unpack(T.npu[:, :], T.nxl[:, 0:160], "nxa nxb", "npu")
+            scatter(T.pos2, "pos2", T.npu[:, 0:48], T.dfl[:, 0:768], "npu dfl")
+        tt(T.e01[:, 0:8, 1], T.mu[:, 160:168], T.vl[:, 0:8], Op.mult, "mu vl0", "e0w")
+        cp("v", T.e01[:, 8:16, 1], T.wl[:, 0:8], "wa", "e1w")
+        cp("v", T.e01[:, 8:16, 0], T.nxl[:, 0:8], "nxa", "e1s")
+        op("p", lambda: P.matmul(T.pf[:, 0:2, :, :, :], am[4], T.e01[:, :, :], True, True), "am4 e0w e0s e1w e1s", "pf")
+        op("p", lambda: P.matmul(T.pg[:, 0:2, :, :], am[4], T.e01[:, :, 0], True, True), "am4 e0s e1s", "pg")
+        op("p", lambda: P.matmul(T.cnt[:, 8:192], T.ib[:, :], T.ot[:, :], True, False), "ib ot", "cnt")
+        if t == 0:
+            cp("v", half(7), S, "ss", "sc")
+        else:
+            tt(half(7), half(7), S, Op.not_equal, "sc ss", "sc")
+        if not last:
+            ts(half(4), S, 1280.0, Op.mult, "ss", "t4")
+            tt(T.bs[:, a_], T.nxl[:, a_], half(4), Op.subtract, "nxa t4", "ba")
+            tt(T.bs[:, b_], T.nxl[:, b_], half(4), Op.add, "nxb t4", "bb")
+            tt(T.dfp[:, a_], T.idc[:, a_], half(4), Op.add, "idc t4", "dfa")
+            tt(T.dfp[:, b_], T.idc[:, b_], half(4), Op.subtract, "idc t4", "dfb")
+            ts(T.ea[:, :], T.vv[:, :], 0.0, Op.is_le, "va vb", "ea eab")
+            ts(T.m2[:, :], T.vv[:, :], 0.0, Op.is_lt, "va vb", "m2")
+            tt(half(8), T.vv[:, b_], T.vv[:, a_], Op.subtract, "va vb", "dv")
+            swap(T.vv, T.vv, half(8), 9, "dv va vb", "va", "vb")
+            masks()
+        else:
+            tt(half(8), T.nxi[:, b_], T.nxi[:, a_], Op.subtract, "nxi", "dv")
+            tt(half(9), half(8), half(7), Op.mult, "dv sc", "t9")
+            tt(T.yo[:, a_], T.nxi[:, a_], half(9), Op.add, "nxi t9", "yoa")
+            tt(T.yo[:, b_], T.nxi[:, b_], half(9), Op.subtract, "nxi t9", "yob")
+        for k in range(1, 23):
+            rp = T.rep[:, 128 * (k % 2):128 * (k % 2) + 128]
+            cp("v", rp, T.win[:, :].indirect(T.ql[:, 8 * k:8 * k + 8]), WALL + " ql%d" % k, "rep%d" % (k % 2))
+            op("v", lambda: V.transpose(entry(k + 1), rp), "rep%d" % (k % 2), "tt%d" % (k + 1))
+            unpack(T.ql[:, 8 * k + 8:8 * k + 16], entry_q(k + 1), "tt%d" % (k + 1), "ql%d" % (k + 1))
+            e = k + 1
+            if e % 2 == 0:
+                vals, rd = T.vs[:, 128 * (e // 2 - 1):128 * (e // 2)], "vs"
+            elif e == 23 and not last:
+                vals, rd = T.vh[:, 13 * 128:14 * 128], "vh2"
+            else:
+                vals, rd = T.vh[:, 128 * (e // 2 + 1):128 * (e // 2 + 2)], "vh1"
+            scatter(pos, pn, T.ql[:, 8 * e:8 * e + 8], vals, "ql%d %s" % (e, rd))
+            if e == 16:
+                home_even(2, 16)
+                home_odd(3, 15)
+            if e == 21:
+                home_odd(17, 21)
+            if e == 22:
+                home_even(18, 22)
+            if e == 23:
+                home_odd(23, 23)
+            if e == 3 and last:
+                dma("s", T.yn[:, :], T.yo[:, :], "dy", "yoa yob", "")
+                dma("s", T.y[:, 0:128], T.arr[:, 128 * t:128 * t + 128], "dy", "arr%d" % t, "")
+        dma("s", T.p1[:, :], pos[0::32, :], "dp", pn + "r0", "p1")
+        dma("s", T.p2[:, :], pos[16::32, :], "dp", pn + "r1", "p2")
+        cp("a", T.aw[:, 0:128], T.arr[:, 128 * t:128 * t + 128], "arr%d" % t, "aw")
+        slots(T.pg[:, 0:17, :, :], "pg", x, 0, 17, xs + " " + xn + "i")
+        op("v", [(lambda c=c: V.tensor_tensor_scan(T.pt[:, c:192:8], T.one[:, :], T.pf[:, 0:24, c // 2, c % 2, 1], 0.0, Op.mult, Op.add))
+                 for c in range(8)], "pf one", "tt")
+        tt(T.uu[:, :], T.pt[:, 0:192], T.lgx[:, :], Op.subtract, "tt lgx", "uu")
+        slots(T.pf[:, 17:23, :, :, 0], "pf", x, 17, 23, xs + " " + xn + "i")
+        for d in range(1, 24):
+            cd = T.cnd[:, 184 * (d - 1):184 * (d - 1) + 192 - 8 * d]
+            tt(cd, T.pt[:, 0:192 - 8 * d], T.uu[:, 8 * d:192], Op.is_le, "tt uu", "cd%d" % d)
+            op("p", lambda: P.matmul(T.cnt[:, 8 * d:192], T.i128[:, :], cd, False, d == 23), "i128 cd%d" % d, "cnt")
+        cp("v", T.sp[:, :], T.cnt[:, 8:192], "cnt", "sp")
+        sv = SV + 12 if last else SV
+        cp("a", x[:, XP0 + 16 * sv:XW], T.aw[:, :].indirect(T.sp[:, sv:184]), "aw xo0 xo17 sp", xn + "p1")
+        tt(T.pm[:, :], T.p1[:, :], T.p2[:, :], Op.max, "p1 p2", "pm pmo")
+        if t < R - 2:
+            dma("s", pos[0::32, :], T.rs[:, :], "dr", "rs0 rs1", pn + "r0")
+            dma("s", pos[16::32, :], T.rs[:, :], "dr", "rs0 rs1", pn + "r1")
+        if not last:
+            ts(T.p1[:, 160:168], T.pm[:, 160:168], float(CB), Op.is_lt, "pmo", "p1", float(CB + SMALL), Op.mult)
+            tt(T.pm[:, 0:160], T.pm[:, 0:160], T.dfp[:, :], Op.max, "pm dfa dfb", "pm")
+            tt(T.pm[:, 160:168], T.pm[:, 160:168], T.p1[:, 160:168], Op.add, "pmo p1", "pmo")
+            ts(T.piu[:, :], T.pm[:, :], float(CB), Op.subtract, "pm pmo", "piu", 0.25, Op.add)
+        else:
+            ts(T.piu[:, 8:168], T.pm[:, 8:168], float(CB + 128), Op.subtract, "pm pmo", "piu", 0.25, Op.add)
+        cp("v", x[:, XP0:XP0 + 16 * sv], T.aw[:, :].indirect(T.sp[:, 0:sv]), "aw xo0 xo17 sp", xn + "p0")
+        xall = "%s %si %so %sp0 %sp1 piu" % (xs, xn, xn, xn, xn)
+        if not last:
+            cp("a", y[:, 2560:2688], T.arr[:, 128 * t:128 * t + 128], "arr%d" % t, yn + "i")
+            four(y, yn + "s", x[:, :], T.piu, xall)
+            spread(T.mu, T.znu, y, 0, 80, "znu %ss0 %ss1" % (yn, yn), "mu")
+            spread(T.mu, T.znu, y, 80, 168, "znu %ss2 %ss3 %si" % (yn, yn, yn), "mu")
+            cp("a", y[:, 2688:2816], x[:, :].indirect(T.piu[:, 160:168]), xall, yn + "o")
+            send_fwd(t + 1)
+            if t < R - 2:
+                scatter(T.pos, "pos", T.ql[:, 0:8], T.vh[:, 0:128], "ql0 vh0")
+            else:
+                scatter(T.pos2, "pos2", T.npu[:, 48:160], T.dfl[:, 768:2560], "npu dfl")
+            tt(T.ea[:, :], T.mu1[:, 0:160], T.ea[:, :], Op.mult, "mu1 ea eab", "ea eab")
+            tt(T.m2[:, :], T.mud[:, 0:160], T.m2[:, :], Op.mult, "mud m2", "m2")
+            tt(T.ea[:, :], T.ea[:, :], T.m2[:, :], Op.add, "ea eab m2", "ea eab")
+            tt(half(8), T.ea[:, b_], T.ea[:, a_], Op.subtract, "ea eab", "dv")
+            swap(T.ea, T.ea, half(8), 9, "dv ea eab", "ea", "eab")
+            bound(T.ea[:, :], "ea eab")
+        else:
+            for j in range(4):
+                c0 = 128 + 640 * j
+                cp("va"[j % 2], T.xn[:, c0:c0 + 640], x[:, :].indirect(T.piu[:, 8 + 40 * j:48 + 40 * j]), xall, "y%d" % j)
+                dma("s", T.y[:, c0:c0 + 640], T.xn[:, c0:c0 + 640], "dy", "y%d" % j, "")
+    for s in sorted(cnt):
+        need("g", (s, cnt[s], {}, None), True)

@@ -368,17 +368,17 @@ def rank_program(g, core, T, topo):
     def scatter(buf, nm, offs, vals, rd):
         op("a", lambda: A.activation(buf[:, :].indirect(offs), vals, Act.Silu), rd, nm + "r0 " + nm + "r1")
 
-    def entry(k):
-        j = (k - 2) // 2
-        return T.tte[:, 4 * j:4 * j + 4, :] if k % 2 == 0 else T.tto[:, 8 * j:8 * j + 8, :]
+    def entry(k, u):
+        j = (k - 2) // 2 * 2 + u
+        return T.tte[:, 2 * j:2 * j + 2, :] if k % 2 == 0 else T.tto[:, 4 * j:4 * j + 4, :]
 
-    def entry_q(k):
-        j = (k - 2) // 2
-        return T.tte[:, 4 * j:4 * j + 4, 0::16] if k % 2 == 0 else T.tto[:, 8 * j:8 * j + 8, 0]
+    def entry_q(k, u):
+        j = (k - 2) // 2 * 2 + u
+        return T.tte[:, 2 * j:2 * j + 2, 0::16] if k % 2 == 0 else T.tto[:, 4 * j:4 * j + 4, 0]
 
     def home_even(k0, k1):
         j0, j1 = (k0 - 2) // 2, (k1 - 2) // 2 + 1
-        rd = " ".join("tt%d" % k for k in range(k0, k1 + 1, 2)) + " am0 am1 am2 am3"
+        rd = " ".join("tt%d tt%db" % (k, k) for k in range(k0, k1 + 1, 2)) + " am0 am1 am2 am3"
         op("p", [(lambda hc=hc, hh=hh: P.matmul(T.pf[:, k0:k1 + 1:2, :, hc, :], am[2 * hc + hh],
                                                 T.tte[:, 4 * j0:4 * j1, 16 * hh:16 * hh + 2], hh == 0, hh == 1))
                  for hc in range(2) for hh in range(2)], rd, "pf")
@@ -389,7 +389,7 @@ def rank_program(g, core, T, topo):
 
     def home_odd(k0, k1):
         j0, j1 = (k0 - 2) // 2, (k1 - 2) // 2 + 1
-        rd = " ".join("tt%d" % k for k in range(k0, k1 + 1, 2)) + " am4"
+        rd = " ".join("tt%d tt%db" % (k, k) for k in range(k0, k1 + 1, 2)) + " am4"
         op("p", lambda: P.matmul(T.pf[:, k0:k1 + 1:2, :, :, :], am[4], T.tto[:, 8 * j0:8 * j1, 0:2], True, True), rd, "pf")
         if k1 <= 16:
             op("p", lambda: P.matmul(T.pg[:, k0:k1 + 1:2, :, :], am[4], T.tto[:, 8 * j0:8 * j1, 0], True, True), rd, "pg")
@@ -459,18 +459,22 @@ def rank_program(g, core, T, topo):
             tt(T.yo[:, a_], T.nxi[:, a_], half(9), Op.add, "nxi t9", "yoa")
             tt(T.yo[:, b_], T.nxi[:, b_], half(9), Op.subtract, "nxi t9", "yob")
         for k in range(1, 23):
-            rp = T.rep[:, 128 * (k % 2):128 * (k % 2) + 128]
-            cp("v", rp, T.win[:, :].indirect(T.ql[:, 8 * k:8 * k + 8]), WALL + " ql%d" % k, "rep%d" % (k % 2))
-            op("v", lambda: V.transpose(entry(k + 1), rp), "rep%d" % (k % 2), "tt%d" % (k + 1))
-            unpack(T.ql[:, 8 * k + 8:8 * k + 16], entry_q(k + 1), "tt%d" % (k + 1), "ql%d" % (k + 1))
             e = k + 1
+            rp = [T.rep[:, 128 * (k % 2) + 64 * u:128 * (k % 2) + 64 * u + 64] for u in range(2)]
+            nm = ["ql%d" % k, "ql%db" % k if k > 1 else "ql1"]
+            for u in range(2):
+                cp("v", rp[u], T.win[:, :].indirect(T.ql[:, 8 * k + 4 * u:8 * k + 4 * u + 4]), WALL + " " + nm[u], "rep%d%d" % (k % 2, u))
+            for u in range(2):
+                op("v", lambda: V.transpose(entry(e, u), rp[u]), "rep%d%d" % (k % 2, u), "tt%d%s" % (e, "b" * u))
+            for u in range(2):
+                unpack(T.ql[:, 8 * e + 4 * u:8 * e + 4 * u + 4], entry_q(e, u), "tt%d%s" % (e, "b" * u), "ql%d%s" % (e, "b" * u))
             if e % 2 == 0:
                 vals, rd = T.vs[:, 128 * (e // 2 - 1):128 * (e // 2)], "vs"
             elif e == 23 and not last:
                 vals, rd = T.vh[:, 13 * 128:14 * 128], "vh2"
             else:
                 vals, rd = T.vh[:, 128 * (e // 2 + 1):128 * (e // 2 + 2)], "vh1"
-            scatter(pos, pn, T.ql[:, 8 * e:8 * e + 8], vals, "ql%d %s" % (e, rd))
+            scatter(pos, pn, T.ql[:, 8 * e:8 * e + 8], vals, "ql%d ql%db %s" % (e, e, rd))
             if e == 16:
                 home_even(2, 16)
                 home_odd(3, 15)

@@ -3,13 +3,13 @@ from concourse.mybir import AluOpType as Op
 from concourse.mybir import ActivationFunctionType as Act
 
 R = 4
-PW = 168
+PW = 176
 ROW = 32 * PW
 XP0 = 2816
 XW = XP0 + 23 * 128
 CB = 8192
 SV = 68
-PK = 3072
+PK = 2944
 SMALL = 2624
 
 F, H, I, U = "float32", "bfloat16", "int32", "uint16"
@@ -19,7 +19,7 @@ SCRATCH = {
     "ew": ("sbuf", [128, 144], H), "pk": ("sbuf", [128, 144], H), "gb": ("sbuf", [128, 2560], H), "gb2": ("sbuf", [128, 2560], H),
     "rl": ("sbuf", [128, R * 64], H), "rb": ("sbuf", [128, 72], H),
     "win": ("sbuf", [128, ROW], F), "pos": ("sbuf", [128, ROW], F), "pos2": ("sbuf", [128, ROW], F),
-    "vh": ("sbuf", [128, 14 * 128], F), "vs": ("sbuf", [128, 11 * 128], F), "dfl": ("sbuf", [128, 2560], F),
+    "vh": ("sbuf", [128, 14 * 128], F), "vs": ("sbuf", [128, 22 * 128], F), "dfl": ("sbuf", [128, 2560], F),
     "rep": ("sbuf", [128, 256], F), "tte": ("sbuf", [128, 44, 32], F), "tto": ("sbuf", [128, 88, 16], F),
     "ql": ("sbuf", [128, 192], U), "xl": ("sbuf", [128, 184], U), "sp": ("sbuf", [128, 184], U), "piu": ("sbuf", [128, PW], U),
     "nxu": ("sbuf", [128, 160], U), "npu": ("sbuf", [128, 160], U), "eiu": ("sbuf", [128, 160], U),
@@ -36,7 +36,7 @@ SCRATCH = {
     "pm": ("sbuf", [128, PW], F), "dd": ("sbuf", [128, 160], F), "d1": ("sbuf", [128, 160], F), "vv": ("sbuf", [128, 160], F),
     "vp": ("sbuf", [128, 160], F), "pp": ("sbuf", [128, 160], F), "wv": ("sbuf", [128, 160], F), "dfp": ("sbuf", [128, 160], F),
     "ea": ("sbuf", [128, 160], F), "eb": ("sbuf", [128, 160], F), "m1": ("sbuf", [128, 160], F), "m2": ("sbuf", [128, 160], F),
-    "h": ("sbuf", [128, 10 * 80], F), "e01": ("sbuf", [128, 16, 2], F), "lgx": ("sbuf", [128, 192], F), "uu": ("sbuf", [128, 192], F),
+    "h": ("sbuf", [128, 14 * 80], F), "e01": ("sbuf", [128, 16, 2], F), "lgx": ("sbuf", [128, 192], F), "uu": ("sbuf", [128, 192], F),
     "one": ("sbuf", [128, 24], F), "cnd": ("sbuf", [128, 23 * 184], H), "tb": ("sbuf", [128, 128], H), "tf": ("sbuf", [128, 128], F),
     "yo": ("sbuf", [128, 160], F),
     "mu": ("psum", [128, 512], F), "mu1": ("psum", [128, 512], F), "mud": ("psum", [128, 512], F),
@@ -224,10 +224,10 @@ def rank_program(g, core, T, topo):
     op("g", lambda: g.iota(T.pci[:, 0:1], [[1, 1]], 0, 1), "", "pci0")
     iota(T.mg[:, :], [[1, 8], [0, 16]], 0, 0, "mg")
     iota(T.ci[:, :], [[1, PW]], 0, 0, "ci")
-    iota(T.win[:, 4200:ROW], [[0, ROW - 4200]], 0, 0, "win3")
-    fill(T.win[:, 0:1400], 0.0, "win0")
-    cp("a", T.win[:, 1400:2800], T.win[:, 0:1400], "win0", "win1")
-    cp("a", T.win[:, 2800:4200], T.win[:, 0:1400], "win0", "win2")
+    iota(T.win[:, 4512:ROW], [[0, ROW - 4512]], 0, 0, "win3")
+    fill(T.win[:, 0:1504], 0.0, "win0")
+    cp("a", T.win[:, 1504:3008], T.win[:, 0:1504], "win0", "win1")
+    cp("a", T.win[:, 3008:4512], T.win[:, 0:1504], "win0", "win2")
     fill(T.pk[:, :], 0.0, "pk")
     fill(T.z[:, :], 0.0, "z")
     ts(T.pci[:, 1:2], T.pci[:, 0:1], 15, Op.bitwise_and, "pci0", "pci1")
@@ -257,14 +257,16 @@ def rank_program(g, core, T, topo):
     send_fwd(0)
     iota(T.vh[:, 0:128], [[1, 128]], XP0 + CB, 0, "vh0")
     iota(T.oti[:, :], [[0, 23], [16, 8]], 0, 0, "oti")
-    iota(T.vh[:, 128:13 * 128], [[256, 12], [1, 128]], XP0 + CB + 128, 0, "vh1")
+    iota(T.vh[:, 128:256], [[1, 128]], XP0 + CB + 128, 0, "vh1")
     iota(T.vh[:, 13 * 128:14 * 128], [[1, 128]], XP0 + 22 * 128 - SMALL, 0, "vh2")
     for j in range(11):
-        iota(T.vs[:, 128 * j:128 * j + 128], [[32, 4], [0, 2], [1, 16]], XP0 + CB + 256 * (j + 1), 0, "vs%d" % j)
+        iota(T.vs[:, 256 * j:256 * j + 128], [[32, 4], [0, 2], [1, 16]], XP0 + CB + 256 * (j + 1), 0, "vs%d" % j)
+    for j in range(11):
+        iota(T.vs[:, 256 * j + 128:256 * j + 256], [[1, 128]], XP0 + CB + 256 * (j + 1) + 128, 0, "vo%d" % j)
     iota(T.dfl[:, :], [[1, 2560]], CB + 128, 0, "dfl")
 
     fill(T.vl[:, 160:164], 0.0, "vl1")
-    fill(T.vl[:, 164:168], -1.0, "vl2")
+    fill(T.vl[:, 164:PW], -1.0, "vl2")
     cp("v", T.vl[:, 0:160], T.voi[:, :], "voi", "vl0")
     dma("s", T.win[0::32, :], T.vl[:, :], "dw", "vl0 vl1 vl2", "win0 win1 win2 win3 wf0")
     dma("s", T.win[16::32, :], T.vl[:, :], "dw", "vl0 vl1 vl2", "wf1")
@@ -290,12 +292,15 @@ def rank_program(g, core, T, topo):
     tt(T.dd[:, a_], T.lei[:, 160:240], T.lei[:, 0:80], Op.subtract, "lei", "dd")
     tt(T.dd[:, b_], T.lei[:, 240:320], T.lei[:, 80:160], Op.subtract, "lei", "dd")
     ts(T.idn[:, :], T.ci[:, 0:160], 16.0, Op.mult, "ci c0", "idn", col(cI), Op.add)
-    ts(T.nxl[:, 160:168], T.ci[:, 160:168], col(cPI), Op.add, "ci cpi", "nxo", float(PK), Op.mult)
+    ts(T.nxl[:, 160:168], T.ci[:, 168:176], col(cPI), Op.add, "ci cpi", "nxo", float(PK), Op.mult)
+    ts(T.nxl[:, 168:176], T.ci[:, 160:168], col(cPI), Op.add, "ci cpi", "nxo", float(PK), Op.mult)
+    fill(T.rs[:, 168:PW], 0.0, "rs0")
+    tt(half(10), T.dd[:, a_], T.dd[:, b_], Op.add, "dd", "ab")
     ts(T.p1[:, 0:160], T.p1[:, 0:160], float(PK), Op.mult, "p1", "p1")
     ts(T.idc[:, :], T.idn[:, :], float(CB), Op.add, "idn", "idc")
     tt(T.bs[:, :], T.p1[:, 0:160], T.idn[:, :], Op.add, "p1 idn", "ba bb")
     ts(T.ql[:, 0:8], T.ci[:, 0:8], col(cPI), Op.add, "ci cpi", "ql0")
-    fill(T.wl[:, 160:168], 0.0, "wo")
+    fill(T.wl[:, 160:PW], 0.0, "wo")
     fill(T.rs[:, 0:160], 0.0, "rs0")
     ts(T.rs[:, 160:168], T.idn[:, 0:8], float(2688 - SMALL), Op.add, "idn", "rs1")
     WALL = "win0 win1 win2 win3 wf0 wf1 wf2 wf3"
@@ -324,14 +329,12 @@ def rank_program(g, core, T, topo):
     ts(am[4], c128, col(cP), Op.is_equal, "ci c0", "am4")
     ts(T.ib[:, :], c128, col(cP), Op.is_equal, "ci c0", "ib")
     ts(T.i128[:, :], c128, col(cP), Op.is_equal, "ci c0", "i128", 128.0, Op.mult)
-    cp("v", T.vv[:, :], T.mu1[:, 0:160], "mu1", "va vb")
 
     def masks():
         ts(T.m1[:, :], T.vv[:, :], 0.0, Op.is_gt, "va vb", "m1")
         ts(T.vp[:, :], T.vv[:, :], 0.0, Op.max, "va vb", "vp")
         tt(T.d1[:, :], T.m1[:, :], T.dd[:, :], Op.mult, "m1 dd", "d1")
         tt(half(0), T.bs[:, b_], T.bs[:, a_], Op.subtract, "ba bb", "dn")
-    masks()
 
     def cross_a():
         tt(T.pp[:, :], T.mu[:, 0:160], T.d1[:, :], Op.mult, "mu d1", "pp")
@@ -355,15 +358,16 @@ def rank_program(g, core, T, topo):
         dma(q2, T.win[16 + f::32, :], src[:, :], "dw", rd, "wf%d" % (2 * f + 1))
 
     def unpack(out, in_, rd, wr):
-        ts(out, in_, 1.0 / PK, Op.mult, rd, wr, -0.4165, Op.add)
+        ts(out, in_, 1.0 / PK, Op.mult, rd, wr, -0.456, Op.add)
 
     def slots(src, nm, x, k0, k1, rd):
         c = slice(8 * k0, 8 * k1)
-        unpack(T.sn[:, c], src, nm, "sn%d" % k0)
-        ts(T.sm[:, c], T.sn[:, c], -float(PK), Op.mult, "sn%d" % k0, "sm%d" % k0)
-        tt(T.sm[:, c], src, T.sm[:, c], Op.add, nm + " sm%d" % k0, "sm%d" % k0)
-        cp("v", T.xl[:, c], T.sm[:, c], "sm%d" % k0, "xl%d" % k0)
-        cp("a", T.aw[:, 128 * (k0 + 1):128 * (k1 + 1)], x[:, 0:2688].indirect(T.xl[:, c]), rd + " xl%d" % k0, "xo%d" % k0)
+
+        return [lambda: unpack(T.sn[:, c], src, nm, "sn%d" % k0),
+                lambda: ts(T.sm[:, c], T.sn[:, c], -float(PK), Op.mult, "sn%d" % k0, "sm%d" % k0),
+                lambda: tt(T.sm[:, c], src, T.sm[:, c], Op.add, nm + " sm%d" % k0, "sm%d" % k0),
+                lambda: cp("v", T.xl[:, c], T.sm[:, c], "sm%d" % k0, "xl%d" % k0),
+                lambda: cp("a", T.aw[:, 128 * (k0 + 1):128 * (k1 + 1)], x[:, 0:2688].indirect(T.xl[:, c]), rd + " xl%d" % k0, "xo%d" % k0)]
 
     def scatter(buf, nm, offs, vals, rd):
         op("a", lambda: A.activation(buf[:, :].indirect(offs), vals, Act.Silu), rd, nm + "r0 " + nm + "r1")
@@ -379,13 +383,13 @@ def rank_program(g, core, T, topo):
     def home_even(k0, k1):
         j0, j1 = (k0 - 2) // 2, (k1 - 2) // 2 + 1
         rd = " ".join("tt%d tt%db" % (k, k) for k in range(k0, k1 + 1, 2)) + " am0 am1 am2 am3"
-        op("p", [(lambda hc=hc, hh=hh: P.matmul(T.pf[:, k0:k1 + 1:2, :, hc, :], am[2 * hc + hh],
-                                                T.tte[:, 4 * j0:4 * j1, 16 * hh:16 * hh + 2], hh == 0, hh == 1))
-                 for hc in range(2) for hh in range(2)], rd, "pf")
         if k1 <= 16:
             op("p", [(lambda hc=hc, hh=hh: P.matmul(T.pg[:, k0:k1 + 1:2, :, hc], am[2 * hc + hh],
                                                     T.tte[:, 4 * j0:4 * j1, 16 * hh], hh == 0, hh == 1))
                      for hc in range(2) for hh in range(2)], rd, "pg")
+        op("p", [(lambda hc=hc, hh=hh: P.matmul(T.pf[:, k0:k1 + 1:2, :, hc, :], am[2 * hc + hh],
+                                                T.tte[:, 4 * j0:4 * j1, 16 * hh:16 * hh + 2], hh == 0, hh == 1))
+                 for hc in range(2) for hh in range(2)], rd, "pf")
 
     def home_odd(k0, k1):
         j0, j1 = (k0 - 2) // 2, (k1 - 2) // 2 + 1
@@ -394,11 +398,13 @@ def rank_program(g, core, T, topo):
         if k1 <= 16:
             op("p", lambda: P.matmul(T.pg[:, k0:k1 + 1:2, :, :], am[4], T.tto[:, 8 * j0:8 * j1, 0], True, True), rd, "pg")
 
-    cross_a()
     scatter(T.pos, "pos", T.ql[:, 0:8], T.vh[:, 0:128], "ql0 vh0")
     four(T.gb2, "gc", T.ew[:, :], T.eiu, "ew eiu")
     spread(T.mud, T.z, T.gb2, 0, 80, "z gc0 gc1", "mud")
     spread(T.mud, T.z, T.gb2, 80, 160, "z gc2 gc3", "mud")
+    cp("v", T.vv[:, :], T.mu1[:, 0:160], "mu1", "va vb")
+    masks()
+    cross_a()
     ts(T.z1[:, :], T.z[:, :], T.ew[:, 0:1], Op.mult, "z ew", "z1")
     tt(col(cND), T.ew[:, 136:137], T.ew[:, 0:1], Op.subtract, "ew", "cnd")
     ts(T.zd[:, :], T.z[:, :], col(cND), Op.mult, "z cnd", "zd")
@@ -427,8 +433,8 @@ def rank_program(g, core, T, topo):
         unpack(T.ql[:, 8:16], T.nxl[:, 0:8], "nxa", "ql1")
         scatter(pos, pn, T.ql[:, 8:16], T.vh[:, 128:256], "ql1 vh1")
         if t == 0:
-            op("a", lambda: A.activation(T.vs[:, :], T.vs[:, :], Act.Identity, bias=col(cH16)),
-               "c0 " + " ".join("vs%d" % j for j in range(11)), "vs")
+            op("a", [(lambda j=j: A.activation(T.vs[:, 256 * j:256 * j + 128], T.vs[:, 256 * j:256 * j + 128], Act.Identity, bias=col(cH16)))
+                     for j in range(11)], "c0 " + " ".join("vs%d" % j for j in range(11)), "vs")
         if t == R - 2:
             unpack(T.npu[:, :], T.nxl[:, 0:160], "nxa nxb", "npu")
             scatter(T.pos2, "pos2", T.npu[:, 0:48], T.dfl[:, 0:768], "npu dfl")
@@ -444,20 +450,24 @@ def rank_program(g, core, T, topo):
             tt(half(7), half(7), S, Op.not_equal, "sc ss", "sc")
         if not last:
             ts(half(4), S, 1280.0, Op.mult, "ss", "t4")
+            tt(half(8), T.vv[:, b_], T.vv[:, a_], Op.subtract, "va vb", "dv")
+            ts(T.ea[:, :], T.vv[:, :], 0.0, Op.is_le, "va vb", "ea eab")
+            tt(half(9), half(8), S, Op.mult, "dv ss", "t9")
+            ts(T.m2[:, :], T.vv[:, :], 0.0, Op.is_lt, "va vb", "m2")
             tt(T.bs[:, a_], T.nxl[:, a_], half(4), Op.subtract, "nxa t4", "ba")
+            tt(T.vv[:, a_], T.vv[:, a_], half(9), Op.add, "va t9", "va")
+            tt(T.vv[:, b_], T.vv[:, b_], half(9), Op.subtract, "vb t9", "vb")
             tt(T.bs[:, b_], T.nxl[:, b_], half(4), Op.add, "nxb t4", "bb")
+            masks()
             tt(T.dfp[:, a_], T.idc[:, a_], half(4), Op.add, "idc t4", "dfa")
             tt(T.dfp[:, b_], T.idc[:, b_], half(4), Op.subtract, "idc t4", "dfb")
-            ts(T.ea[:, :], T.vv[:, :], 0.0, Op.is_le, "va vb", "ea eab")
-            ts(T.m2[:, :], T.vv[:, :], 0.0, Op.is_lt, "va vb", "m2")
-            tt(half(8), T.vv[:, b_], T.vv[:, a_], Op.subtract, "va vb", "dv")
-            swap(T.vv, T.vv, half(8), 9, "dv va vb", "va", "vb")
-            masks()
+            tt(half(11), half(10), S, Op.mult, "ab ss", "sab")
         else:
             tt(half(8), T.nxi[:, b_], T.nxi[:, a_], Op.subtract, "nxi", "dv")
             tt(half(9), half(8), half(7), Op.mult, "dv sc", "t9")
             tt(T.yo[:, a_], T.nxi[:, a_], half(9), Op.add, "nxi t9", "yoa")
             tt(T.yo[:, b_], T.nxi[:, b_], half(9), Op.subtract, "nxi t9", "yob")
+        early = slots(T.pg[:, 0:17, :, :], "pg", x, 0, 17, xs + " " + xn + "i")
         for k in range(1, 23):
             e = k + 1
             rp = [T.rep[:, 128 * (k % 2) + 64 * u:128 * (k % 2) + 64 * u + 64] for u in range(2)]
@@ -468,16 +478,23 @@ def rank_program(g, core, T, topo):
                 op("v", lambda: V.transpose(entry(e, u), rp[u]), "rep%d%d" % (k % 2, u), "tt%d%s" % (e, "b" * u))
             for u in range(2):
                 unpack(T.ql[:, 8 * e + 4 * u:8 * e + 4 * u + 4], entry_q(e, u), "tt%d%s" % (e, "b" * u), "ql%d%s" % (e, "b" * u))
-            if e % 2 == 0:
-                vals, rd = T.vs[:, 128 * (e // 2 - 1):128 * (e // 2)], "vs"
-            elif e == 23 and not last:
-                vals, rd = T.vh[:, 13 * 128:14 * 128], "vh2"
-            else:
-                vals, rd = T.vh[:, 128 * (e // 2 + 1):128 * (e // 2 + 2)], "vh1"
-            scatter(pos, pn, T.ql[:, 8 * e:8 * e + 8], vals, "ql%d ql%db %s" % (e, e, rd))
+            if e == 23 and not last:
+                scatter(pos, pn, T.ql[:, 8 * e:8 * e + 8], T.vh[:, 13 * 128:14 * 128], "ql23 ql23b vh2")
+            elif e >= 22:
+                scatter(pos, pn, T.ql[:, 8 * e:8 * e + 8], T.vs[:, 128 * (e - 2):128 * (e - 1)], "ql%d ql%db vs vo10" % (e, e))
+            elif e % 2 == 1:
+                scatter(pos, pn, T.ql[:, 8 * e - 8:8 * e + 8], T.vs[:, 128 * (e - 3):128 * (e - 1)],
+                        "ql%d ql%db ql%d ql%db vs vo%d" % (e - 1, e - 1, e, e, (e - 3) // 2))
+            if e == 12:
+                cp("a", T.aw[:, 0:128], T.arr[:, 128 * t:128 * t + 128], "arr%d" % t, "aw")
+                if not last:
+                    cp("a", y[:, 2560:2688], T.arr[:, 128 * t:128 * t + 128], "arr%d" % t, yn + "i")
+            if e == 15:
+                home_odd(3, 15)
             if e == 16:
                 home_even(2, 16)
-                home_odd(3, 15)
+            if e >= 20:
+                early[e - 20]()
             if e == 21:
                 home_odd(17, 21)
             if e == 22:
@@ -489,13 +506,16 @@ def rank_program(g, core, T, topo):
                 dma("s", T.y[:, 0:128], T.arr[:, 128 * t:128 * t + 128], "dy", "arr%d" % t, "")
         dma("s", T.p1[:, :], pos[0::32, :], "dp", pn + "r0", "p1")
         dma("s", T.p2[:, :], pos[16::32, :], "dp", pn + "r1", "p2")
-        cp("a", T.aw[:, 0:128], T.arr[:, 128 * t:128 * t + 128], "arr%d" % t, "aw")
-        slots(T.pg[:, 0:17, :, :], "pg", x, 0, 17, xs + " " + xn + "i")
+        early[4]()
         op("v", [(lambda c=c: V.tensor_tensor_scan(T.pt[:, c:192:8], T.one[:, :], T.pf[:, 0:24, c // 2, c % 2, 1], 0.0, Op.mult, Op.add))
                  for c in range(8)], "pf one", "tt")
+        late = slots(T.pf[:, 17:23, :, :, 0], "pf", x, 17, 23, xs + " " + xn + "i")
+        late[0]()
         tt(T.uu[:, :], T.pt[:, 0:192], T.lgx[:, :], Op.subtract, "tt lgx", "uu")
-        slots(T.pf[:, 17:23, :, :, 0], "pf", x, 17, 23, xs + " " + xn + "i")
+        late[1]()
         for d in range(1, 24):
+            if d in (2, 3, 4):
+                late[d]()
             cd = T.cnd[:, 184 * (d - 1):184 * (d - 1) + 192 - 8 * d]
             tt(cd, T.pt[:, 0:192 - 8 * d], T.uu[:, 8 * d:192], Op.is_le, "tt uu", "cd%d" % d)
             op("p", lambda: P.matmul(T.cnt[:, 8 * d:192], T.i128[:, :], cd, False, d == 23), "i128 cd%d" % d, "cnt")
@@ -506,17 +526,24 @@ def rank_program(g, core, T, topo):
         if t < R - 2:
             dma("s", pos[0::32, :], T.rs[:, :], "dr", "rs0 rs1", pn + "r0")
             dma("s", pos[16::32, :], T.rs[:, :], "dr", "rs0 rs1", pn + "r1")
+        def part(j, c0, c1):
+            cp("v", x[:, XP0 + 16 * c0:XP0 + 16 * c1], T.aw[:, :].indirect(T.sp[:, c0:c1]), "aw xo0 xo17 sp", xn + "p%d" % j)
+        part(0, 0, 16)
+        tt(T.pm[:, 160:168], T.pm[:, 160:168], T.pm[:, 168:176], Op.max, "pmo", "pmo")
         if not last:
-            ts(T.p1[:, 160:168], T.pm[:, 160:168], float(CB), Op.is_lt, "pmo", "p1", float(CB + SMALL), Op.mult)
             tt(T.pm[:, 0:160], T.pm[:, 0:160], T.dfp[:, :], Op.max, "pm dfa dfb", "pm")
+            ts(T.p1[:, 160:168], T.pm[:, 160:168], float(CB), Op.is_lt, "pmo", "p1", float(CB + SMALL), Op.mult)
+            part(2, 16, 32)
             tt(T.pm[:, 160:168], T.pm[:, 160:168], T.p1[:, 160:168], Op.add, "pmo p1", "pmo")
-            ts(T.piu[:, :], T.pm[:, :], float(CB), Op.subtract, "pm pmo", "piu", 0.25, Op.add)
+            part(3, 32, 48)
+            ts(T.piu[:, 0:168], T.pm[:, 0:168], float(CB), Op.subtract, "pm pmo", "piu", 0.25, Op.add)
+            part(4, 48, sv)
         else:
+            part(2, 16, 32)
             ts(T.piu[:, 8:168], T.pm[:, 8:168], float(CB + 128), Op.subtract, "pm pmo", "piu", 0.25, Op.add)
-        cp("v", x[:, XP0:XP0 + 16 * sv], T.aw[:, :].indirect(T.sp[:, 0:sv]), "aw xo0 xo17 sp", xn + "p0")
-        xall = "%s %si %so %sp0 %sp1 piu" % (xs, xn, xn, xn, xn)
+            part(3, 32, sv)
+        xall = "%s %si %so %sp0 %sp1 %sp2 %sp3 %sp4 piu" % (xs, xn, xn, xn, xn, xn, xn, xn)
         if not last:
-            cp("a", y[:, 2560:2688], T.arr[:, 128 * t:128 * t + 128], "arr%d" % t, yn + "i")
             four(y, yn + "s", x[:, :], T.piu, xall)
             spread(T.mu, T.znu, y, 0, 80, "znu %ss0 %ss1" % (yn, yn), "mu")
             spread(T.mu, T.znu, y, 80, 168, "znu %ss2 %ss3 %si" % (yn, yn, yn), "mu")
@@ -529,9 +556,11 @@ def rank_program(g, core, T, topo):
             tt(T.ea[:, :], T.mu1[:, 0:160], T.ea[:, :], Op.mult, "mu1 ea eab", "ea eab")
             tt(T.m2[:, :], T.mud[:, 0:160], T.m2[:, :], Op.mult, "mud m2", "m2")
             tt(T.ea[:, :], T.ea[:, :], T.m2[:, :], Op.add, "ea eab m2", "ea eab")
-            tt(half(8), T.ea[:, b_], T.ea[:, a_], Op.subtract, "ea eab", "dv")
-            swap(T.ea, T.ea, half(8), 9, "dv ea eab", "ea", "eab")
-            bound(T.ea[:, :], "ea eab")
+            tt(half(8), T.ea[:, a_], T.ea[:, b_], Op.subtract, "ea eab", "dv")
+            tt(T.eb[:, :], T.ea[:, :], T.dd[:, :], Op.mult, "ea eab dd", "eb")
+            tt(half(12), half(8), half(11), Op.mult, "dv sab", "g1")
+            tt(half(13), T.eb[:, b_], T.eb[:, a_], Op.subtract, "eb", "r0")
+            tt(half(3), half(12), half(13), Op.add, "g1 r0", "rr")
         else:
             for j in range(4):
                 c0 = 128 + 640 * j

@@ -5,44 +5,52 @@ from concourse.mybir import ActivationFunctionType as Act
 R = 4
 PW = 176
 ROW = 32 * PW
-XP0 = 2816
+XP0 = 2688
 XW = XP0 + 23 * 128
+EW = 16 * PW
 CB = 8192
-SV = 68
-PK = 2944
-SMALL = 2624
+SV = 82
+KB = 10
+PK = 4096
+QC, SC = ROW // 2, 1280
+RND = 1.5 * 2.0 ** 23 * PK
+YC = (8, 24, 40, 80, 120, 144, 168)
+SMALL = 2496
+CUT = (0, 38, 74, 118, 160)
 
 F, H, I, U = "float32", "bfloat16", "int32", "uint16"
 SCRATCH = {
     "xn": ("sbuf", [128, 2688], H), "xa": ("sbuf", [128, XW], H), "xb": ("sbuf", [128, XW], H),
     "aw": ("sbuf", [128, 128 + 23 * 128], H), "arr": ("sbuf", [128, R * 128], H),
-    "ew": ("sbuf", [128, 144], H), "pk": ("sbuf", [128, 144], H), "gb": ("sbuf", [128, 2560], H), "gb2": ("sbuf", [128, 2560], H),
+    "pk": ("sbuf", [128, 144], H), "gb": ("sbuf", [128, 2560], H), "vlb": ("sbuf", [128, PW], H),
     "rl": ("sbuf", [128, R * 64], H), "rb": ("sbuf", [128, 72], H),
     "win": ("sbuf", [128, ROW], F), "pos": ("sbuf", [128, ROW], F), "pos2": ("sbuf", [128, ROW], F),
-    "vh": ("sbuf", [128, 14 * 128], F), "vs": ("sbuf", [128, 22 * 128], F), "dfl": ("sbuf", [128, 2560], F),
+    "vh": ("sbuf", [128, 3 * 128], F), "vs": ("sbuf", [128, 11, 256], F), "dfl": ("sbuf", [128, 2560], F),
     "rep": ("sbuf", [128, 256], F), "tte": ("sbuf", [128, 44, 32], F), "tto": ("sbuf", [128, 88, 16], F),
     "ql": ("sbuf", [128, 192], U), "xl": ("sbuf", [128, 184], U), "sp": ("sbuf", [128, 184], U), "piu": ("sbuf", [128, PW], U),
-    "nxu": ("sbuf", [128, 160], U), "npu": ("sbuf", [128, 160], U), "eiu": ("sbuf", [128, 160], U),
+    "nxu": ("sbuf", [128, 160], U), "npu": ("sbuf", [128, 160], U), "viu": ("sbuf", [128, 160], U),
     "nui": ("sbuf", [128, 4], I), "nxi": ("sbuf", [128, 160], I), "lei": ("sbuf", [128, 320], I),
     "voi": ("sbuf", [128, 160], I), "lgi": ("sbuf", [128, 8], I), "ti1": ("sbuf", [128, 160], I), "ti2": ("sbuf", [128, 160], I),
     "pci": ("sbuf", [128, 8], I), "col": ("sbuf", [128, 24], F), "ci": ("sbuf", [128, PW], F), "mg": ("sbuf", [128, 128], F),
     "oti": ("sbuf", [128, 184], F), "ot": ("sbuf", [128, 184], H),
     "z": ("sbuf", [128, 144], H), "znu": ("sbuf", [128, 144], H), "z1": ("sbuf", [128, 144], H), "zd": ("sbuf", [128, 144], H),
-    "zs": ("sbuf", [128, 144], H), "bnu": ("sbuf", [128, 128], H), "ib": ("sbuf", [128, 128], H), "i128": ("sbuf", [128, 128], H),
-    "am": ("sbuf", [128, 5 * 128], F),
+    "bnu": ("sbuf", [128, 128], H), "ib": ("sbuf", [128, 128], H), "i128": ("sbuf", [128, 128], H),
+    "am": ("sbuf", [128, 5 * 128], F), "hm": ("sbuf", [128, 4 * 128], F),
     "nxl": ("sbuf", [128, PW], F), "wl": ("sbuf", [128, PW], F), "bs": ("sbuf", [128, 160], F), "idc": ("sbuf", [128, 160], F),
-    "sn": ("sbuf", [128, 184], I), "sm": ("sbuf", [128, 184], F), "pg": ("psum", [128, 64, 4, 2], F), "vl": ("sbuf", [128, PW], F),
-    "rs": ("sbuf", [128, PW], F), "idn": ("sbuf", [128, 160], F), "p1": ("sbuf", [128, PW], F), "p2": ("sbuf", [128, PW], F),
+    "sn": ("sbuf", [128, 184], I), "sm": ("sbuf", [128, 184], F), "pg": ("psum", [128, 64, 4, 2], F),
+    "rs": ("sbuf", [128, PW], F), "rz": ("sbuf", [128, PW], F), "idn": ("sbuf", [128, 160], F), "p1": ("sbuf", [128, PW], F), "p2": ("sbuf", [128, PW], F),
     "pm": ("sbuf", [128, PW], F), "dd": ("sbuf", [128, 160], F), "d1": ("sbuf", [128, 160], F), "vv": ("sbuf", [128, 160], F),
-    "vp": ("sbuf", [128, 160], F), "pp": ("sbuf", [128, 160], F), "wv": ("sbuf", [128, 160], F), "dfp": ("sbuf", [128, 160], F),
-    "ea": ("sbuf", [128, 160], F), "eb": ("sbuf", [128, 160], F), "m1": ("sbuf", [128, 160], F), "m2": ("sbuf", [128, 160], F),
-    "h": ("sbuf", [128, 14 * 80], F), "e01": ("sbuf", [128, 16, 2], F), "lgx": ("sbuf", [128, 192], F), "uu": ("sbuf", [128, 192], F),
+    "vp": ("sbuf", [128, 160], F), "wv": ("sbuf", [128, 160], F), "dfp": ("sbuf", [128, 160], F),
+    "cf": ("sbuf", [128, 160], F), "c1": ("sbuf", [128, 160], F), "c2": ("sbuf", [128, 160], F), "u1": ("sbuf", [128, 160], F),
+    "m1": ("sbuf", [128, 160], F), "m2": ("sbuf", [128, 160], F),
+    "h": ("sbuf", [128, 14 * 80], F), "lgx": ("sbuf", [128, 192], F), "uu": ("sbuf", [128, 192], F),
     "one": ("sbuf", [128, 24], F), "cnd": ("sbuf", [128, 23 * 184], H), "tb": ("sbuf", [128, 128], H), "tf": ("sbuf", [128, 128], F),
     "yo": ("sbuf", [128, 160], F),
-    "mu": ("psum", [128, 512], F), "mu1": ("psum", [128, 512], F), "mud": ("psum", [128, 512], F),
+    "mu": ("psum", [128, 512], F), "mu1": ("psum", [128, 512], F), "mud": ("psum", [128, 512], F), "sx": ("psum", [128, 512], F),
     "pf": ("psum", [128, 32, 4, 2, 2], F), "pt": ("psum", [128, 512], F), "cnt": ("psum", [128, 512], F),
 }
-SEMAPHORES = (["cv", "ca", "cp", "cg", "ld0", "ld1", "ld2", "ld3", "ld4", "dw", "dp", "dr", "dr2", "dy", "back", "sb", "rback", "rsb"]
+SEMAPHORES = (["cv", "ca", "cp", "cg", "ld0", "ld1", "ld2", "ld3", "ld4", "ld5", "dv", "dc", "dk", "dw", "dp", "dr", "dr2", "dy",
+               "back", "sb", "rback", "rsb"]
               + ["a%d" % t for t in range(R)] + ["s%d" % t for t in range(R)]
               + ["ra%d" % t for t in range(R)] + ["rs%d" % t for t in range(R)])
 
@@ -54,36 +62,36 @@ def _bits(engines):
     return m
 
 
-def _relay(src, dst, T, topo, nth):
+def _relay(src, dst, T, topo):
     if topo.may_write(src, dst):
         return None
     c = [k for k in topo.cores_of(src) if T.rank_of(k) is None and topo.may_write(k, dst)]
     c.sort(key=lambda k: (topo.die(k) != topo.die(src), k))
-    return c[nth]
+    return c[0]
 
 
 def _relay_program(g, core, T, topo):
     n = len(T.cores)
+    jobs = []
     for r in range(n):
         src = T.cores[r]
         for step in (1, 2):
             dst = T.cores[(r - step) % n]
-            if _relay(src, dst, T, topo, 1) == core:
-                eng = topo.engines(core, dst)[:8]
-                rid, pid = topo.addr(dst, core)
-                g.wait_ge(T.sem.rback, 8)
-                g.remote_dma(T.ew[:, 72 * (step - 1):72 * step], T.rb[:, :], T.sem.back, T.sem.rsb, pid, rid, _bits(eng))
-                g.wait_ge(T.sem.rsb, 8)
+            if _relay(src, dst, T, topo) == core:
+                c0 = EW + 72 * (step - 1)
+                jobs.append((1, dst, T.xb[:, c0:c0 + 72], T.rb[:, :], "rback", "back", "rsb"))
             dst = T.cores[(r + step) % n]
-            if _relay(src, dst, T, topo, 0) == core:
-                eng = topo.engines(core, dst)[:8]
-                rid, pid = topo.addr(dst, core)
+            if _relay(src, dst, T, topo) == core:
                 for t in range(R):
-                    g.wait_ge(T.sem["ra%d" % t], 8)
                     c0 = 128 * t + 64 * (step - 1)
-                    g.remote_dma(T.arr[:, c0:c0 + 64], T.rl[:, 64 * t:64 * t + 64], T.sem["a%d" % t], T.sem["rs%d" % t], pid, rid, _bits(eng))
-                for t in range(R):
-                    g.wait_ge(T.sem["rs%d" % t], 8)
+                    jobs.append((2 * t, dst, T.arr[:, c0:c0 + 64], T.rl[:, 64 * t:64 * t + 64], "ra%d" % t, "a%d" % t, "rs%d" % t))
+    jobs.sort(key=lambda j: j[0])
+    for turn, dst, there, here, came, lands, sent in jobs:
+        rid, pid = topo.addr(dst, core)
+        g.wait_ge(T.sem[came], 8)
+        g.remote_dma(there, here, T.sem[lands], T.sem[sent], pid, rid, _bits(topo.engines(core, dst)[:8]))
+    for job in jobs:
+        g.wait_ge(T.sem[job[6]], 8)
 
 
 def rank_program(g, core, T, topo):
@@ -154,13 +162,13 @@ def rank_program(g, core, T, topo):
         for x in regions.split():
             lastw[x] = (sem, 16, {}, None)
 
-    def send(dsts, nth, srcs, outs, relay_out, rsem, relay_sem, lsem, rd):
+    def send(dsts, srcs, outs, relay_out, rsem, relay_sem, lsem, rd):
         rd = rd.split()
         before("g", rd, [], False)
         used, trs = [], []
-        order = sorted(range(2), key=lambda j: _relay(core, dsts[j], T, topo, nth) is not None)
+        order = sorted(range(2), key=lambda j: _relay(core, dsts[j], T, topo) is not None)
         for j in order:
-            rel = _relay(core, dsts[j], T, topo, nth)
+            rel = _relay(core, dsts[j], T, topo)
             to = dsts[j] if rel is None else rel
             eng = [e for e in topo.engines(core, to) if e not in used][:8]
             used += eng
@@ -193,15 +201,18 @@ def rank_program(g, core, T, topo):
     def iota(out, pattern, base, cm, wr):
         op("g", lambda: g.iota(out, pattern, base, cm, allow_small_or_imprecise_dtypes=True), "", wr)
 
-    def spread(out, zt, src, c0, c1, rd, wr):
-        op("p", [(lambda i=i: P.matmul(out[:, c0:c1], zt[:, 15 - i:143 - i], src[:, 16 * c0 + i:16 * c1:16], i == 0, i == 15))
-                 for i in range(16)], rd, wr)
+    def spread(out, zt, src, s0, rd, wr):
+        s1 = s0 + 16 * out.shape[1]
+        op("p", [(lambda i=i: P.matmul(out, zt[:, 15 - i:143 - i], src[:, s0 + i:s1:16], i == 0, i == 15)) for i in range(16)], rd, wr)
 
     def col(j):
         return T.col[:, j:j + 1]
 
     def half(j):
         return T.h[:, 80 * j:80 * j + 80]
+
+    def px(j):
+        return T.sx[:, 80 * j:80 * j + 80]
 
     a_, b_ = slice(0, 80), slice(80, 160)
     X = [T.xa, T.xb]
@@ -212,162 +223,160 @@ def rank_program(g, core, T, topo):
     for t in range(R):
         landed("a%d" % t, "arr%d" % t)
 
-    dma("s", T.nui[:, 0:1], T.nu[:, :], "ld0", "", "nui")
-    dma("a", T.xa[:, 2560:2688], T.x[:, 0:128], "ld0", "", "xai")
-    dma("s", T.voi[:, :], T.vol[:, :], "ld1", "", "voi")
-    dma("a", T.nxi[:, :], T.nx[:, :], "ld1", "", "nxi")
-    dma("a", T.xa[:, 2688:2816], T.x[:, 2560:2688], "ld4", "", "xao")
-    dma("s", T.xn[:, :], T.x[:, :], "ld2", "", "xn0 xn1")
-    dma("a", T.lei[:, :], T.le[:, :], "ld3", "", "lei")
-    dma("s", T.lgi[:, :], T.lag[:, :], "ld3", "", "lgi")
+    dma("s", T.xa[:, 2560:2688], T.x[:, 2560:2688], "ld4", "", "xao")
+    dma("a", T.nui[:, 0:1], T.nu[:, :], "ld0", "", "nui")
+    dma("a", T.aw[:, 128:256], T.x[:, 0:128], "ld0", "", "xo0")
+    dma("s", T.nxi[:, :], T.nx[:, :], "ld1", "", "nxi")
+    dma("a", T.voi[:, :], T.vol[:, :], "ld5", "", "voi")
+    dma("s", T.xn[:, :], T.x[:, :], "ld2", "", "xn")
+
+    def send_fwd(t):
+        x = X[t % 2]
+        send(fwd, [x[:, 2560:2624], x[:, 2624:2688]], [T.arr[:, 128 * t:128 * t + 64], T.arr[:, 128 * t + 64:128 * t + 128]],
+             T.rl[:, 64 * t:64 * t + 64], "a%d" % t, "ra%d" % t, "s%d" % t, XN[t % 2] + "o")
 
     op("g", lambda: g.iota(T.pci[:, 0:1], [[1, 1]], 0, 1), "", "pci0")
     iota(T.mg[:, :], [[1, 8], [0, 16]], 0, 0, "mg")
     iota(T.ci[:, :], [[1, PW]], 0, 0, "ci")
-    iota(T.win[:, 4512:ROW], [[0, ROW - 4512]], 0, 0, "win3")
-    fill(T.win[:, 0:1504], 0.0, "win0")
-    cp("a", T.win[:, 1504:3008], T.win[:, 0:1504], "win0", "win1")
-    cp("a", T.win[:, 3008:4512], T.win[:, 0:1504], "win0", "win2")
-    fill(T.pk[:, :], 0.0, "pk")
-    fill(T.z[:, :], 0.0, "z")
+    send_fwd(0)
+    fill(T.xb[:, 0:EW], 0.0, "vw")
+    cp("a", T.win[:, 0:EW], T.xb[:, 0:EW], "vw", "win0")
     ts(T.pci[:, 1:2], T.pci[:, 0:1], 15, Op.bitwise_and, "pci0", "pci1")
     ts(T.pci[:, 2:3], T.pci[:, 0:1], 4, Op.logical_shift_right, "pci0", "pci2")
     ts(T.pci[:, 3:4], T.pci[:, 0:1], 16, Op.bitwise_and, "pci0", "pci3")
     ts(T.pci[:, 4:5], T.pci[:, 0:1], 31, Op.bitwise_and, "pci0", "pci4")
+    fill(T.pk[:, :], 0.0, "pk")
     cP, cI, cG, cH16, cI32, cOD, cS0, cSG, cNU, cH, cNH, cPP, cPM, cPI, cHO, cND = range(16)
     cp("v", T.col[:, 0:5], T.pci[:, 0:5], "pci0 pci1 pci2 pci3 pci4", "c0")
+    cp("v", col(cNU), T.nui[:, 0:1], "nui", "cnu")
     ts(col(cOD), col(cI), 1.0, Op.is_equal, "c0", "cod")
     ts(col(cS0), col(cI), 0.0, Op.is_equal, "c0", "cs0")
-    tt(col(cSG), col(cS0), col(cOD), Op.subtract, "cod cs0", "csg")
 
-    cp("v", col(cNU), T.nui[:, 0:1], "nui", "cnu")
     ts(T.bnu[:, :], T.mg[:, :], col(cG), Op.is_equal, "mg c0 cnu", "bnu", col(cNU), Op.mult)
+    tt(col(cSG), col(cS0), col(cOD), Op.subtract, "cod cs0", "csg")
+    op("p", lambda: P.matmul(T.cnt[:, 0:128], T.bnu[:, :], T.aw[:, 128:256], True, True), "bnu xo0", "cnt")
     cp("v", T.pk[:, 0:1], col(cNU), "cnu pk", "pk0")
     cp("v", T.pk[:, 136:137], col(cNU), "cnu pk", "pk1")
-    op("p", lambda: P.matmul(T.cnt[:, 0:128], T.bnu[:, :], T.xa[:, 2560:2688], True, True), "bnu xai", "cnt")
+    fill(T.vlb[:, :], 0.0, "vlb")
     ts(T.tb[:, :], T.cnt[:, 0:128], col(cSG), Op.mult, "cnt csg", "tb")
     ts(T.tf[:, :], T.cnt[:, 0:128], col(cOD), Op.mult, "cnt cod", "tf")
+    fill(T.z[:, :], 0.0, "z")
     tt(T.pk[:, 8:136], T.tf[:, :], T.tb[:, :], Op.add, "tb tf pk", "pk2")
-    send(bwd, 1, [T.pk[:, 0:72], T.pk[:, 72:144]], [T.ew[:, 0:72], T.ew[:, 72:144]], T.rb[:, :], "back", "rback", "sb", "pk pk0 pk1 pk2")
-
-    def send_fwd(t):
-        x = X[t % 2]
-        send(fwd, 0, [x[:, 2688:2752], x[:, 2752:2816]], [T.arr[:, 128 * t:128 * t + 64], T.arr[:, 128 * t + 64:128 * t + 128]],
-             T.rl[:, 64 * t:64 * t + 64], "a%d" % t, "ra%d" % t, "s%d" % t, XN[t % 2] + "o")
-    send_fwd(0)
-    iota(T.vh[:, 0:128], [[1, 128]], XP0 + CB, 0, "vh0")
+    send(bwd, [T.pk[:, 0:72], T.pk[:, 72:144]], [T.xb[:, EW:EW + 72], T.xb[:, EW + 72:EW + 144]], T.rb[:, :],
+         "back", "rback", "sb", "pk pk0 pk1 pk2")
+    before("s", [], ["pk2"], False)
+    dma("s", T.lei[:, :], T.le[:, :], "ld3", "", "lei")
+    dma("s", T.lgi[:, :], T.lag[:, :], "ld3", "", "lgi")
+    iota(T.vh[:, 256:384], [[32, 4], [0, 2], [1, 16]], XP0 + CB + 256, 0, "vh3")
+    iota(T.vh[:, 0:128], [[1, 128]], XP0 + CB + 128, 0, "vh1")
+    iota(T.win[:, 4512:ROW], [[0, ROW - 4512]], 0, 0, "win2")
     iota(T.oti[:, :], [[0, 23], [16, 8]], 0, 0, "oti")
-    iota(T.vh[:, 128:256], [[1, 128]], XP0 + CB + 128, 0, "vh1")
-    iota(T.vh[:, 13 * 128:14 * 128], [[1, 128]], XP0 + 22 * 128 - SMALL, 0, "vh2")
-    for j in range(11):
-        iota(T.vs[:, 256 * j:256 * j + 128], [[32, 4], [0, 2], [1, 16]], XP0 + CB + 256 * (j + 1), 0, "vs%d" % j)
-    for j in range(11):
-        iota(T.vs[:, 256 * j + 128:256 * j + 256], [[1, 128]], XP0 + CB + 256 * (j + 1) + 128, 0, "vo%d" % j)
+    iota(T.vh[:, 128:256], [[1, 128]], XP0 + 22 * 128 - SMALL, 0, "vh2")
+    iota(T.vs[:, :, 128:256], [[256, 11], [1, 128]], XP0 + CB + 384, 0, "vo")
+    am = [T.am[:, 128 * j:128 * j + 128] for j in range(5)]
+    low, high, ones, full = (T.hm[:, 128 * j:128 * j + 128] for j in range(4))
+    iota(low, [[0, 4], [-1, 2], [0, 16]], 1, 0, "hm0")
+    iota(high, [[0, 4], [1, 2], [0, 16]], 0, 0, "hm1")
+    iota(T.hm[:, 256:512], [[127, 2], [0, 128]], 1, 0, "hm2")
+    for out, src, shift, nm in ((am[0], low, 0, "am0"), (am[1], high, 16, "am1"), (am[2], low, -16, "am2"), (am[3], high, 0, "am3"),
+                                (am[4], ones, 0, "am4"), (T.ib[:, :], ones, 0, "ib"), (T.i128[:, :], full, 0, "i128")):
+        op("g", lambda: g.affine_select(out, src, [[-1, 128]], Op.is_equal, 0.0, shift, 1), "hm0 hm1 hm2", nm)
     iota(T.dfl[:, :], [[1, 2560]], CB + 128, 0, "dfl")
 
-    fill(T.vl[:, 160:164], 0.0, "vl1")
-    fill(T.vl[:, 164:PW], -1.0, "vl2")
-    cp("v", T.vl[:, 0:160], T.voi[:, :], "voi", "vl0")
-    dma("s", T.win[0::32, :], T.vl[:, :], "dw", "vl0 vl1 vl2", "win0 win1 win2 win3 wf0")
-    dma("s", T.win[16::32, :], T.vl[:, :], "dw", "vl0 vl1 vl2", "wf1")
+    cp("v", T.vlb[:, 0:160], T.voi[:, :], "voi vlb", "vlb")
+    dma("a", T.xb[0::16, 0:EW], T.vlb[:, :], "dv", "vlb", "vw")
     cp("v", T.nxu[:, :], T.nxi[:, :], "nxi", "nxu")
     ts(T.z[:, 15:143:16], T.ci[:, 0:8], col(cG), Op.is_equal, "ci c0 z", "z")
     ts(T.ti1[:, :], T.nxi[:, :], 4, Op.logical_shift_right, "nxi", "ti1")
     ts(T.ti2[:, :], T.nxi[:, :], 15, Op.bitwise_and, "nxi", "ti2")
-    ts(col(cHO), col(cH16), float(PW), Op.mult, "c0", "cho")
-    ts(col(cPI), col(cI32), float(PW), Op.mult, "c0", "cpi")
     ts(T.znu[:, :], T.z[:, :], col(cNU), Op.mult, "z cnu", "znu")
-    ts(T.zs[:, :], T.z[:, :], col(cS0), Op.mult, "z cs0", "zs")
-    ts(T.pm[:, 0:160], T.ti2[:, :], float(PW), Op.mult, "ti2 cho", "pm", col(cHO), Op.add)
-    tt(T.p1[:, 0:160], T.pm[:, 0:160], T.ti1[:, :], Op.add, "pm ti1", "p1")
-    cp("v", T.npu[:, :], T.p1[:, 0:160], "p1", "npu")
-    ts(T.eiu[:, :], T.nxi[:, :], 2552.0, Op.subtract, "nxi", "eiu", 7.0, Op.max)
+    MO, M1 = T.pt[:, 0:160], T.pt[:, 336:496]
+    ts(MO, T.nxi[:, :], 2560.0, Op.is_ge, "nxi", "tt")
+    ts(T.sx[:, 0:160], T.ti2[:, :], float(PW), Op.mult, "ti2", "px0 px1")
+    ts(T.pm[:, 0:160], T.nxi[:, :], float(EW + 8 - 2560), Op.add, "nxi", "pm")
+    spread(T.mu[:, 160:168], T.znu, T.aw, 128, "znu xo0", "mu")
+    tt(T.p1[:, 0:160], T.sx[:, 0:160], T.ti1[:, :], Op.add, "px0 px1 ti1", "p1")
+    tt(T.sx[:, 160:320], MO, T.pm[:, 0:160], Op.mult, "tt pm", "px2 px3")
+    ts(col(cHO), col(cH16), float(PW), Op.mult, "c0", "cho", -float(QC), Op.add)
+    tt(T.pm[:, 0:160], T.sx[:, 160:320], T.p1[:, 0:160], Op.max, "px2 px3 p1", "pm")
+    ts(col(cPI), col(cI32), float(PW), Op.mult, "c0", "cpi", -float(QC), Op.add)
+    cp("v", T.viu[:, :], T.pm[:, 0:160], "pm", "viu")
 
     def four(out, name, window, offs, rd):
         for j in range(4):
-            cp("va"[j % 2], out[:, 640 * j:640 * j + 640], window.indirect(offs[:, 40 * j:40 * j + 40]), rd, "%s%d" % (name, j))
-    four(T.xa, "xas", T.xn[:, :], T.nxu, "xn0 xn1 nxu")
-    spread(T.mu, T.znu, T.xa, 0, 80, "znu xas0 xas1", "mu")
-    spread(T.mu, T.znu, T.xa, 80, 168, "znu xas2 xas3 xai", "mu")
-    tt(T.dd[:, a_], T.lei[:, 160:240], T.lei[:, 0:80], Op.subtract, "lei", "dd")
-    tt(T.dd[:, b_], T.lei[:, 240:320], T.lei[:, 80:160], Op.subtract, "lei", "dd")
+            cp("va"[j % 2], out[:, 16 * CUT[j]:16 * CUT[j + 1]], window.indirect(offs[:, CUT[j]:CUT[j + 1]]), rd, "%s%d" % (name, j))
+
+    def contents(out, nm, zt, zn, src, sn):
+        spread(out[:, 0:CUT[2]], zt, src, 0, "%s %s0 %s1" % (zn, sn, sn), nm)
+        spread(out[:, CUT[2]:160], zt, src, 16 * CUT[2], "%s %s2 %s3" % (zn, sn, sn), nm)
+
+    four(T.xa, "xas", T.xn[:, :], T.nxu, "xn nxu")
+    contents(T.mu, "mu", T.znu, "znu", T.xa, "xas")
     ts(T.idn[:, :], T.ci[:, 0:160], 16.0, Op.mult, "ci c0", "idn", col(cI), Op.add)
-    ts(T.nxl[:, 160:168], T.ci[:, 168:176], col(cPI), Op.add, "ci cpi", "nxo", float(PK), Op.mult)
-    ts(T.nxl[:, 168:176], T.ci[:, 160:168], col(cPI), Op.add, "ci cpi", "nxo", float(PK), Op.mult)
-    fill(T.rs[:, 168:PW], 0.0, "rs0")
-    tt(half(10), T.dd[:, a_], T.dd[:, b_], Op.add, "dd", "ab")
-    ts(T.p1[:, 0:160], T.p1[:, 0:160], float(PK), Op.mult, "p1", "p1")
-    ts(T.idc[:, :], T.idn[:, :], float(CB), Op.add, "idn", "idc")
-    tt(T.bs[:, :], T.p1[:, 0:160], T.idn[:, :], Op.add, "p1 idn", "ba bb")
-    ts(T.ql[:, 0:8], T.ci[:, 0:8], col(cPI), Op.add, "ci cpi", "ql0")
-    fill(T.wl[:, 160:PW], 0.0, "wo")
-    fill(T.rs[:, 0:160], 0.0, "rs0")
-    ts(T.rs[:, 160:168], T.idn[:, 0:8], float(2688 - SMALL), Op.add, "idn", "rs1")
-    WALL = "win0 win1 win2 win3 wf0 wf1 wf2 wf3"
-    four(T.gb, "gb", T.win[:, :], T.npu, WALL + " npu")
-    spread(T.mu1, T.zs, T.gb, 0, 80, "zs gb0 gb1", "mu1")
-    spread(T.mu1, T.zs, T.gb, 80, 160, "zs gb2 gb3", "mu1")
-    for buf, nm, sem in ((T.pos, "pos", "dr"), (T.pos2, "pos2", "dr2")):
-        dma("s", buf[0::32, :], T.rs[:, :], sem, "rs0 rs1", nm + "r0")
-        dma("s", buf[16::32, :], T.rs[:, :], sem, "rs0 rs1", nm + "r1")
-    ts(col(cH), col(cH16), 1.0 / 16, Op.mult, "c0", "ch")
-    ts(col(cNH), col(cH16), 0.0, Op.is_equal, "c0", "cnh")
-    ts(col(cPP), col(cP), 16.0, Op.add, "c0", "cpp")
-    ts(col(cPM), col(cP), -16.0, Op.add, "c0", "cpm")
+    fill(T.rs[:, :], 0.0, "rs0")
+    ts(T.sx[:, 0:160], T.p1[:, 0:160], col(cHO), Op.add, "p1 cho", "px0 px1", float(PK), Op.mult)
+    ts(T.idc[:, :], T.idn[:, :], -float(SC), Op.add, "idn", "idc")
+    ts(T.rs[:, 160:168], T.idn[:, 0:8], float(2560 - SMALL), Op.add, "idn rs0", "rs1")
+    ts(T.rs[:, 0:8], T.idn[:, 0:8], float(XP0 + CB), Op.add, "idn rs0", "rs2")
+    WALL = "win0 win1 win2 wf0 wf1 wf2 wf3"
+
+    def reset(buf, nm, sem):
+        dma("s", buf[0::32, :], T.rs[:, :], sem, "rs0 rs1 rs2", nm + "r0")
+        dma("s", buf[16::32, :], T.rz[:, :], sem, "rz", nm + "r1")
+    fill(T.rz[:, :], 0.0, "rz")
+    reset(T.pos, "pos", "dr")
+    reset(T.pos2, "pos2", "dr2")
+    tt(T.bs[:, :], T.sx[:, 0:160], T.idc[:, :], Op.add, "px0 px1 idc", "ba bb")
+    four(T.gb, "gb", T.xb[:, 0:EW + 144], T.viu, "vw ew viu")
+    contents(T.mu1, "mu1", T.z, "z", T.gb, "gb")
+    cp("a", T.win[:, EW:4512], T.xn[:, 0:4512 - EW], "xn", "win1")
+    tt(T.dd[:, a_], T.lei[:, 160:240], T.lei[:, 0:80], Op.subtract, "lei", "dda")
+    tt(T.dd[:, b_], T.lei[:, 240:320], T.lei[:, 80:160], Op.subtract, "lei", "ddb")
     cp("v", T.lgx[:, 0:8], T.lgi[:, :], "lgi", "lgx")
     for w0, w1 in ((8, 16), (16, 32), (32, 64), (64, 128), (128, 192)):
         cp("a", T.lgx[:, w0:w1], T.lgx[:, 0:w1 - w0], "lgx", "lgx")
-    fill(T.one[:, :], 1.0, "one")
-    ts(T.e01[:, 0:8, 0], T.idn[:, 0:8], 2560.0, Op.add, "idn", "e0s")
-    ts(T.ot[:, :], T.oti[:, :], col(cI), Op.add, "oti c0", "ot")
-    am = [T.am[:, 128 * j:128 * j + 128] for j in range(5)]
-    c128 = T.ci[:, 0:128]
-    ts(am[0], c128, col(cP), Op.is_equal, "ci c0 cnh", "am0", col(cNH), Op.mult)
-    ts(am[1], c128, col(cPP), Op.is_equal, "ci cpp cnh", "am1", col(cNH), Op.mult)
-    ts(am[2], c128, col(cPM), Op.is_equal, "ci cpm ch", "am2", col(cH), Op.mult)
-    ts(am[3], c128, col(cP), Op.is_equal, "ci c0 ch", "am3", col(cH), Op.mult)
-    ts(am[4], c128, col(cP), Op.is_equal, "ci c0", "am4")
-    ts(T.ib[:, :], c128, col(cP), Op.is_equal, "ci c0", "ib")
-    ts(T.i128[:, :], c128, col(cP), Op.is_equal, "ci c0", "i128", 128.0, Op.mult)
+    ts(T.m1[:, :], T.nxi[:, :], 2560.0, Op.is_lt, "nxi", "m1s")
+    tt(T.c1[:, :], MO, T.dd[:, :], Op.mult, "tt dda ddb", "c1")
+    tt(half(0), T.bs[:, b_], T.bs[:, a_], Op.subtract, "ba bb", "dn")
+    ts(T.nxl[:, 160:168], T.ci[:, 168:176], col(cPI), Op.add, "ci cpi", "nxo", float(PK), Op.mult)
+    tt(T.d1[:, :], T.dd[:, :], T.c1[:, :], Op.subtract, "c1 dda ddb", "d1")
+    ts(T.nxl[:, 168:176], T.ci[:, 160:168], col(cPI), Op.add, "ci cpi", "nxt", float(PK), Op.mult)
+    fill(T.wl[:, 160:PW], 0.0, "wo")
+    tt(T.u1[:, :], T.mu1[:, 0:160], T.c1[:, :], Op.mult, "mu1 c1", "u1")
+    tt(T.vp[:, :], T.mu1[:, 0:160], T.m1[:, :], Op.mult, "mu1 m1s", "vp")
+    tt(half(3), T.u1[:, b_], T.u1[:, a_], Op.subtract, "u1", "rr")
+
+    def later_constants():
+        ts(T.z1[:, :], T.z[:, :], T.xb[:, EW:EW + 1], Op.mult, "z ew", "z1")
+        ts(col(cND), T.xb[:, EW:EW + 1], -2.0, Op.mult, "ew", "cnd", T.xb[:, EW + 136:EW + 137], Op.add)
+        ts(M1, T.nxi[:, :], 2624.0, Op.is_ge, "nxi", "m1")
+        ts(T.zd[:, :], T.z[:, :], col(cND), Op.mult, "z cnd", "zd")
+        tt(T.vv[:, :], T.vp[:, :], M1, Op.subtract, "vp m1", "va vb")
+        tt(half(10), T.dd[:, a_], T.dd[:, b_], Op.add, "dda ddb", "ab")
+        ts(T.idc[:, :], T.idn[:, :], float(CB), Op.add, "idn", "idc")
+        ts(T.ot[:, :], T.oti[:, :], col(cI), Op.add, "oti c0", "ot")
+        fill(T.one[:, :], 1.0, "one")
 
     def masks():
-        ts(T.m1[:, :], T.vv[:, :], 0.0, Op.is_gt, "va vb", "m1")
-        ts(T.vp[:, :], T.vv[:, :], 0.0, Op.max, "va vb", "vp")
-        tt(T.d1[:, :], T.m1[:, :], T.dd[:, :], Op.mult, "m1 dd", "d1")
-        tt(half(0), T.bs[:, b_], T.bs[:, a_], Op.subtract, "ba bb", "dn")
-
-    def cross_a():
-        tt(T.pp[:, :], T.mu[:, 0:160], T.d1[:, :], Op.mult, "mu d1", "pp")
-        tt(T.wv[:, :], T.mu[:, 0:160], T.vp[:, :], Op.mult, "mu vp", "wv")
-        tt(half(1), T.pp[:, a_], T.pp[:, b_], Op.subtract, "pp", "qq")
-        tt(half(2), T.wv[:, b_], T.wv[:, a_], Op.subtract, "wv", "dwv")
-
-    def bound(e, rd):
-        tt(T.eb[:, :], e, T.dd[:, :], Op.mult, rd + " dd", "eb")
-        tt(half(3), T.eb[:, b_], T.eb[:, a_], Op.subtract, "eb", "rr")
+        op("a", lambda: A.activation(T.m1[:, :], T.vv[:, :], Act.Relu, bias=1.0, scale=-1.0), "va vb", "m1s")
+        op("a", lambda: A.activation(T.m2[:, :], T.vv[:, :], Act.Relu, scale=-1.0), "va vb", "m2s")
 
     S = T.pt[:, 256:336]
-
-    def swap(dst, src, d, j, rd, wa, wb):
-        tt(half(j), d, S, Op.mult, rd + " ss", "t%d" % j)
-        tt(dst[:, a_], src[:, a_], half(j), Op.add, rd + " t%d" % j, wa)
-        tt(dst[:, b_], src[:, b_], half(j), Op.subtract, rd + " t%d" % j, wb)
 
     def rows(f, src, q2, rd):
         dma("s", T.win[f::32, :], src[:, :], "dw", rd, "wf%d" % (2 * f))
         dma(q2, T.win[16 + f::32, :], src[:, :], "dw", rd, "wf%d" % (2 * f + 1))
 
     def unpack(out, in_, rd, wr):
-        ts(out, in_, 1.0 / PK, Op.mult, rd, wr, -0.456, Op.add)
+        ts(out, in_, 1.0 / PK, Op.mult, rd, wr, float(QC), Op.add)
 
     def slots(src, nm, x, k0, k1, rd):
         c = slice(8 * k0, 8 * k1)
 
-        return [lambda: unpack(T.sn[:, c], src, nm, "sn%d" % k0),
-                lambda: ts(T.sm[:, c], T.sn[:, c], -float(PK), Op.mult, "sn%d" % k0, "sm%d" % k0),
-                lambda: tt(T.sm[:, c], src, T.sm[:, c], Op.add, nm + " sm%d" % k0, "sm%d" % k0),
-                lambda: cp("v", T.xl[:, c], T.sm[:, c], "sm%d" % k0, "xl%d" % k0),
-                lambda: cp("a", T.aw[:, 128 * (k0 + 1):128 * (k1 + 1)], x[:, 0:2688].indirect(T.xl[:, c]), rd + " xl%d" % k0, "xo%d" % k0)]
+        return [lambda: ts(T.sm[:, c], src, RND, Op.add, nm, "sm%d" % k0, RND, Op.subtract),
+                lambda: tt(T.sm[:, c], src, T.sm[:, c], Op.subtract, nm + " sm%d" % k0, "sm%d" % k0),
+                lambda: ts(T.xl[:, c], T.sm[:, c], float(SC), Op.add, "sm%d" % k0, "xl%d" % k0),
+                lambda: cp("a", T.aw[:, 128 * (k0 + 1):128 * (k1 + 1)], x[:, 0:2560].indirect(T.xl[:, c]), rd + " xl%d" % k0, "xo%d" % k0)]
 
     def scatter(buf, nm, offs, vals, rd):
         op("a", lambda: A.activation(buf[:, :].indirect(offs), vals, Act.Silu), rd, nm + "r0 " + nm + "r1")
@@ -380,191 +389,210 @@ def rank_program(g, core, T, topo):
         j = (k - 2) // 2 * 2 + u
         return T.tte[:, 2 * j:2 * j + 2, 0::16] if k % 2 == 0 else T.tto[:, 4 * j:4 * j + 4, 0]
 
-    def home_even(k0, k1):
+    def home(k0, k1, both):
         j0, j1 = (k0 - 2) // 2, (k1 - 2) // 2 + 1
-        rd = " ".join("tt%d tt%db" % (k, k) for k in range(k0, k1 + 1, 2)) + " am0 am1 am2 am3"
-        if k1 <= 16:
-            op("p", [(lambda hc=hc, hh=hh: P.matmul(T.pg[:, k0:k1 + 1:2, :, hc], am[2 * hc + hh],
-                                                    T.tte[:, 4 * j0:4 * j1, 16 * hh], hh == 0, hh == 1))
-                     for hc in range(2) for hh in range(2)], rd, "pg")
-        op("p", [(lambda hc=hc, hh=hh: P.matmul(T.pf[:, k0:k1 + 1:2, :, hc, :], am[2 * hc + hh],
-                                                T.tte[:, 4 * j0:4 * j1, 16 * hh:16 * hh + 2], hh == 0, hh == 1))
-                 for hc in range(2) for hh in range(2)], rd, "pf")
-
-    def home_odd(k0, k1):
-        j0, j1 = (k0 - 2) // 2, (k1 - 2) // 2 + 1
-        rd = " ".join("tt%d tt%db" % (k, k) for k in range(k0, k1 + 1, 2)) + " am4"
-        op("p", lambda: P.matmul(T.pf[:, k0:k1 + 1:2, :, :, :], am[4], T.tto[:, 8 * j0:8 * j1, 0:2], True, True), rd, "pf")
-        if k1 <= 16:
-            op("p", lambda: P.matmul(T.pg[:, k0:k1 + 1:2, :, :], am[4], T.tto[:, 8 * j0:8 * j1, 0], True, True), rd, "pg")
-
-    scatter(T.pos, "pos", T.ql[:, 0:8], T.vh[:, 0:128], "ql0 vh0")
-    four(T.gb2, "gc", T.ew[:, :], T.eiu, "ew eiu")
-    spread(T.mud, T.z, T.gb2, 0, 80, "z gc0 gc1", "mud")
-    spread(T.mud, T.z, T.gb2, 80, 160, "z gc2 gc3", "mud")
-    cp("v", T.vv[:, :], T.mu1[:, 0:160], "mu1", "va vb")
-    masks()
-    cross_a()
-    ts(T.z1[:, :], T.z[:, :], T.ew[:, 0:1], Op.mult, "z ew", "z1")
-    tt(col(cND), T.ew[:, 136:137], T.ew[:, 0:1], Op.subtract, "ew", "cnd")
-    ts(T.zd[:, :], T.z[:, :], col(cND), Op.mult, "z cnd", "zd")
-    bound(T.mud[:, 0:160], "mud")
+        ks = slice(k0, k1 + 1, 2)
+        rd = " ".join("tt%d tt%db" % (k, k) for k in range(k0, k1 + 1, 2)) + " am0 am1 am2 am3 am4"
+        if k0 % 2 == 0:
+            calls = [(lambda hc=hc, hh=hh: P.matmul(
+                T.pf[:, ks, :, hc, :] if both else T.pg[:, ks, :, hc], am[2 * hc + hh],
+                T.tte[:, 4 * j0:4 * j1, 16 * hh:16 * hh + 2] if both else T.tte[:, 4 * j0:4 * j1, 16 * hh], hh == 0, hh == 1))
+                for hc in range(2) for hh in range(2)]
+        else:
+            calls = [lambda: P.matmul(T.pf[:, ks, :, :, :] if both else T.pg[:, ks, :, :], am[4],
+                                      T.tto[:, 8 * j0:8 * j1, 0:2] if both else T.tto[:, 8 * j0:8 * j1, 0], True, True)]
+        op("p", calls, rd, "pf" if both else "pg")
 
     for t in range(R):
         last = t == R - 1
         x, xn, y, yn = X[t % 2], XN[t % 2], X[1 - t % 2], XN[1 - t % 2]
         xs = " ".join("%ss%d" % (xn, j) for j in range(4))
         pos, pn = (T.pos2, "pos2") if last else (T.pos, "pos")
-        if t > 0:
-            cross_a()
-        tt(S, half(1), half(3), Op.is_lt, "qq rr", "ss")
-        if not last:
-            spread(T.mu1, T.z1, x, 0, 160, "z1 " + xs, "mu1")
-            spread(T.mud, T.zd, x, 0, 160, "zd " + xs, "mud")
-        q2 = "s" if last else "a"
-        tt(half(5), half(0), S, Op.mult, "dn ss", "t5")
+        arrival = T.arr[:, 128 * t:128 * t + 128]
+        tt(px(0), T.mu[:, a_], T.d1[:, a_], Op.mult, "mu d1", "px0")
+        tt(half(1), T.mu[:, b_], T.d1[:, b_], Op.mult, "mu d1", "pb")
+        tt(T.wv[:, a_], T.mu[:, a_], T.vp[:, a_], Op.mult, "mu vp", "wva")
+        tt(px(1), px(0), half(1), Op.subtract, "px0 pb", "px1")
+        tt(px(2), T.mu[:, b_], T.vp[:, b_], Op.mult, "mu vp", "px2")
+        tt(S, px(1), half(3), Op.is_lt, "px1 rr", "ss")
+        tt(half(2), px(2), T.wv[:, a_], Op.subtract, "wva px2", "dwv")
+        tt(px(0), half(0), S, Op.mult, "dn ss", "px0")
         tt(half(6), half(2), S, Op.mult, "dwv ss", "t6")
-        tt(T.nxl[:, a_], T.bs[:, a_], half(5), Op.add, "ba t5", "nxa")
-        tt(T.nxl[:, b_], T.bs[:, b_], half(5), Op.subtract, "bb t5", "nxb")
-        rows(0, T.nxl, q2, "nxa nxb nxo")
-        tt(T.wl[:, a_], T.wv[:, a_], half(6), Op.add, "wv t6", "wa")
-        tt(T.wl[:, b_], T.wv[:, b_], half(6), Op.subtract, "wv t6", "wb")
+        tt(T.nxl[:, a_], T.bs[:, a_], px(0), Op.add, "ba px0", "nxa")
+        tt(T.nxl[:, b_], T.bs[:, b_], px(0), Op.subtract, "bb px0", "nxb")
+        q2 = "s" if last else "a"
+        rows(0, T.nxl, q2, "nxa nxb nxo nxt win0 win1 win2")
+        tt(T.wl[:, b_], px(2), half(6), Op.subtract, "px2 t6", "wb")
+        tt(T.wl[:, a_], T.wv[:, a_], half(6), Op.add, "wva t6", "wa")
         rows(1, T.wl, q2, "wa wb wo")
+        dma("s", T.aw[:, 0:128], arrival, "dc", "arr%d" % t, "aw")
         unpack(T.ql[:, 8:16], T.nxl[:, 0:8], "nxa", "ql1")
-        scatter(pos, pn, T.ql[:, 8:16], T.vh[:, 128:256], "ql1 vh1")
-        if t == 0:
-            op("a", [(lambda j=j: A.activation(T.vs[:, 256 * j:256 * j + 128], T.vs[:, 256 * j:256 * j + 128], Act.Identity, bias=col(cH16)))
-                     for j in range(11)], "c0 " + " ".join("vs%d" % j for j in range(11)), "vs")
-        if t == R - 2:
-            unpack(T.npu[:, :], T.nxl[:, 0:160], "nxa nxb", "npu")
-            scatter(T.pos2, "pos2", T.npu[:, 0:48], T.dfl[:, 0:768], "npu dfl")
-        tt(T.e01[:, 0:8, 1], T.mu[:, 160:168], T.vl[:, 0:8], Op.mult, "mu vl0", "e0w")
-        cp("v", T.e01[:, 8:16, 1], T.wl[:, 0:8], "wa", "e1w")
-        cp("v", T.e01[:, 8:16, 0], T.nxl[:, 0:8], "nxa", "e1s")
-        op("p", lambda: P.matmul(T.pf[:, 0:2, :, :, :], am[4], T.e01[:, :, :], True, True), "am4 e0w e0s e1w e1s", "pf")
-        op("p", lambda: P.matmul(T.pg[:, 0:2, :, :], am[4], T.e01[:, :, 0], True, True), "am4 e0s e1s", "pg")
-        op("p", lambda: P.matmul(T.cnt[:, 8:192], T.ib[:, :], T.ot[:, :], True, False), "ib ot", "cnt")
+        first = slots(T.nxl[:, 0:8], "nxa", x, 1, 2, xs)
+        first[0]()
+        scatter(pos, pn, T.ql[:, 8:16], T.vh[:, 0:128], "ql1 vh1")
+        tt(T.pf[:, 0, :, :, 1], T.mu[:, 160:168], T.voi[:, 0:8], Op.mult, "mu voi", "pf")
+        first[1]()
+        cp("v", T.pf[:, 1, :, :, 1], T.wl[:, 0:8], "wa", "pf")
+        first[2]()
         if t == 0:
             cp("v", half(7), S, "ss", "sc")
         else:
             tt(half(7), half(7), S, Op.not_equal, "sc ss", "sc")
-        if not last:
-            ts(half(4), S, 1280.0, Op.mult, "ss", "t4")
-            tt(half(8), T.vv[:, b_], T.vv[:, a_], Op.subtract, "va vb", "dv")
-            ts(T.ea[:, :], T.vv[:, :], 0.0, Op.is_le, "va vb", "ea eab")
-            tt(half(9), half(8), S, Op.mult, "dv ss", "t9")
-            ts(T.m2[:, :], T.vv[:, :], 0.0, Op.is_lt, "va vb", "m2")
-            tt(T.bs[:, a_], T.nxl[:, a_], half(4), Op.subtract, "nxa t4", "ba")
-            tt(T.vv[:, a_], T.vv[:, a_], half(9), Op.add, "va t9", "va")
-            tt(T.vv[:, b_], T.vv[:, b_], half(9), Op.subtract, "vb t9", "vb")
-            tt(T.bs[:, b_], T.nxl[:, b_], half(4), Op.add, "nxb t4", "bb")
+        if t == 0:
+            later_constants()
             masks()
-            tt(T.dfp[:, a_], T.idc[:, a_], half(4), Op.add, "idc t4", "dfa")
-            tt(T.dfp[:, b_], T.idc[:, b_], half(4), Op.subtract, "idc t4", "dfb")
-            tt(half(11), half(10), S, Op.mult, "ab ss", "sab")
+            op("a", lambda: A.activation(T.vs[:, 0, 0:128], T.vh[:, 256:384], Act.Identity, bias=col(cH16)), "vh3 c0", "vs0")
+            op("a", [(lambda j=j: A.activation(T.vs[:, j, 0:128], T.vs[:, 0, 0:128], Act.Identity, bias=256.0 * j))
+                     for j in range(1, 11)], "vs0", "vs")
+        first[3]()
+        if not last:
+            spread(T.mu1[:, 0:160], T.z1, x, 0, "z1 " + xs, "mu1")
+            spread(T.mud[:, 0:160], T.zd, x, 0, "zd " + xs, "mud")
+        if t == R - 2:
+            unpack(T.npu[:, :], T.nxl[:, 0:160], "nxa nxb", "npu")
+            scatter(T.pos2, "pos2", T.npu[:, 0:48], T.dfl[:, 0:768], "npu dfl")
+        if not last:
+            ts(px(1), S, 1280.0, Op.mult, "ss", "px1")
+            tt(half(8), T.vv[:, b_], T.vv[:, a_], Op.subtract, "va vb", "dv")
+            tt(px(3), half(10), S, Op.mult, "ab ss", "px3")
+            tt(px(0), half(8), S, Op.mult, "dv ss", "px0")
+            tt(px(4), px(3), T.dd[:, a_], Op.subtract, "px3 dda", "px4")
+            tt(px(5), T.dd[:, b_], px(3), Op.subtract, "px3 ddb", "px5")
+            tt(T.bs[:, a_], T.nxl[:, a_], px(1), Op.subtract, "nxa px1", "ba")
+            tt(T.bs[:, b_], T.nxl[:, b_], px(1), Op.add, "nxb px1", "bb")
+            tt(T.c1[:, :], T.sx[:, 320:480], T.m1[:, :], Op.mult, "m1s px4 px5", "c1")
+            tt(T.c2[:, :], T.sx[:, 320:480], T.m2[:, :], Op.mult, "m2s px4 px5", "c2")
+            tt(T.vv[:, a_], T.vv[:, a_], px(0), Op.add, "va px0", "va")
+            tt(T.vv[:, b_], T.vv[:, b_], px(0), Op.subtract, "vb px0", "vb")
+            tt(T.dfp[:, a_], T.idc[:, a_], px(1), Op.add, "idc px1", "dfa")
+            tt(T.dfp[:, b_], T.idc[:, b_], px(1), Op.subtract, "idc px1", "dfb")
+            tt(half(0), T.bs[:, b_], T.bs[:, a_], Op.subtract, "ba bb", "dn")
         else:
             tt(half(8), T.nxi[:, b_], T.nxi[:, a_], Op.subtract, "nxi", "dv")
             tt(half(9), half(8), half(7), Op.mult, "dv sc", "t9")
             tt(T.yo[:, a_], T.nxi[:, a_], half(9), Op.add, "nxi t9", "yoa")
             tt(T.yo[:, b_], T.nxi[:, b_], half(9), Op.subtract, "nxi t9", "yob")
-        early = slots(T.pg[:, 0:17, :, :], "pg", x, 0, 17, xs + " " + xn + "i")
+        early = slots(T.pg[:, 2:KB, :, :], "pg", x, 2, KB, xs)
         for k in range(1, 23):
             e = k + 1
             rp = [T.rep[:, 128 * (k % 2) + 64 * u:128 * (k % 2) + 64 * u + 64] for u in range(2)]
             nm = ["ql%d" % k, "ql%db" % k if k > 1 else "ql1"]
             for u in range(2):
                 cp("v", rp[u], T.win[:, :].indirect(T.ql[:, 8 * k + 4 * u:8 * k + 4 * u + 4]), WALL + " " + nm[u], "rep%d%d" % (k % 2, u))
+            if e in (KB + 1, KB + 2):
+                early[2 * (e - KB - 1)]()
             for u in range(2):
                 op("v", lambda: V.transpose(entry(e, u), rp[u]), "rep%d%d" % (k % 2, u), "tt%d%s" % (e, "b" * u))
+            if e == KB + 1:
+                early[1]()
             for u in range(2):
                 unpack(T.ql[:, 8 * e + 4 * u:8 * e + 4 * u + 4], entry_q(e, u), "tt%d%s" % (e, "b" * u), "ql%d%s" % (e, "b" * u))
             if e == 23 and not last:
-                scatter(pos, pn, T.ql[:, 8 * e:8 * e + 8], T.vh[:, 13 * 128:14 * 128], "ql23 ql23b vh2")
+                scatter(pos, pn, T.ql[:, 8 * e:8 * e + 8], T.vh[:, 128:256], "ql23 ql23b vh2")
             elif e >= 22:
-                scatter(pos, pn, T.ql[:, 8 * e:8 * e + 8], T.vs[:, 128 * (e - 2):128 * (e - 1)], "ql%d ql%db vs vo10" % (e, e))
+                scatter(pos, pn, T.ql[:, 8 * e:8 * e + 8], T.vs[:, 10, 128 * (e - 22):128 * (e - 21)], "ql%d ql%db vs vo" % (e, e))
             elif e % 2 == 1:
-                scatter(pos, pn, T.ql[:, 8 * e - 8:8 * e + 8], T.vs[:, 128 * (e - 3):128 * (e - 1)],
-                        "ql%d ql%db ql%d ql%db vs vo%d" % (e - 1, e - 1, e, e, (e - 3) // 2))
-            if e == 12:
-                cp("a", T.aw[:, 0:128], T.arr[:, 128 * t:128 * t + 128], "arr%d" % t, "aw")
+                scatter(pos, pn, T.ql[:, 8 * e - 8:8 * e + 8], T.vs[:, (e - 3) // 2, :],
+                        "ql%d ql%db ql%d ql%db vs0 vs vo" % (e - 1, e - 1, e, e))
+            if e == KB + 2:
+                early[3]()
+            if e in (KB - 2, KB - 1):
+                home(2 + e % 2, e, False)
+            if e == KB + 1:
+                home(2, KB, True)
+                home(3, KB + 1, True)
+                op("p", lambda: P.matmul(T.cnt[:, 8:192], T.ib[:, :], T.ot[:, :], True, False), "ib ot", "cnt")
                 if not last:
-                    cp("a", y[:, 2560:2688], T.arr[:, 128 * t:128 * t + 128], "arr%d" % t, yn + "i")
-            if e == 15:
-                home_odd(3, 15)
-            if e == 16:
-                home_even(2, 16)
-            if e >= 20:
-                early[e - 20]()
+                    spread(T.mu[:, 160:168], T.znu, T.arr, 128 * t, "znu arr%d" % t, "mu")
             if e == 21:
-                home_odd(17, 21)
+                home(KB + 3, 21, True)
             if e == 22:
-                home_even(18, 22)
+                home(KB + 2, 22, True)
             if e == 23:
-                home_odd(23, 23)
+                home(23, 23, True)
             if e == 3 and last:
                 dma("s", T.yn[:, :], T.yo[:, :], "dy", "yoa yob", "")
-                dma("s", T.y[:, 0:128], T.arr[:, 128 * t:128 * t + 128], "dy", "arr%d" % t, "")
+                dma("s", T.y[:, 0:128], arrival, "dy", "arr%d" % t, "")
         dma("s", T.p1[:, :], pos[0::32, :], "dp", pn + "r0", "p1")
         dma("s", T.p2[:, :], pos[16::32, :], "dp", pn + "r1", "p2")
-        early[4]()
+        if not last:
+            tt(T.u1[:, :], T.mu1[:, 0:160], T.c1[:, :], Op.mult, "mu1 c1", "u1")
+            tt(T.sx[:, 0:160], T.mud[:, 0:160], T.c2[:, :], Op.mult, "mud c2", "px0 px1")
+            ts(T.vp[:, :], T.vv[:, :], 0.0, Op.max, "va vb", "vp")
+            tt(T.u1[:, :], T.u1[:, :], T.sx[:, 0:160], Op.add, "u1 px0 px1", "u1")
+        late = slots(T.pf[:, KB:23, :, :, 0], "pf", x, KB, 23, xs)
+        late[0]()
         op("v", [(lambda c=c: V.tensor_tensor_scan(T.pt[:, c:192:8], T.one[:, :], T.pf[:, 0:24, c // 2, c % 2, 1], 0.0, Op.mult, Op.add))
                  for c in range(8)], "pf one", "tt")
-        late = slots(T.pf[:, 17:23, :, :, 0], "pf", x, 17, 23, xs + " " + xn + "i")
-        late[0]()
-        tt(T.uu[:, :], T.pt[:, 0:192], T.lgx[:, :], Op.subtract, "tt lgx", "uu")
         late[1]()
+        tt(T.uu[:, :], T.pt[:, 0:192], T.lgx[:, :], Op.subtract, "tt lgx", "uu")
+        late[2]()
+        late[3]()
         for d in range(1, 24):
-            if d in (2, 3, 4):
-                late[d]()
             cd = T.cnd[:, 184 * (d - 1):184 * (d - 1) + 192 - 8 * d]
             tt(cd, T.pt[:, 0:192 - 8 * d], T.uu[:, 8 * d:192], Op.is_le, "tt uu", "cd%d" % d)
             op("p", lambda: P.matmul(T.cnt[:, 8 * d:192], T.i128[:, :], cd, False, d == 23), "i128 cd%d" % d, "cnt")
-        cp("v", T.sp[:, :], T.cnt[:, 8:192], "cnt", "sp")
-        sv = SV + 12 if last else SV
-        cp("a", x[:, XP0 + 16 * sv:XW], T.aw[:, :].indirect(T.sp[:, sv:184]), "aw xo0 xo17 sp", xn + "p1")
-        tt(T.pm[:, :], T.p1[:, :], T.p2[:, :], Op.max, "p1 p2", "pm pmo")
-        if t < R - 2:
-            dma("s", pos[0::32, :], T.rs[:, :], "dr", "rs0 rs1", pn + "r0")
-            dma("s", pos[16::32, :], T.rs[:, :], "dr", "rs0 rs1", pn + "r1")
+        if not last:
+            ts(M1, T.vv[:, :], 0.0, Op.is_gt, "va vb", "m1")
+        sv = SV - 4 if last else SV
+        cp("v", T.sp[:, sv:184], T.cnt[:, 8 + sv:192], "cnt", "spa")
+        cp("v", T.sp[:, 0:sv], T.cnt[:, 8:8 + sv], "cnt", "spv")
+        AW = "aw xo0 xo1 xo2 xo%d" % KB
+        if t == 1:
+            for q in "va":
+                before(q, [], ["ew"], True)
+        cp("a", x[:, XP0 + 16 * sv:XW], T.aw[:, :].indirect(T.sp[:, sv:184]), AW + " spa", xn + "p1")
+
         def part(j, c0, c1):
-            cp("v", x[:, XP0 + 16 * c0:XP0 + 16 * c1], T.aw[:, :].indirect(T.sp[:, c0:c1]), "aw xo0 xo17 sp", xn + "p%d" % j)
-        part(0, 0, 16)
-        tt(T.pm[:, 160:168], T.pm[:, 160:168], T.pm[:, 168:176], Op.max, "pmo", "pmo")
+            cp("v", x[:, XP0 + 16 * c0:XP0 + 16 * c1], T.aw[:, :].indirect(T.sp[:, c0:c1]), AW + " spv", xn + "p%d" % j)
+        if t < R - 2:
+            reset(pos, pn, "dr")
         if not last:
-            tt(T.pm[:, 0:160], T.pm[:, 0:160], T.dfp[:, :], Op.max, "pm dfa dfb", "pm")
-            ts(T.p1[:, 160:168], T.pm[:, 160:168], float(CB), Op.is_lt, "pmo", "p1", float(CB + SMALL), Op.mult)
-            part(2, 16, 32)
-            tt(T.pm[:, 160:168], T.pm[:, 160:168], T.p1[:, 160:168], Op.add, "pmo p1", "pmo")
-            part(3, 32, 48)
-            ts(T.piu[:, 0:168], T.pm[:, 0:168], float(CB), Op.subtract, "pm pmo", "piu", 0.25, Op.add)
-            part(4, 48, sv)
+            PM = T.pg[:, 0:20, :, :]
+            op("p", [lambda: P.matmul(PM, am[4], T.p1[:, 0:160], True, False),
+                     lambda: P.matmul(PM, am[4], T.p2[:, 0:160], False, True)], "am4 p1 p2", "pg")
+            part(0, 16, sv)
+            tt(T.pm[:, 0:160], PM, T.dfp[:, :], Op.max, "pg dfa dfb", "pm")
+            part(2, 0, 8)
+            ts(T.piu[:, 0:160], T.pm[:, 0:160], float(CB), Op.subtract, "pm", "piu", 0.25, Op.add)
+            part(3, 8, 16)
         else:
-            part(2, 16, 32)
-            ts(T.piu[:, 8:168], T.pm[:, 8:168], float(CB + 128), Op.subtract, "pm pmo", "piu", 0.25, Op.add)
-            part(3, 32, sv)
-        xall = "%s %si %so %sp0 %sp1 %sp2 %sp3 %sp4 piu" % (xs, xn, xn, xn, xn, xn, xn, xn)
+            part(0, 16, sv)
+            tt(T.sx[:, 0:PW], T.p1[:, :], T.p2[:, :], Op.max, "p1 p2", "px0 px1 px2")
+            part(2, 0, 8)
+            ts(T.piu[:, 8:160], T.sx[:, 8:160], float(CB + 128), Op.subtract, "px0 px1", "piu", 0.25, Op.add)
+            cp("v", T.pm[:, 168:176], T.sx[:, 168:176], "px2", "pmt")
+            part(3, 8, 16)
+            tt(T.pm[:, 160:168], T.sx[:, 160:168], T.pm[:, 168:176], Op.max, "px2 pmt", "pmo")
+        xall = "%s %so %sp0 %sp1 %sp2 %sp3 piu" % (xs, xn, xn, xn, xn, xn)
         if not last:
+            dma("s", T.aw[:, 128:256], arrival, "dk", "arr%d" % t, "xo0")
+            if t == 0:
+                for q in "va":
+                    before(q, [], ["vw"], True)
             four(y, yn + "s", x[:, :], T.piu, xall)
-            spread(T.mu, T.znu, y, 0, 80, "znu %ss0 %ss1" % (yn, yn), "mu")
-            spread(T.mu, T.znu, y, 80, 168, "znu %ss2 %ss3 %si" % (yn, yn, yn), "mu")
-            cp("a", y[:, 2688:2816], x[:, :].indirect(T.piu[:, 160:168]), xall, yn + "o")
-            send_fwd(t + 1)
+            contents(T.mu, "mu", T.znu, "znu", y, yn + "s")
             if t < R - 2:
-                scatter(T.pos, "pos", T.ql[:, 0:8], T.vh[:, 0:128], "ql0 vh0")
-            else:
+                masks()
+            tt(T.pm[:, 160:176], T.p1[:, 160:176], T.p2[:, 160:176], Op.max, "p1 p2", "pmt")
+            tt(T.d1[:, :], M1, T.dd[:, :], Op.mult, "m1 dda ddb", "d1")
+            tt(T.pm[:, 160:168], T.pm[:, 160:168], T.pm[:, 168:176], Op.max, "pmt", "pmo")
+            tt(half(3), T.u1[:, a_], T.u1[:, b_], Op.add, "u1", "rr")
+            ts(T.p1[:, 160:168], T.pm[:, 160:168], float(CB), Op.is_lt, "pmo", "p1", float(CB + SMALL), Op.mult)
+            tt(T.pm[:, 160:168], T.pm[:, 160:168], T.p1[:, 160:168], Op.add, "pmo p1", "pmo")
+            ts(T.piu[:, 160:168], T.pm[:, 160:168], float(CB), Op.subtract, "pmo", "pio", 0.25, Op.add)
+            cp("a", y[:, 2560:2688], x[:, :].indirect(T.piu[:, 160:168]), xall + " pio", yn + "o")
+            send_fwd(t + 1)
+            if t == R - 2:
                 scatter(T.pos2, "pos2", T.npu[:, 48:160], T.dfl[:, 768:2560], "npu dfl")
-            tt(T.ea[:, :], T.mu1[:, 0:160], T.ea[:, :], Op.mult, "mu1 ea eab", "ea eab")
-            tt(T.m2[:, :], T.mud[:, 0:160], T.m2[:, :], Op.mult, "mud m2", "m2")
-            tt(T.ea[:, :], T.ea[:, :], T.m2[:, :], Op.add, "ea eab m2", "ea eab")
-            tt(half(8), T.ea[:, a_], T.ea[:, b_], Op.subtract, "ea eab", "dv")
-            tt(T.eb[:, :], T.ea[:, :], T.dd[:, :], Op.mult, "ea eab dd", "eb")
-            tt(half(12), half(8), half(11), Op.mult, "dv sab", "g1")
-            tt(half(13), T.eb[:, b_], T.eb[:, a_], Op.subtract, "eb", "r0")
-            tt(half(3), half(12), half(13), Op.add, "g1 r0", "rr")
         else:
-            for j in range(4):
-                c0 = 128 + 640 * j
-                cp("va"[j % 2], T.xn[:, c0:c0 + 640], x[:, :].indirect(T.piu[:, 8 + 40 * j:48 + 40 * j]), xall, "y%d" % j)
-                dma("s", T.y[:, c0:c0 + 640], T.xn[:, c0:c0 + 640], "dy", "y%d" % j, "")
+            for j in range(6):
+                if j == 2:
+                    ts(T.piu[:, 160:168], T.pm[:, 160:168], float(CB + 128), Op.subtract, "pmo", "pio", 0.25, Op.add)
+                cp("va"[j % 2], T.xn[:, 16 * YC[j]:16 * YC[j + 1]], x[:, :].indirect(T.piu[:, YC[j]:YC[j + 1]]),
+                   xall + " pio" * (j == 5), "y%d" % j)
+                if j % 2:
+                    c = slice(16 * YC[j - 1], 16 * YC[j + 1])
+                    dma("s", T.y[:, c], T.xn[:, c], "dy", "y%d y%d" % (j - 1, j), "")
     for s in sorted(cnt):
         need("g", (s, cnt[s], {}, None), True)

@@ -7,49 +7,55 @@ PW = 176
 ROW = 32 * PW
 XP0 = 2688
 XW = XP0 + 23 * 128
-EW = 16 * PW
-CB = 8192
-SV = 82
-KB = 10
+XB = [2688 + t * XW for t in range(R + 1)]
+VW = XB[1]
+EW = VW + 16 * PW
+CB = 32768
+KA = 8
+SA = 126
+KS = (2, 10)
 PK = 4096
 QC, SC = ROW // 2, 1280
 RND = 1.5 * 2.0 ** 23 * PK
-YC = (8, 24, 40, 80, 120, 144, 168)
-SMALL = 2496
-CUT = (0, 38, 74, 118, 160)
+YC = (8, 20, 32, 64, 96, 122, 148, 158, 168)
+CUT = (0, 40, 80, 120, 160)
+CUTX = (0, 80, 80, 120, 160)
 
 F, H, I, U = "float32", "bfloat16", "int32", "uint16"
 SCRATCH = {
-    "xn": ("sbuf", [128, 2688], H), "xa": ("sbuf", [128, XW], H), "xb": ("sbuf", [128, XW], H),
+    "xx": ("sbuf", [128, XB[R]], H), "aq": ("sbuf", [128, 160], F), "q3": ("sbuf", [128, 168], F),
+    "ha": ("sbuf", [128, 160], F), "hb": ("sbuf", [128, 160], F),
     "aw": ("sbuf", [128, 128 + 23 * 128], H), "arr": ("sbuf", [128, R * 128], H),
-    "pk": ("sbuf", [128, 144], H), "gb": ("sbuf", [128, 2560], H), "vlb": ("sbuf", [128, PW], H),
+    "pk": ("sbuf", [128, 144], H), "gb": ("sbuf", [128, 2688], H), "vlb": ("sbuf", [128, PW], H),
     "rl": ("sbuf", [128, R * 64], H), "rb": ("sbuf", [128, 72], H),
     "win": ("sbuf", [128, ROW], F), "pos": ("sbuf", [128, ROW], F), "pos2": ("sbuf", [128, ROW], F),
-    "vh": ("sbuf", [128, 3 * 128], F), "vs": ("sbuf", [128, 11, 256], F), "dfl": ("sbuf", [128, 2560], F),
+    "p3": ("sbuf", [128, PW], F), "p4": ("sbuf", [128, PW], F),
+    "vh": ("sbuf", [128, 4 * 128], F), "vs": ("sbuf", [128, 11, 256], F),
     "rep": ("sbuf", [128, 256], F), "tte": ("sbuf", [128, 44, 32], F), "tto": ("sbuf", [128, 88, 16], F),
     "ql": ("sbuf", [128, 192], U), "xl": ("sbuf", [128, 184], U), "sp": ("sbuf", [128, 184], U), "piu": ("sbuf", [128, PW], U),
-    "nxu": ("sbuf", [128, 160], U), "npu": ("sbuf", [128, 160], U), "viu": ("sbuf", [128, 160], U),
+    "nxu": ("sbuf", [128, 160], U), "viu": ("sbuf", [128, 160], U),
     "nui": ("sbuf", [128, 4], I), "nxi": ("sbuf", [128, 160], I), "lei": ("sbuf", [128, 320], I),
     "voi": ("sbuf", [128, 160], I), "lgi": ("sbuf", [128, 8], I), "ti1": ("sbuf", [128, 160], I), "ti2": ("sbuf", [128, 160], I),
     "pci": ("sbuf", [128, 8], I), "col": ("sbuf", [128, 24], F), "ci": ("sbuf", [128, PW], F), "mg": ("sbuf", [128, 128], F),
     "oti": ("sbuf", [128, 184], F), "ot": ("sbuf", [128, 184], H),
     "z": ("sbuf", [128, 144], H), "znu": ("sbuf", [128, 144], H), "z1": ("sbuf", [128, 144], H), "zd": ("sbuf", [128, 144], H),
     "bnu": ("sbuf", [128, 128], H), "ib": ("sbuf", [128, 128], H), "i128": ("sbuf", [128, 128], H),
-    "am": ("sbuf", [128, 5 * 128], F), "hm": ("sbuf", [128, 4 * 128], F),
-    "nxl": ("sbuf", [128, PW], F), "wl": ("sbuf", [128, PW], F), "bs": ("sbuf", [128, 160], F), "idc": ("sbuf", [128, 160], F),
-    "sn": ("sbuf", [128, 184], I), "sm": ("sbuf", [128, 184], F), "pg": ("psum", [128, 64, 4, 2], F),
-    "rs": ("sbuf", [128, PW], F), "rz": ("sbuf", [128, PW], F), "idn": ("sbuf", [128, 160], F), "p1": ("sbuf", [128, PW], F), "p2": ("sbuf", [128, PW], F),
+    "am": ("sbuf", [128, 9 * 128], F), "hm": ("sbuf", [128, 4 * 128], F),
+    "nxl": ("sbuf", [128, PW], F), "wl": ("sbuf", [128, PW], F), "idc": ("sbuf", [128, 160], F),
+    "oi": ("sbuf", [128, 16], I), "sm": ("sbuf", [128, 184], F), "pg": ("psum", [128, 64, 4, 2], F),
+    "rs": ("sbuf", [128, PW], F), "rz": ("sbuf", [128, PW], F), "idn": ("sbuf", [128, 160], F),
+    "p1": ("sbuf", [128, PW], F), "p2": ("sbuf", [128, PW], F),
     "pm": ("sbuf", [128, PW], F), "dd": ("sbuf", [128, 160], F), "d1": ("sbuf", [128, 160], F), "vv": ("sbuf", [128, 160], F),
     "vp": ("sbuf", [128, 160], F), "wv": ("sbuf", [128, 160], F), "dfp": ("sbuf", [128, 160], F),
-    "cf": ("sbuf", [128, 160], F), "c1": ("sbuf", [128, 160], F), "c2": ("sbuf", [128, 160], F), "u1": ("sbuf", [128, 160], F),
-    "m1": ("sbuf", [128, 160], F), "m2": ("sbuf", [128, 160], F),
-    "h": ("sbuf", [128, 14 * 80], F), "lgx": ("sbuf", [128, 192], F), "uu": ("sbuf", [128, 192], F),
+    "c1": ("sbuf", [128, 160], F), "c2": ("sbuf", [128, 160], F), "u1": ("sbuf", [128, 160], F), "u2": ("sbuf", [128, 160], F),
+    "m0": ("sbuf", [128, 160], F), "m1": ("sbuf", [128, 160], F), "m2": ("sbuf", [128, 160], F),
+    "h": ("sbuf", [128, 8 * 80], F), "lgx": ("sbuf", [128, 192], F), "uu": ("sbuf", [128, 192], F),
     "one": ("sbuf", [128, 24], F), "cnd": ("sbuf", [128, 23 * 184], H), "tb": ("sbuf", [128, 128], H), "tf": ("sbuf", [128, 128], F),
     "yo": ("sbuf", [128, 160], F),
-    "mu": ("psum", [128, 512], F), "mu1": ("psum", [128, 512], F), "mud": ("psum", [128, 512], F), "sx": ("psum", [128, 512], F),
+    "mu": ("psum", [128, 512], F), "mu1": ("psum", [128, 512], F), "pb": ("psum", [128, 512], F), "sx": ("psum", [128, 512], F),
     "pf": ("psum", [128, 32, 4, 2, 2], F), "pt": ("psum", [128, 512], F), "cnt": ("psum", [128, 512], F),
 }
-SEMAPHORES = (["cv", "ca", "cp", "cg", "ld0", "ld1", "ld2", "ld3", "ld4", "ld5", "dv", "dc", "dk", "dw", "dp", "dr", "dr2", "dy",
+SEMAPHORES = (["cv", "ca", "cp", "cg", "ld0", "ld1", "ld2", "ld3", "ld4", "ld5", "dv", "dc", "dk", "dw", "dp", "dp2", "dr", "dr2", "dr3", "dy",
                "back", "sb", "rback", "rsb"]
               + ["a%d" % t for t in range(R)] + ["s%d" % t for t in range(R)]
               + ["ra%d" % t for t in range(R)] + ["rs%d" % t for t in range(R)])
@@ -79,7 +85,7 @@ def _relay_program(g, core, T, topo):
             dst = T.cores[(r - step) % n]
             if _relay(src, dst, T, topo) == core:
                 c0 = EW + 72 * (step - 1)
-                jobs.append((1, dst, T.xb[:, c0:c0 + 72], T.rb[:, :], "rback", "back", "rsb"))
+                jobs.append((1, dst, T.xx[:, c0:c0 + 72], T.rb[:, :], "rback", "back", "rsb"))
             dst = T.cores[(r + step) % n]
             if _relay(src, dst, T, topo) == core:
                 for t in range(R):
@@ -215,32 +221,33 @@ def rank_program(g, core, T, topo):
         return T.sx[:, 80 * j:80 * j + 80]
 
     a_, b_ = slice(0, 80), slice(80, 160)
-    X = [T.xa, T.xb]
-    XN = ["xa", "xb"]
+
+
+    def xr(t, c0, c1):
+        return T.xx[:, XB[t] + c0:XB[t] + c1]
     fwd = [T.cores[(rank + 1) % n], T.cores[(rank + 2) % n]]
     bwd = [T.cores[(rank - 1) % n], T.cores[(rank - 2) % n]]
     landed("back", "ew")
     for t in range(R):
         landed("a%d" % t, "arr%d" % t)
 
-    dma("s", T.xa[:, 2560:2688], T.x[:, 2560:2688], "ld4", "", "xao")
+    dma("s", xr(0, 2560, 2688), T.x[:, 2560:2688], "ld4", "", "x0o")
     dma("a", T.nui[:, 0:1], T.nu[:, :], "ld0", "", "nui")
     dma("a", T.aw[:, 128:256], T.x[:, 0:128], "ld0", "", "xo0")
     dma("s", T.nxi[:, :], T.nx[:, :], "ld1", "", "nxi")
     dma("a", T.voi[:, :], T.vol[:, :], "ld5", "", "voi")
-    dma("s", T.xn[:, :], T.x[:, :], "ld2", "", "xn")
+    dma("s", T.xx[:, 0:2688], T.x[:, :], "ld2", "", "xn")
 
     def send_fwd(t):
-        x = X[t % 2]
-        send(fwd, [x[:, 2560:2624], x[:, 2624:2688]], [T.arr[:, 128 * t:128 * t + 64], T.arr[:, 128 * t + 64:128 * t + 128]],
-             T.rl[:, 64 * t:64 * t + 64], "a%d" % t, "ra%d" % t, "s%d" % t, XN[t % 2] + "o")
+        send(fwd, [xr(t, 2560, 2624), xr(t, 2624, 2688)], [T.arr[:, 128 * t:128 * t + 64], T.arr[:, 128 * t + 64:128 * t + 128]],
+             T.rl[:, 64 * t:64 * t + 64], "a%d" % t, "ra%d" % t, "s%d" % t, "x%do" % t)
 
     op("g", lambda: g.iota(T.pci[:, 0:1], [[1, 1]], 0, 1), "", "pci0")
     iota(T.mg[:, :], [[1, 8], [0, 16]], 0, 0, "mg")
     iota(T.ci[:, :], [[1, PW]], 0, 0, "ci")
     send_fwd(0)
-    fill(T.xb[:, 0:EW], 0.0, "vw")
-    cp("a", T.win[:, 0:EW], T.xb[:, 0:EW], "vw", "win0")
+    fill(T.xx[:, VW:VW + QC // 2], 0.0, "vw")
+    op("a", [(lambda j=j: A.activation(T.win[:, j:j + QC // 2], T.xx[:, VW:VW + QC // 2], Act.Copy)) for j in (0, QC // 2)], "vw", "win0")
     ts(T.pci[:, 1:2], T.pci[:, 0:1], 15, Op.bitwise_and, "pci0", "pci1")
     ts(T.pci[:, 2:3], T.pci[:, 0:1], 4, Op.logical_shift_right, "pci0", "pci2")
     ts(T.pci[:, 3:4], T.pci[:, 0:1], 16, Op.bitwise_and, "pci0", "pci3")
@@ -262,106 +269,139 @@ def rank_program(g, core, T, topo):
     ts(T.tf[:, :], T.cnt[:, 0:128], col(cOD), Op.mult, "cnt cod", "tf")
     fill(T.z[:, :], 0.0, "z")
     tt(T.pk[:, 8:136], T.tf[:, :], T.tb[:, :], Op.add, "tb tf pk", "pk2")
-    send(bwd, [T.pk[:, 0:72], T.pk[:, 72:144]], [T.xb[:, EW:EW + 72], T.xb[:, EW + 72:EW + 144]], T.rb[:, :],
+    send(bwd, [T.pk[:, 0:72], T.pk[:, 72:144]], [T.xx[:, EW:EW + 72], T.xx[:, EW + 72:EW + 144]], T.rb[:, :],
          "back", "rback", "sb", "pk pk0 pk1 pk2")
+    am = [T.am[:, 128 * j:128 * j + 128] for j in range(9)]
+    low, high, ones, full = (T.hm[:, 128 * j:128 * j + 128] for j in range(4))
+
+    def diagonal(out, src, shift, rd, wr):
+        op("g", lambda: g.affine_select(out, src, [[-1, 128]], Op.is_equal, 0.0, shift, 1), rd, wr)
+    iota(T.hm[:, 256:512], [[127, 2], [0, 128]], 1, 0, "hm2")
+    diagonal(am[4], ones, 0, "hm2", "am4")
+    iota(T.rs[:, :], [[0, PW]], 0, 0, "rs0")
+    iota(T.rz[:, :], [[0, PW]], 0, 0, "rz")
+    iota(T.vh[:, 256:384], [[32, 4], [0, 2], [1, 16]], XP0 + CB + 256, 0, "vh3")
+    iota(T.win[:, 4512:ROW], [[0, ROW - 4512]], 0, 0, "win2")
+    iota(T.vh[:, 0:128], [[1, 128]], XP0 + CB + 128, 0, "vh1")
+    iota(T.vs[:, :, 0:128], [[256, 11], [1, 128]], XP0 + CB + 384, 0, "vo")
+    iota(low, [[0, 4], [-1, 2], [0, 16]], 1, 0, "hm0")
+    iota(high, [[0, 4], [1, 2], [0, 16]], 0, 0, "hm1")
+    iota(T.oti[:, :], [[0, 23], [16, 8]], 0, 0, "oti")
+    for out, src, shift, nm in ((am[0], low, 0, "am0"), (am[1], high, 16, "am1"), (am[2], low, -16, "am2"), (am[3], high, 0, "am3"),
+                                (T.ib[:, :], ones, 0, "ib"), (T.i128[:, :], full, 0, "i128")):
+        diagonal(out, src, shift, "hm0 hm1 hm2", nm)
+    iota(T.vh[:, 128:256], [[1, 128]], XP0 + 22 * 128, 0, "vh2")
+    iota(T.one[:, :], [[0, 24]], 1, 0, "one")
+
+    cp("v", T.nxu[:, :], T.nxi[:, :], "nxi", "nxu")
+    cp("v", T.vlb[:, 0:160], T.voi[:, :], "voi vlb", "vlb")
+    fill(T.xx[:, VW + QC // 2:EW], 0.0, "vw2")
+    dma("s", T.xx[0::16, VW:EW], T.vlb[:, :], "dv", "vlb", "vw vw2")
     before("s", [], ["pk2"], False)
     dma("s", T.lei[:, :], T.le[:, :], "ld3", "", "lei")
     dma("s", T.lgi[:, :], T.lag[:, :], "ld3", "", "lgi")
-    iota(T.vh[:, 256:384], [[32, 4], [0, 2], [1, 16]], XP0 + CB + 256, 0, "vh3")
-    iota(T.vh[:, 0:128], [[1, 128]], XP0 + CB + 128, 0, "vh1")
-    iota(T.win[:, 4512:ROW], [[0, ROW - 4512]], 0, 0, "win2")
-    iota(T.oti[:, :], [[0, 23], [16, 8]], 0, 0, "oti")
-    iota(T.vh[:, 128:256], [[1, 128]], XP0 + 22 * 128 - SMALL, 0, "vh2")
-    iota(T.vs[:, :, 128:256], [[256, 11], [1, 128]], XP0 + CB + 384, 0, "vo")
-    am = [T.am[:, 128 * j:128 * j + 128] for j in range(5)]
-    low, high, ones, full = (T.hm[:, 128 * j:128 * j + 128] for j in range(4))
-    iota(low, [[0, 4], [-1, 2], [0, 16]], 1, 0, "hm0")
-    iota(high, [[0, 4], [1, 2], [0, 16]], 0, 0, "hm1")
-    iota(T.hm[:, 256:512], [[127, 2], [0, 128]], 1, 0, "hm2")
-    for out, src, shift, nm in ((am[0], low, 0, "am0"), (am[1], high, 16, "am1"), (am[2], low, -16, "am2"), (am[3], high, 0, "am3"),
-                                (am[4], ones, 0, "am4"), (T.ib[:, :], ones, 0, "ib"), (T.i128[:, :], full, 0, "i128")):
-        op("g", lambda: g.affine_select(out, src, [[-1, 128]], Op.is_equal, 0.0, shift, 1), "hm0 hm1 hm2", nm)
-    iota(T.dfl[:, :], [[1, 2560]], CB + 128, 0, "dfl")
-
-    cp("v", T.vlb[:, 0:160], T.voi[:, :], "voi vlb", "vlb")
-    dma("a", T.xb[0::16, 0:EW], T.vlb[:, :], "dv", "vlb", "vw")
-    cp("v", T.nxu[:, :], T.nxi[:, :], "nxi", "nxu")
     ts(T.z[:, 15:143:16], T.ci[:, 0:8], col(cG), Op.is_equal, "ci c0 z", "z")
     ts(T.ti1[:, :], T.nxi[:, :], 4, Op.logical_shift_right, "nxi", "ti1")
     ts(T.ti2[:, :], T.nxi[:, :], 15, Op.bitwise_and, "nxi", "ti2")
     ts(T.znu[:, :], T.z[:, :], col(cNU), Op.mult, "z cnu", "znu")
-    MO, M1 = T.pt[:, 0:160], T.pt[:, 336:496]
-    ts(MO, T.nxi[:, :], 2560.0, Op.is_ge, "nxi", "tt")
+    AB, SCR = T.pt[:, 256:336], T.pt[:, 336:416]
+    BS, DN, RR = T.pb[:, 0:160], T.pb[:, 160:240], T.pb[:, 240:320]
+    DD = T.pb[:, 320:400], T.pb[:, 400:480], T.pb[:, 320:480]
+    MU1, MU2 = T.mu1[:, 0:160], T.mu1[:, 256:416]
+    ts(T.m2[:, :], T.nxi[:, :], 2560.0, Op.is_ge, "nxi", "m2s")
     ts(T.sx[:, 0:160], T.ti2[:, :], float(PW), Op.mult, "ti2", "px0 px1")
-    ts(T.pm[:, 0:160], T.nxi[:, :], float(EW + 8 - 2560), Op.add, "nxi", "pm")
+    ts(T.sx[:, 160:320], T.nxi[:, :], float(EW - VW + 8 - 2560), Op.add, "nxi", "px2 px3")
     spread(T.mu[:, 160:168], T.znu, T.aw, 128, "znu xo0", "mu")
     tt(T.p1[:, 0:160], T.sx[:, 0:160], T.ti1[:, :], Op.add, "px0 px1 ti1", "p1")
-    tt(T.sx[:, 160:320], MO, T.pm[:, 0:160], Op.mult, "tt pm", "px2 px3")
-    ts(col(cHO), col(cH16), float(PW), Op.mult, "c0", "cho", -float(QC), Op.add)
+    tt(T.sx[:, 160:320], T.sx[:, 160:320], T.m2[:, :], Op.mult, "px2 px3 m2s", "px2 px3")
+    ts(col(cHO), col(cH16), float(PW * PK), Op.mult, "c0", "cho", -float(QC * PK + SC), Op.add)
     tt(T.pm[:, 0:160], T.sx[:, 160:320], T.p1[:, 0:160], Op.max, "px2 px3 p1", "pm")
-    ts(col(cPI), col(cI32), float(PW), Op.mult, "c0", "cpi", -float(QC), Op.add)
+    ts(col(cPI), col(cI32), float(PW * PK), Op.mult, "c0", "cpi", -float(QC * PK), Op.add)
     cp("v", T.viu[:, :], T.pm[:, 0:160], "pm", "viu")
 
-    def four(out, name, window, offs, rd):
+    def gathers(out, o0, name, window, offs, rd, cut, queues):
         for j in range(4):
-            cp("va"[j % 2], out[:, 16 * CUT[j]:16 * CUT[j + 1]], window.indirect(offs[:, CUT[j]:CUT[j + 1]]), rd, "%s%d" % (name, j))
+            if cut[j] < cut[j + 1]:
+                cp(queues[j], out[:, o0 + 16 * cut[j]:o0 + 16 * cut[j + 1]], window.indirect(offs[:, cut[j]:cut[j + 1]]), rd,
+                   "%s%d" % (name, j))
 
-    def contents(out, nm, zt, zn, src, sn):
-        spread(out[:, 0:CUT[2]], zt, src, 0, "%s %s0 %s1" % (zn, sn, sn), nm)
-        spread(out[:, CUT[2]:160], zt, src, 16 * CUT[2], "%s %s2 %s3" % (zn, sn, sn), nm)
+    MUA, MUB = T.mu[:, a_], T.mu1[:, 160:240]
 
-    four(T.xa, "xas", T.xn[:, :], T.nxu, "xn nxu")
-    contents(T.mu, "mu", T.znu, "znu", T.xa, "xas")
-    ts(T.idn[:, :], T.ci[:, 0:160], 16.0, Op.mult, "ci c0", "idn", col(cI), Op.add)
-    fill(T.rs[:, :], 0.0, "rs0")
-    ts(T.sx[:, 0:160], T.p1[:, 0:160], col(cHO), Op.add, "p1 cho", "px0 px1", float(PK), Op.mult)
-    ts(T.idc[:, :], T.idn[:, :], -float(SC), Op.add, "idn", "idc")
-    ts(T.rs[:, 160:168], T.idn[:, 0:8], float(2560 - SMALL), Op.add, "idn rs0", "rs1")
-    ts(T.rs[:, 0:8], T.idn[:, 0:8], float(XP0 + CB), Op.add, "idn rs0", "rs2")
+    def contents(t):
+        spread(MUA, T.znu, T.xx, XB[t], "znu x%ds0 x%ds1" % (t, t), "mu")
+        spread(MUB, T.znu, T.xx, XB[t] + 1280, "znu x%ds2 x%ds3" % (t, t), "mu1")
+
+    def first_half(first):
+        first()
+        tt(half(2), MUA, T.d1[:, a_], Op.mult, "mu d1", "h2")
+        tt(T.wv[:, a_], MUA, T.vp[:, a_], Op.mult, "mu vp", "wva")
+        tt(half(1), half(2), RR, Op.subtract, "h2 pb", "h1")
+
+    def act(out, in_, func, rd, wr, **how):
+        op("a", lambda: A.activation(out, in_, func, **how), rd, wr)
+
+    def sums(terms, rd, wr):
+        op("p", [(lambda j=j: P.matmul(terms[j][0], terms[j][1], terms[j][2], j == 0, j == len(terms) - 1)) for j in range(len(terms))],
+           rd + " am4 amx", wr)
+
+    act(T.idn[:, :], T.ci[:, 0:160], Act.Identity, "ci c0", "idn", scale=16.0, bias=col(cI))
+    gathers(T.xx, XB[0], "x0s", T.xx[:, 0:2688], T.nxu, "xn nxu", CUTX, "aava")
+    contents(0)
     WALL = "win0 win1 win2 wf0 wf1 wf2 wf3"
 
     def reset(buf, nm, sem):
-        dma("s", buf[0::32, :], T.rs[:, :], sem, "rs0 rs1 rs2", nm + "r0")
+        dma("s", buf[0::32, :], (T.rs if nm == "pos" else T.rz)[:, :], sem, "rs0 rs1 rs2" if nm == "pos" else "rz", nm + "r0")
         dma("s", buf[16::32, :], T.rz[:, :], sem, "rz", nm + "r1")
-    fill(T.rz[:, :], 0.0, "rz")
+    act(T.rs[:, 160:168], T.idn[:, 0:8], Act.Identity, "idn rs0", "rs1", bias=2560.0)
+    act(T.rs[:, 0:8], T.idn[:, 0:8], Act.Identity, "idn rs0", "rs2", bias=float(XP0 + CB))
+    reset(T.pos2, "pos2", "dr3")
     reset(T.pos, "pos", "dr")
-    reset(T.pos2, "pos2", "dr2")
-    tt(T.bs[:, :], T.sx[:, 0:160], T.idc[:, :], Op.add, "px0 px1 idc", "ba bb")
-    four(T.gb, "gb", T.xb[:, 0:EW + 144], T.viu, "vw ew viu")
-    contents(T.mu1, "mu1", T.z, "z", T.gb, "gb")
-    cp("a", T.win[:, EW:4512], T.xn[:, 0:4512 - EW], "xn", "win1")
-    tt(T.dd[:, a_], T.lei[:, 160:240], T.lei[:, 0:80], Op.subtract, "lei", "dda")
-    tt(T.dd[:, b_], T.lei[:, 240:320], T.lei[:, 80:160], Op.subtract, "lei", "ddb")
-    cp("v", T.lgx[:, 0:8], T.lgi[:, :], "lgi", "lgx")
-    for w0, w1 in ((8, 16), (16, 32), (32, 64), (64, 128), (128, 192)):
-        cp("a", T.lgx[:, w0:w1], T.lgx[:, 0:w1 - w0], "lgx", "lgx")
-    ts(T.m1[:, :], T.nxi[:, :], 2560.0, Op.is_lt, "nxi", "m1s")
-    tt(T.c1[:, :], MO, T.dd[:, :], Op.mult, "tt dda ddb", "c1")
-    tt(half(0), T.bs[:, b_], T.bs[:, a_], Op.subtract, "ba bb", "dn")
-    ts(T.nxl[:, 160:168], T.ci[:, 168:176], col(cPI), Op.add, "ci cpi", "nxo", float(PK), Op.mult)
-    tt(T.d1[:, :], T.dd[:, :], T.c1[:, :], Op.subtract, "c1 dda ddb", "d1")
-    ts(T.nxl[:, 168:176], T.ci[:, 160:168], col(cPI), Op.add, "ci cpi", "nxt", float(PK), Op.mult)
-    fill(T.wl[:, 160:PW], 0.0, "wo")
-    tt(T.u1[:, :], T.mu1[:, 0:160], T.c1[:, :], Op.mult, "mu1 c1", "u1")
-    tt(T.vp[:, :], T.mu1[:, 0:160], T.m1[:, :], Op.mult, "mu1 m1s", "vp")
-    tt(half(3), T.u1[:, b_], T.u1[:, a_], Op.subtract, "u1", "rr")
+    cp("a", T.wl[:, 160:PW], T.rz[:, 0:16], "rz", "wo")
+    dma("s", T.win[:, QC:4512], T.win[:, 0:4512 - QC], "dr2", "win0 ew", "win1")
+    gathers(T.gb, 0, "gb", T.xx[:, VW:EW + 144], T.viu, "vw vw2 ew viu", CUT, "vava")
+    spread(T.mu1[:, a_], T.z, T.gb, 0, "z gb0 gb1", "mu1")
+    spread(T.mu1[:, b_], T.z, T.gb, 1280, "z gb2 gb3", "mu1")
+    act(T.m1[:, :], T.m2[:, :], Act.Identity, "m2s", "m1s", scale=-1.0, bias=1.0)
+    act(T.pm[:, 0:160], T.p1[:, 0:160], Act.Identity, "p1 cho", "pm", scale=float(PK), bias=col(cHO))
+    act(half(5), T.pm[:, b_], Act.Identity, "pm", "dv", bias=1280.0)
+    op("v", [lambda: V.tensor_tensor(DD[0], T.lei[:, 160:240], T.lei[:, 0:80], Op.subtract),
+             lambda: V.tensor_tensor(DD[1], T.lei[:, 240:320], T.lei[:, 80:160], Op.subtract)], "lei", "pb")
+    act(T.nxl[:, 160:168], T.ci[:, 168:176], Act.Identity, "ci cpi", "nxo", scale=float(PK), bias=col(cPI))
+    act(T.nxl[:, 168:176], T.ci[:, 160:168], Act.Identity, "ci cpi", "nxt", scale=float(PK), bias=col(cPI))
+    tt(BS, T.pm[:, 0:160], T.idn[:, :], Op.add, "pm idn", "bs0")
+    tt(T.c1[:, :], DD[2], T.m2[:, :], Op.mult, "pb m2s", "c1")
+    tt(T.d1[:, :], DD[2], T.m1[:, :], Op.mult, "pb m1s", "d1")
+    tt(DN, half(5), T.pm[:, a_], Op.subtract, "pm dv bs0", "dn0")
+    tt(half(2), MUA, T.d1[:, a_], Op.mult, "mu d1", "h2")
+    cp("a", T.dd[:, :], DD[2], "pb c1 d1 dn0", "dda ddb pbr")
+    tt(T.u1[:, :], MU1, T.c1[:, :], Op.mult, "mu1 c1", "u1")
+    tt(T.vp[:, :], MU1, T.m1[:, :], Op.mult, "mu1 m1s", "vp")
+    tt(px(3), T.u1[:, b_], T.u1[:, a_], Op.subtract, "u1", "px3")
+    tt(T.wv[:, a_], MUA, T.vp[:, a_], Op.mult, "mu vp", "wva")
+    tt(half(1), half(2), px(3), Op.subtract, "h2 px3 pbr", "h1")
+    op("a", [(lambda j=j, c=c: A.activation(am[j], am[4], Act.Identity, scale=c))
+             for j, c in ((5, -1.0), (6, 1280.0), (7, -1280.0), (8, 2560.0))], "am4", "amx")
+    act(T.idc[:, :], T.idn[:, :], Act.Identity, "idn", "idc", bias=float(CB))
+    cp("a", col(cH), T.xx[:, EW:EW + 1], "ew", "ch")
+    act(col(cND), T.xx[:, EW:EW + 1], Act.Identity, "ew", "cnd", scale=-2.0, bias=T.xx[:, EW + 136:EW + 137])
+    act(T.z1[:, :], T.z[:, :], Act.Identity, "z ch", "z1", scale=col(cH))
+    act(T.zd[:, :], T.z[:, :], Act.Identity, "z cnd", "zd", scale=col(cND))
+    act(T.vh[:, 384:512], T.vh[:, 256:384], Act.Identity, "vh3 c0", "vs0", bias=col(cH16))
+    op("a", [(lambda j=j: A.activation(T.vs[:, j, 128:256], T.vh[:, 384:512], Act.Identity, bias=256.0 * (j + 1))) for j in range(10)],
+       "vs0", "vs")
+    PF, PM = T.pg[:, 0:20, :, :], T.pg[:, 20:40, :, :]
 
     def later_constants():
-        ts(T.z1[:, :], T.z[:, :], T.xb[:, EW:EW + 1], Op.mult, "z ew", "z1")
-        ts(col(cND), T.xb[:, EW:EW + 1], -2.0, Op.mult, "ew", "cnd", T.xb[:, EW + 136:EW + 137], Op.add)
-        ts(M1, T.nxi[:, :], 2624.0, Op.is_ge, "nxi", "m1")
-        ts(T.zd[:, :], T.z[:, :], col(cND), Op.mult, "z cnd", "zd")
-        tt(T.vv[:, :], T.vp[:, :], M1, Op.subtract, "vp m1", "va vb")
-        tt(half(10), T.dd[:, a_], T.dd[:, b_], Op.add, "dda ddb", "ab")
-        ts(T.idc[:, :], T.idn[:, :], float(CB), Op.add, "idn", "idc")
-        ts(T.ot[:, :], T.oti[:, :], col(cI), Op.add, "oti c0", "ot")
-        fill(T.one[:, :], 1.0, "one")
+        ts(T.sx[:, 320:480], T.nxi[:, :], 2624.0, Op.is_ge, "nxi", "px4 px5")
+        tt(T.vv[:, :], T.vp[:, :], T.sx[:, 320:480], Op.subtract, "vp px4 px5", "va vb")
+        tt(AB, T.dd[:, a_], T.dd[:, b_], Op.add, "dda ddb", "ab")
+        cp("v", T.lgx[:, 0:8], T.lgi[:, :], "lgi", "lgx")
 
     def masks():
-        op("a", lambda: A.activation(T.m1[:, :], T.vv[:, :], Act.Relu, bias=1.0, scale=-1.0), "va vb", "m1s")
-        op("a", lambda: A.activation(T.m2[:, :], T.vv[:, :], Act.Relu, scale=-1.0), "va vb", "m2s")
+        act(T.m1[:, :], T.vv[:, :], Act.Relu, "va vb", "m1s", bias=1.0, scale=-1.0)
+        act(T.m2[:, :], T.vv[:, :], Act.Relu, "va vb", "m2s", scale=-1.0)
 
-    S = T.pt[:, 256:336]
+    S = half(0)
 
     def rows(f, src, q2, rd):
         dma("s", T.win[f::32, :], src[:, :], "dw", rd, "wf%d" % (2 * f))
@@ -376,7 +416,7 @@ def rank_program(g, core, T, topo):
         return [lambda: ts(T.sm[:, c], src, RND, Op.add, nm, "sm%d" % k0, RND, Op.subtract),
                 lambda: tt(T.sm[:, c], src, T.sm[:, c], Op.subtract, nm + " sm%d" % k0, "sm%d" % k0),
                 lambda: ts(T.xl[:, c], T.sm[:, c], float(SC), Op.add, "sm%d" % k0, "xl%d" % k0),
-                lambda: cp("a", T.aw[:, 128 * (k0 + 1):128 * (k1 + 1)], x[:, 0:2560].indirect(T.xl[:, c]), rd + " xl%d" % k0, "xo%d" % k0)]
+                lambda: cp("a", T.aw[:, 128 * (k0 + 1):128 * (k1 + 1)], x.indirect(T.xl[:, c]), rd + " xl%d" % k0, "xo%d" % k0)]
 
     def scatter(buf, nm, offs, vals, rd):
         op("a", lambda: A.activation(buf[:, :].indirect(offs), vals, Act.Silu), rd, nm + "r0 " + nm + "r1")
@@ -389,210 +429,224 @@ def rank_program(g, core, T, topo):
         j = (k - 2) // 2 * 2 + u
         return T.tte[:, 2 * j:2 * j + 2, 0::16] if k % 2 == 0 else T.tto[:, 4 * j:4 * j + 4, 0]
 
-    def home(k0, k1, both):
+    def home(k0, k1):
         j0, j1 = (k0 - 2) // 2, (k1 - 2) // 2 + 1
         ks = slice(k0, k1 + 1, 2)
         rd = " ".join("tt%d tt%db" % (k, k) for k in range(k0, k1 + 1, 2)) + " am0 am1 am2 am3 am4"
         if k0 % 2 == 0:
-            calls = [(lambda hc=hc, hh=hh: P.matmul(
-                T.pf[:, ks, :, hc, :] if both else T.pg[:, ks, :, hc], am[2 * hc + hh],
-                T.tte[:, 4 * j0:4 * j1, 16 * hh:16 * hh + 2] if both else T.tte[:, 4 * j0:4 * j1, 16 * hh], hh == 0, hh == 1))
-                for hc in range(2) for hh in range(2)]
+            calls = [(lambda hc=hc, hh=hh: P.matmul(T.pf[:, ks, :, hc, :], am[2 * hc + hh], T.tte[:, 4 * j0:4 * j1, 16 * hh:16 * hh + 2],
+                                                    hh == 0, hh == 1)) for hc in range(2) for hh in range(2)]
         else:
-            calls = [lambda: P.matmul(T.pf[:, ks, :, :, :] if both else T.pg[:, ks, :, :], am[4],
-                                      T.tto[:, 8 * j0:8 * j1, 0:2] if both else T.tto[:, 8 * j0:8 * j1, 0], True, True)]
-        op("p", calls, rd, "pf" if both else "pg")
+            calls = [lambda: P.matmul(T.pf[:, ks, :, :, :], am[4], T.tto[:, 8 * j0:8 * j1, 0:2], True, True)]
+        op("p", calls, rd, "pf")
 
     for t in range(R):
         last = t == R - 1
-        x, xn, y, yn = X[t % 2], XN[t % 2], X[1 - t % 2], XN[1 - t % 2]
+        x, xn, yn = xr(t, 0, 2560), "x%d" % t, "x%d" % (t + 1)
         xs = " ".join("%ss%d" % (xn, j) for j in range(4))
-        pos, pn = (T.pos2, "pos2") if last else (T.pos, "pos")
+        pos, pn, sv = T.pos, "pos", 8 * KA
         arrival = T.arr[:, 128 * t:128 * t + 128]
-        tt(px(0), T.mu[:, a_], T.d1[:, a_], Op.mult, "mu d1", "px0")
-        tt(half(1), T.mu[:, b_], T.d1[:, b_], Op.mult, "mu d1", "pb")
-        tt(T.wv[:, a_], T.mu[:, a_], T.vp[:, a_], Op.mult, "mu vp", "wva")
-        tt(px(1), px(0), half(1), Op.subtract, "px0 pb", "px1")
-        tt(px(2), T.mu[:, b_], T.vp[:, b_], Op.mult, "mu vp", "px2")
-        tt(S, px(1), half(3), Op.is_lt, "px1 rr", "ss")
-        tt(half(2), px(2), T.wv[:, a_], Op.subtract, "wva px2", "dwv")
-        tt(px(0), half(0), S, Op.mult, "dn ss", "px0")
-        tt(half(6), half(2), S, Op.mult, "dwv ss", "t6")
-        tt(T.nxl[:, a_], T.bs[:, a_], px(0), Op.add, "ba px0", "nxa")
-        tt(T.nxl[:, b_], T.bs[:, b_], px(0), Op.subtract, "bb px0", "nxb")
-        q2 = "s" if last else "a"
-        rows(0, T.nxl, q2, "nxa nxb nxo nxt win0 win1 win2")
-        tt(T.wl[:, b_], px(2), half(6), Op.subtract, "px2 t6", "wb")
-        tt(T.wl[:, a_], T.wv[:, a_], half(6), Op.add, "wva t6", "wa")
-        rows(1, T.wl, q2, "wa wb wo")
+        tt(px(0), MUB, T.d1[:, b_], Op.mult, "mu1 d1", "px0")
+        tt(px(2), MUB, T.vp[:, b_], Op.mult, "mu1 vp", "px2")
+        tt(S, half(1), px(0), Op.is_lt, "h1 px0", "ss")
+        tt(px(1), px(2), T.wv[:, a_], Op.subtract, "wva px2", "px1")
+        tt(half(3), DN, S, Op.mult, "pb ss", "t5")
+        tt(half(4), px(1), S, Op.mult, "px1 ss", "t6")
+        tt(T.nxl[:, a_], T.pb[:, a_], half(3), Op.add, "pb t5", "nxa")
+        tt(T.nxl[:, b_], T.pb[:, b_], half(3), Op.subtract, "pb t5", "nxb")
+        rows(0, T.nxl, "a" if t else "s", "nxa nxb nxo nxt win0 win1 win2")
+        tt(T.wl[:, b_], px(2), half(4), Op.subtract, "px2 t6", "wb")
+        tt(T.wl[:, a_], T.wv[:, a_], half(4), Op.add, "wva t6", "wa")
+        rows(1, T.wl, "a" if t else "s", "wa wb wo")
+        if t > 0:
+            before("g", WALL.split(), [], False)
+            send_fwd(t)
         dma("s", T.aw[:, 0:128], arrival, "dc", "arr%d" % t, "aw")
         unpack(T.ql[:, 8:16], T.nxl[:, 0:8], "nxa", "ql1")
-        first = slots(T.nxl[:, 0:8], "nxa", x, 1, 2, xs)
-        first[0]()
-        scatter(pos, pn, T.ql[:, 8:16], T.vh[:, 0:128], "ql1 vh1")
         tt(T.pf[:, 0, :, :, 1], T.mu[:, 160:168], T.voi[:, 0:8], Op.mult, "mu voi", "pf")
-        first[1]()
-        cp("v", T.pf[:, 1, :, :, 1], T.wl[:, 0:8], "wa", "pf")
-        first[2]()
-        if t == 0:
-            cp("v", half(7), S, "ss", "sc")
-        else:
-            tt(half(7), half(7), S, Op.not_equal, "sc ss", "sc")
         if t == 0:
             later_constants()
+        sums([(T.pg[:, 40:60, :, :], am[4], T.idc[:, :]), (T.pg[:, 40:50, :, :], am[6], S), (T.pg[:, 50:60, :, :], am[7], S)], "idc ss", "pg")
+        if t == 0:
             masks()
-            op("a", lambda: A.activation(T.vs[:, 0, 0:128], T.vh[:, 256:384], Act.Identity, bias=col(cH16)), "vh3 c0", "vs0")
-            op("a", [(lambda j=j: A.activation(T.vs[:, j, 0:128], T.vs[:, 0, 0:128], Act.Identity, bias=256.0 * j))
-                     for j in range(1, 11)], "vs0", "vs")
-        first[3]()
+        scatter(pos, pn, T.ql[:, 8:16], T.vh[:, 0:128], "ql1 vh1")
+        cp("a", T.pf[:, 1, :, :, 1], T.wl[:, 0:8], "wa", "pf")
+        if t == 0:
+            cp("v", SCR, S, "ss", "sc")
+        else:
+            tt(SCR, SCR, S, Op.not_equal, "sc ss", "sc")
         if not last:
-            spread(T.mu1[:, 0:160], T.z1, x, 0, "z1 " + xs, "mu1")
-            spread(T.mud[:, 0:160], T.zd, x, 0, "zd " + xs, "mud")
-        if t == R - 2:
-            unpack(T.npu[:, :], T.nxl[:, 0:160], "nxa nxb", "npu")
-            scatter(T.pos2, "pos2", T.npu[:, 0:48], T.dfl[:, 0:768], "npu dfl")
-        if not last:
-            ts(px(1), S, 1280.0, Op.mult, "ss", "px1")
-            tt(half(8), T.vv[:, b_], T.vv[:, a_], Op.subtract, "va vb", "dv")
-            tt(px(3), half(10), S, Op.mult, "ab ss", "px3")
-            tt(px(0), half(8), S, Op.mult, "dv ss", "px0")
+            tt(px(1), T.vv[:, b_], T.vv[:, a_], Op.subtract, "va vb", "px1")
+            tt(px(3), AB, S, Op.mult, "ab ss", "px3")
+            tt(px(0), px(1), S, Op.mult, "px1 ss", "px0")
             tt(px(4), px(3), T.dd[:, a_], Op.subtract, "px3 dda", "px4")
             tt(px(5), T.dd[:, b_], px(3), Op.subtract, "px3 ddb", "px5")
-            tt(T.bs[:, a_], T.nxl[:, a_], px(1), Op.subtract, "nxa px1", "ba")
-            tt(T.bs[:, b_], T.nxl[:, b_], px(1), Op.add, "nxb px1", "bb")
-            tt(T.c1[:, :], T.sx[:, 320:480], T.m1[:, :], Op.mult, "m1s px4 px5", "c1")
-            tt(T.c2[:, :], T.sx[:, 320:480], T.m2[:, :], Op.mult, "m2s px4 px5", "c2")
             tt(T.vv[:, a_], T.vv[:, a_], px(0), Op.add, "va px0", "va")
             tt(T.vv[:, b_], T.vv[:, b_], px(0), Op.subtract, "vb px0", "vb")
-            tt(T.dfp[:, a_], T.idc[:, a_], px(1), Op.add, "idc px1", "dfa")
-            tt(T.dfp[:, b_], T.idc[:, b_], px(1), Op.subtract, "idc px1", "dfb")
-            tt(half(0), T.bs[:, b_], T.bs[:, a_], Op.subtract, "ba bb", "dn")
+            act(T.vp[:, :], T.vv[:, :], Act.Relu, "va vb", "vp")
+            act(T.m0[:, :], T.vp[:, :], Act.Sign, "vp", "m0")
+            tt(T.c1[:, :], T.sx[:, 320:480], T.m1[:, :], Op.mult, "m1s px4 px5", "c1")
+            tt(T.c2[:, :], T.sx[:, 320:480], T.m2[:, :], Op.mult, "m2s px4 px5", "c2")
         else:
-            tt(half(8), T.nxi[:, b_], T.nxi[:, a_], Op.subtract, "nxi", "dv")
-            tt(half(9), half(8), half(7), Op.mult, "dv sc", "t9")
-            tt(T.yo[:, a_], T.nxi[:, a_], half(9), Op.add, "nxi t9", "yoa")
-            tt(T.yo[:, b_], T.nxi[:, b_], half(9), Op.subtract, "nxi t9", "yob")
-        early = slots(T.pg[:, 2:KB, :, :], "pg", x, 2, KB, xs)
+            tt(half(5), T.nxi[:, b_], T.nxi[:, a_], Op.subtract, "nxi", "dv")
+            tt(px(0), half(5), SCR, Op.mult, "dv sc", "px0")
+            tt(T.yo[:, a_], T.nxi[:, a_], px(0), Op.add, "nxi px0", "yoa")
+            tt(T.yo[:, b_], T.nxi[:, b_], px(0), Op.subtract, "nxi px0", "yob")
+        ts(T.xl[:, 8:16], T.pg[:, 40, :, :], float(CB), Op.subtract, "pg", "xl1")
+        cp("a", T.aw[:, 256:384], x.indirect(T.xl[:, 8:16]), xs + " xl1", "xo1")
+        if t > 1:
+            tt(T.aq[:, :], PF, T.aq[:, :], Op.max, "pg aq", "aq")
+        if not last:
+            cp("a", T.dfp[:, :], T.pg[:, 40:60, :, :], "pg xl1 aq", "dfp")
+            spread(MU1, T.z1, T.xx, XB[t], "z1 " + xs, "mu1")
+        else:
+            ts(T.q3[:, 160:168], T.idn[:, 0:8], float(2560 + CB + 128), Op.add, "idn", "q3o")
+        if not last:
+            spread(MU2, T.zd, T.xx, XB[t], "zd " + xs, "mu1")
+        early = {k1: slots(T.pf[:, k0:k1, :, :, 0], "pf", x, k0, k1, xs) for k0, k1 in zip(KS, KS[1:])}
         for k in range(1, 23):
             e = k + 1
             rp = [T.rep[:, 128 * (k % 2) + 64 * u:128 * (k % 2) + 64 * u + 64] for u in range(2)]
             nm = ["ql%d" % k, "ql%db" % k if k > 1 else "ql1"]
             for u in range(2):
                 cp("v", rp[u], T.win[:, :].indirect(T.ql[:, 8 * k + 4 * u:8 * k + 4 * u + 4]), WALL + " " + nm[u], "rep%d%d" % (k % 2, u))
-            if e in (KB + 1, KB + 2):
-                early[2 * (e - KB - 1)]()
+            for k1 in early:
+                if e in (k1 + 1, k1 + 2):
+                    early[k1][2 * (e - k1 - 1)]()
             for u in range(2):
                 op("v", lambda: V.transpose(entry(e, u), rp[u]), "rep%d%d" % (k % 2, u), "tt%d%s" % (e, "b" * u))
-            if e == KB + 1:
-                early[1]()
-            for u in range(2):
+            if e - 1 in early:
+                early[e - 1][1]()
+            if e == 23:
+                if not last:
+                    tt(T.u1[:, :], MU1, T.c1[:, :], Op.mult, "mu1 c1", "u1")
+                unpack(T.ql[:, 184:192], T.tto[:, 80:88, 0], "tt23 tt23b", "ql23 ql23b")
+            for u in range(2 * (e < 23)):
                 unpack(T.ql[:, 8 * e + 4 * u:8 * e + 4 * u + 4], entry_q(e, u), "tt%d%s" % (e, "b" * u), "ql%d%s" % (e, "b" * u))
-            if e == 23 and not last:
-                scatter(pos, pn, T.ql[:, 8 * e:8 * e + 8], T.vh[:, 128:256], "ql23 ql23b vh2")
-            elif e >= 22:
-                scatter(pos, pn, T.ql[:, 8 * e:8 * e + 8], T.vs[:, 10, 128 * (e - 22):128 * (e - 21)], "ql%d ql%db vs vo" % (e, e))
-            elif e % 2 == 1:
-                scatter(pos, pn, T.ql[:, 8 * e - 8:8 * e + 8], T.vs[:, (e - 3) // 2, :],
-                        "ql%d ql%db ql%d ql%db vs0 vs vo" % (e - 1, e - 1, e, e))
-            if e == KB + 2:
-                early[3]()
-            if e in (KB - 2, KB - 1):
-                home(2 + e % 2, e, False)
-            if e == KB + 1:
-                home(2, KB, True)
-                home(3, KB + 1, True)
-                op("p", lambda: P.matmul(T.cnt[:, 8:192], T.ib[:, :], T.ot[:, :], True, False), "ib ot", "cnt")
+            if e in (2, 23):
+                vals = T.vh[:, 384:512] if e == 2 else T.vs[:, 10, 0:128] if last else T.vh[:, 128:256]
+                scatter(pos, pn, T.ql[:, 8 * e:8 * e + 8], vals, "ql%d ql%db vs0 vo vh2" % (e, e) if e > 2 else "ql2 ql2b vs0")
+            elif e % 2 == 0:
+                scatter(*((T.pos2, "pos2") if e in (4, 8, 12, 16) else (pos, pn)), T.ql[:, 8 * e - 8:8 * e + 8], T.vs[:, (e - 4) // 2, :],
+                        "ql%d ql%db ql%d ql%db vs vo" % (e - 1, e - 1, e, e))
+            if e - 2 in early:
+                early[e - 2][3]()
+            for k0, k1 in zip(KS, KS[1:]):
+                if e in (k1 - 2, k1 - 1):
+                    home(k0 + e % 2, e)
+            if t == 0 and e == 3:
+                act(T.ot[:, :], T.oti[:, :], Act.Identity, "oti c0", "ot", bias=col(cI))
+            if t == 0 and e in (3, 5, 7, 9, 11):
+                w0 = 8 << (e - 3) // 2
+                cp("a", T.lgx[:, w0:min(2 * w0, 192)], T.lgx[:, 0:min(w0, 192 - w0)], "lgx", "lgx")
+            if e == KS[1] and not last:
+                sums([(BS, am[4], T.nxl[:, 0:160]), (T.pb[:, a_], am[7], S), (T.pb[:, b_], am[6], S)], "nxa nxb ss", "pb")
+                sums([(DN, am[4], T.nxl[:, b_]), (DN, am[5], T.nxl[:, a_]), (DN, am[8], S)], "nxa nxb ss", "pb")
+            if e == KS[1] and t > 0:
+                sums([(PF, am[4], p[:, 0:160]) for p in (T.p1, T.p2, T.p3, T.p4)] + [(PF, am[5], T.ha[:, :])], "p1 p2 p3 p4 ha", "pg")
+            if e == 16:
+                dma("s", T.p3[:, :], T.pos2[0::32, :], "dp2", "pos2r0", "p3")
+                dma("s", T.p4[:, :], T.pos2[16::32, :], "dp2", "pos2r1", "p4")
+                if not last:
+                    reset(T.pos2, "pos2", "dr3")
+            if e == 17:
                 if not last:
                     spread(T.mu[:, 160:168], T.znu, T.arr, 128 * t, "znu arr%d" % t, "mu")
-            if e == 21:
-                home(KB + 3, 21, True)
+                op("p", lambda: P.matmul(T.cnt[:, 8 + sv:192], T.ib[:, :], T.ot[:, sv:184], True, False), "ib ot", "cnt")
+                op("p", lambda: P.matmul(T.mu[:, 264:264 + sv], T.ib[:, :], T.ot[:, 0:sv], True, False), "ib ot", "mu")
+            if e in (21, 22):
+                home(KS[-1] + e % 2, e)
             if e == 22:
-                home(KB + 2, 22, True)
-            if e == 23:
-                home(23, 23, True)
+                op("p", [lambda: P.matmul(PM, am[4], T.p3[:, 0:160], True, False), lambda: P.matmul(PM, am[4], T.p4[:, 0:160], False, False)],
+                   "am4 p3 p4", "pg")
             if e == 3 and last:
                 dma("s", T.yn[:, :], T.yo[:, :], "dy", "yoa yob", "")
                 dma("s", T.y[:, 0:128], arrival, "dy", "arr%d" % t, "")
         dma("s", T.p1[:, :], pos[0::32, :], "dp", pn + "r0", "p1")
         dma("s", T.p2[:, :], pos[16::32, :], "dp", pn + "r1", "p2")
-        if not last:
-            tt(T.u1[:, :], T.mu1[:, 0:160], T.c1[:, :], Op.mult, "mu1 c1", "u1")
-            tt(T.sx[:, 0:160], T.mud[:, 0:160], T.c2[:, :], Op.mult, "mud c2", "px0 px1")
-            ts(T.vp[:, :], T.vv[:, :], 0.0, Op.max, "va vb", "vp")
-            tt(T.u1[:, :], T.u1[:, :], T.sx[:, 0:160], Op.add, "u1 px0 px1", "u1")
-        late = slots(T.pf[:, KB:23, :, :, 0], "pf", x, KB, 23, xs)
-        late[0]()
-        op("v", [(lambda c=c: V.tensor_tensor_scan(T.pt[:, c:192:8], T.one[:, :], T.pf[:, 0:24, c // 2, c % 2, 1], 0.0, Op.mult, Op.add))
-                 for c in range(8)], "pf one", "tt")
-        late[1]()
-        tt(T.uu[:, :], T.pt[:, 0:192], T.lgx[:, :], Op.subtract, "tt lgx", "uu")
-        late[2]()
-        late[3]()
-        for d in range(1, 24):
+        tt(T.uu[:, 0:8], T.tto[:, 80:88, 1], T.lgx[:, 0:8], Op.subtract, "tt23 tt23b lgx", "wl23")
+        late = slots(T.pf[:, KS[-1]:23, :, :, 0], "pf", x, KS[-1], 23, xs)
+        AW = "aw xo0 xo1 " + " ".join("xo%d" % k0 for k0 in KS)
+        for j, (c0, c1) in enumerate(((0, 2), (2, 4), (4, 8))):
+            late[j]()
+            if j == 2:
+                late[3]()
+            op("v", [(lambda c=c: V.tensor_tensor_scan(T.pt[:, c:184:8], T.one[:, 0:23], T.pf[:, 0:23, c // 2, c % 2, 1], 0.0,
+                                                       Op.mult, Op.add)) for c in range(c0, c1)], "pf one", "ts%d" % j)
+        if last:
+            tt(T.q3[:, 0:160], PF, T.aq[:, :], Op.max, "pg aq", "q3")
+        else:
+            tt(T.u2[:, :], MU2, T.c2[:, :], Op.mult, "mu1 c2", "u2")
+        tt(T.uu[:, 184:192], T.pt[:, 176:184], T.uu[:, 0:8], Op.add, "ts0 ts1 ts2 wl23", "ul")
+        tt(T.uu[:, 8:184], T.pt[:, 8:184], T.lgx[:, 8:184], Op.subtract, "ts0 ts1 ts2 lgx", "uu")
+        for d in [23] + list(range(1, 23)):
             cd = T.cnd[:, 184 * (d - 1):184 * (d - 1) + 192 - 8 * d]
-            tt(cd, T.pt[:, 0:192 - 8 * d], T.uu[:, 8 * d:192], Op.is_le, "tt uu", "cd%d" % d)
-            op("p", lambda: P.matmul(T.cnt[:, 8 * d:192], T.i128[:, :], cd, False, d == 23), "i128 cd%d" % d, "cnt")
+            tt(cd, T.pt[:, 0:192 - 8 * d], T.uu[:, 8 * d:192], Op.is_le, "ts0 ts1 ts2 ul" + " uu" * (d < 23), "cd%d" % d)
+            c0, cut = 184 * (d - 1), max(8 * (KA + 1 - d), 0)
+            if cut:
+                op("p", lambda: P.matmul(T.mu[:, 256 + 8 * d:264 + sv], T.i128[:, :], T.cnd[:, c0:c0 + cut], False, d == KA),
+                   "i128 cd%d" % d, "mu")
+            for b in ([d] if d < KA - 3 or d > KA else range(KA - 3, d + 1) if d == KA else []):
+                c0, cut = 184 * (b - 1), max(8 * (KA + 1 - b), 0)
+                op("p", lambda: P.matmul(T.cnt[:, 8 * b + cut:192], T.i128[:, :], T.cnd[:, c0 + cut:c0 + 192 - 8 * b], False, b == 22),
+                   "i128 cd%d" % b, "cnt")
+            if d == KA + 3:
+                cp("v", T.sp[:, 0:sv], T.mu[:, 264:264 + sv], "mu", "spa")
+                if t == 1:
+                    for q in "va":
+                        before(q, [], ["ew"], True)
+                cp("a", xr(t, XP0, XP0 + 16 * sv), T.aw[:, 0:128 * (KA + 1)].indirect(T.sp[:, 0:sv]),
+                   "aw xo0 xo1 spa " + " ".join("xo%d" % k0 for k0 in KS if k0 < KA), xn + "p1")
         if not last:
-            ts(M1, T.vv[:, :], 0.0, Op.is_gt, "va vb", "m1")
-        sv = SV - 4 if last else SV
-        cp("v", T.sp[:, sv:184], T.cnt[:, 8 + sv:192], "cnt", "spa")
-        cp("v", T.sp[:, 0:sv], T.cnt[:, 8:8 + sv], "cnt", "spv")
-        AW = "aw xo0 xo1 xo2 xo%d" % KB
-        if t == 1:
-            for q in "va":
-                before(q, [], ["ew"], True)
-        cp("a", x[:, XP0 + 16 * sv:XW], T.aw[:, :].indirect(T.sp[:, sv:184]), AW + " spa", xn + "p1")
+            tt(T.d1[:, :], DD[2], T.m0[:, :], Op.mult, "pb m0", "d1")
+        cp("v", T.sp[:, sv:184], T.cnt[:, 8 + sv:192], "cnt", "spv")
+        cp("a", xr(t, XP0 + 16 * sv, XP0 + 16 * SA), T.aw[:, :].indirect(T.sp[:, sv:SA]), AW + " spv", xn + "p4")
 
         def part(j, c0, c1):
-            cp("v", x[:, XP0 + 16 * c0:XP0 + 16 * c1], T.aw[:, :].indirect(T.sp[:, c0:c1]), AW + " spv", xn + "p%d" % j)
-        if t < R - 2:
-            reset(pos, pn, "dr")
+            cp("v", xr(t, XP0 + 16 * c0, XP0 + 16 * c1), T.aw[:, :].indirect(T.sp[:, c0:c1]), AW + " spv", xn + "p%d" % j)
+        op("p", [lambda: P.matmul(PM, am[4], T.p1[:, 0:160], False, False), lambda: P.matmul(PM, am[4], T.p2[:, 0:160], False, True)],
+           "am4 p1 p2", "pg")
         if not last:
-            PM = T.pg[:, 0:20, :, :]
-            op("p", [lambda: P.matmul(PM, am[4], T.p1[:, 0:160], True, False),
-                     lambda: P.matmul(PM, am[4], T.p2[:, 0:160], False, True)], "am4 p1 p2", "pg")
-            part(0, 16, sv)
-            tt(T.pm[:, 0:160], PM, T.dfp[:, :], Op.max, "pg dfa dfb", "pm")
-            part(2, 0, 8)
+            reset(pos, pn, "dr")
+            sums([(RR, am[4], u[:, s]) for u in (T.u1, T.u2) for s in (a_, b_)], "u1 u2", "pb")
+            tt(T.oi[:, 0:8], T.p1[:, 160:168], T.p2[:, 160:168], Op.max, "p1 p2", "oi0")
+            part(0, SA, 168)
+            tt(T.pm[:, 0:160], PM, T.dfp[:, :], Op.max, "pg dfp", "pm")
+            part(2, 168, 176)
             ts(T.piu[:, 0:160], T.pm[:, 0:160], float(CB), Op.subtract, "pm", "piu", 0.25, Op.add)
-            part(3, 8, 16)
+            part(3, 176, 184)
+            ts(T.oi[:, 8:16], T.oi[:, 0:8], CB - 1, Op.bitwise_and, "oi0", "oi1")
         else:
-            part(0, 16, sv)
-            tt(T.sx[:, 0:PW], T.p1[:, :], T.p2[:, :], Op.max, "p1 p2", "px0 px1 px2")
-            part(2, 0, 8)
-            ts(T.piu[:, 8:160], T.sx[:, 8:160], float(CB + 128), Op.subtract, "px0 px1", "piu", 0.25, Op.add)
-            cp("v", T.pm[:, 168:176], T.sx[:, 168:176], "px2", "pmt")
-            part(3, 8, 16)
-            tt(T.pm[:, 160:168], T.sx[:, 160:168], T.pm[:, 168:176], Op.max, "px2 pmt", "pmo")
-        xall = "%s %so %sp0 %sp1 %sp2 %sp3 piu" % (xs, xn, xn, xn, xn, xn)
+            tt(T.sx[:, 0:8], T.p1[:, 160:168], T.p2[:, 160:168], Op.max, "p1 p2", "px0")
+            part(0, SA, 168)
+            tt(T.pm[:, 0:160], PM, T.q3[:, 0:160], Op.max, "pg q3", "pm")
+            tt(T.pm[:, 160:168], T.sx[:, 0:8], T.q3[:, 160:168], Op.max, "px0 q3o", "pmo")
+            part(2, 168, 176)
+            ts(T.piu[:, 8:168], T.pm[:, 8:168], XB[t] - CB - 128 + 0.25, Op.add, "pm pmo", "piu")
+            part(3, 176, 184)
+        xall = "%s %so %sp0 %sp1 %sp2 %sp3 %sp4 piu" % (xs, xn, xn, xn, xn, xn, xn)
         if not last:
             dma("s", T.aw[:, 128:256], arrival, "dk", "arr%d" % t, "xo0")
             if t == 0:
                 for q in "va":
-                    before(q, [], ["vw"], True)
-            four(y, yn + "s", x[:, :], T.piu, xall)
-            contents(T.mu, "mu", T.znu, "znu", y, yn + "s")
+                    before(q, [], ["vw", "vw2"], True)
+            gathers(T.xx, XB[t + 1], yn + "s", xr(t, 0, XW), T.piu, xall, CUT, "vava")
+            contents(t + 1)
+            act(T.ha[:, :], PM, Act.Abs, "pg pm", "ha", bias=-float(XW - 64))
+            first_half(lambda: cp("v", T.piu[:, 160:168], T.oi[:, 8:16], "oi1", "pio"))
+            act(T.hb[:, :], T.ha[:, :], Act.Relu, "ha", "hb", bias=200000.0, scale=-1000.0)
+            if t == 0:
+                act(T.aq[:, :], T.idn[:, :], Act.Identity, "idn", "aq", bias=float(CB + 128 - XB[R - 1]))
+            act(T.ha[:, :], T.hb[:, :], Act.Relu, "hb", "ha", bias=float(CB + 128), scale=-1.0)
+            cp("a", xr(t + 1, 2560, 2688), xr(t, 0, XW).indirect(T.piu[:, 160:168]), xall + " pio", yn + "o")
+            act(T.ha[:, :], T.ha[:, :], Act.Identity, "ha", "ha", bias=float(XB[R - 1] - XB[t] - CB - 128))
             if t < R - 2:
                 masks()
-            tt(T.pm[:, 160:176], T.p1[:, 160:176], T.p2[:, 160:176], Op.max, "p1 p2", "pmt")
-            tt(T.d1[:, :], M1, T.dd[:, :], Op.mult, "m1 dda ddb", "d1")
-            tt(T.pm[:, 160:168], T.pm[:, 160:168], T.pm[:, 168:176], Op.max, "pmt", "pmo")
-            tt(half(3), T.u1[:, a_], T.u1[:, b_], Op.add, "u1", "rr")
-            ts(T.p1[:, 160:168], T.pm[:, 160:168], float(CB), Op.is_lt, "pmo", "p1", float(CB + SMALL), Op.mult)
-            tt(T.pm[:, 160:168], T.pm[:, 160:168], T.p1[:, 160:168], Op.add, "pmo p1", "pmo")
-            ts(T.piu[:, 160:168], T.pm[:, 160:168], float(CB), Op.subtract, "pmo", "pio", 0.25, Op.add)
-            cp("a", y[:, 2560:2688], x[:, :].indirect(T.piu[:, 160:168]), xall + " pio", yn + "o")
-            send_fwd(t + 1)
-            if t == R - 2:
-                scatter(T.pos2, "pos2", T.npu[:, 48:160], T.dfl[:, 768:2560], "npu dfl")
         else:
-            for j in range(6):
-                if j == 2:
-                    ts(T.piu[:, 160:168], T.pm[:, 160:168], float(CB + 128), Op.subtract, "pmo", "pio", 0.25, Op.add)
-                cp("va"[j % 2], T.xn[:, 16 * YC[j]:16 * YC[j + 1]], x[:, :].indirect(T.piu[:, YC[j]:YC[j + 1]]),
-                   xall + " pio" * (j == 5), "y%d" % j)
+            for j in range(len(YC) - 1):
+                cp("va"[j % 2], T.gb[:, 16 * YC[j]:16 * YC[j + 1]], T.xx[:, :].indirect(T.piu[:, YC[j]:YC[j + 1]]), xall, "y%d" % j)
                 if j % 2:
                     c = slice(16 * YC[j - 1], 16 * YC[j + 1])
-                    dma("s", T.y[:, c], T.xn[:, c], "dy", "y%d y%d" % (j - 1, j), "")
+                    dma("s", T.y[:, c], T.gb[:, c], "dy", "y%d y%d" % (j - 1, j), "")
     for s in sorted(cnt):
         need("g", (s, cnt[s], {}, None), True)

from concourse.bass import DstId, RemoteDMATransfer
from concourse.mybir import AluOpType as Op
from concourse.mybir import ActivationFunctionType as Act

R = 4
PW = 176
ROW = 32 * PW
XP0 = 2688
XW = XP0 + 23 * 128
XB = [2688 + t * XW for t in range(R + 1)]
VW = XB[1]
EW = VW + 16 * PW
CB = 32768
KA = 8
SA = 126
KS = (2, 10)
PK = 4096
QC, SC = ROW // 2, 1280
RND = 1.5 * 2.0 ** 23 * PK
YC = (8, 20, 32, 64, 96, 122, 148, 158, 168)
CUT = (0, 40, 80, 120, 160)
CUTX = (0, 80, 80, 120, 160)

F, H, I, U = "float32", "bfloat16", "int32", "uint16"
SCRATCH = {
    "xx": ("sbuf", [128, XB[R]], H), "aq": ("sbuf", [128, 160], F), "q3": ("sbuf", [128, 168], F),
    "ha": ("sbuf", [128, 160], F), "hb": ("sbuf", [128, 160], F),
    "aw": ("sbuf", [128, 128 + 23 * 128], H), "arr": ("sbuf", [128, R * 128], H),
    "pk": ("sbuf", [128, 144], H), "gb": ("sbuf", [128, 2688], H), "vlb": ("sbuf", [128, PW], H),
    "rl": ("sbuf", [128, R * 64], H), "rb": ("sbuf", [128, 72], H),
    "win": ("sbuf", [128, ROW], F), "pos": ("sbuf", [128, ROW], F), "pos2": ("sbuf", [128, ROW], F),
    "p3": ("sbuf", [128, PW], F), "p4": ("sbuf", [128, PW], F),
    "vh": ("sbuf", [128, 4 * 128], F), "vs": ("sbuf", [128, 11, 256], F),
    "rep": ("sbuf", [128, 256], F), "tte": ("sbuf", [128, 44, 32], F), "tto": ("sbuf", [128, 88, 16], F),
    "ql": ("sbuf", [128, 192], U), "xl": ("sbuf", [128, 184], U), "sp": ("sbuf", [128, 184], U), "piu": ("sbuf", [128, PW], U),
    "nxu": ("sbuf", [128, 160], U), "viu": ("sbuf", [128, 160], U),
    "nui": ("sbuf", [128, 4], I), "nxi": ("sbuf", [128, 160], I), "lei": ("sbuf", [128, 320], I),
    "voi": ("sbuf", [128, 160], I), "lgi": ("sbuf", [128, 8], I), "ti1": ("sbuf", [128, 160], I), "ti2": ("sbuf", [128, 160], I),
    "pci": ("sbuf", [128, 8], I), "col": ("sbuf", [128, 24], F), "ci": ("sbuf", [128, PW], F), "mg": ("sbuf", [128, 128], F),
    "oti": ("sbuf", [128, 184], F), "ot": ("sbuf", [128, 184], H),
    "z": ("sbuf", [128, 144], H), "znu": ("sbuf", [128, 144], H), "z1": ("sbuf", [128, 144], H), "zd": ("sbuf", [128, 144], H),
    "bnu": ("sbuf", [128, 128], H), "ib": ("sbuf", [128, 128], H), "i128": ("sbuf", [128, 128], H),
    "am": ("sbuf", [128, 9 * 128], F), "hm": ("sbuf", [128, 4 * 128], F),
    "nxl": ("sbuf", [128, PW], F), "wl": ("sbuf", [128, PW], F), "idc": ("sbuf", [128, 160], F),
    "oi": ("sbuf", [128, 16], I), "sm": ("sbuf", [128, 184], F), "pg": ("psum", [128, 64, 4, 2], F),
    "rs": ("sbuf", [128, PW], F), "rz": ("sbuf", [128, PW], F), "idn": ("sbuf", [128, 160], F),
    "p1": ("sbuf", [128, PW], F), "p2": ("sbuf", [128, PW], F),
    "pm": ("sbuf", [128, PW], F), "dd": ("sbuf", [128, 160], F), "d1": ("sbuf", [128, 160], F), "vv": ("sbuf", [128, 160], F),
    "vp": ("sbuf", [128, 160], F), "wv": ("sbuf", [128, 160], F), "dfp": ("sbuf", [128, 160], F),
    "c1": ("sbuf", [128, 160], F), "c2": ("sbuf", [128, 160], F), "u1": ("sbuf", [128, 160], F), "u2": ("sbuf", [128, 160], F),
    "m0": ("sbuf", [128, 160], F), "m1": ("sbuf", [128, 160], F), "m2": ("sbuf", [128, 160], F),
    "h": ("sbuf", [128, 8 * 80], F), "lgx": ("sbuf", [128, 192], F), "uu": ("sbuf", [128, 192], F),
    "one": ("sbuf", [128, 24], F), "cnd": ("sbuf", [128, 23 * 184], H), "tb": ("sbuf", [128, 128], H), "tf": ("sbuf", [128, 128], F),
    "yo": ("sbuf", [128, 160], F),
    "mu": ("psum", [128, 512], F), "mu1": ("psum", [128, 512], F), "pb": ("psum", [128, 512], F), "sx": ("psum", [128, 512], F),
    "pf": ("psum", [128, 32, 4, 2, 2], F), "pt": ("psum", [128, 512], F), "cnt": ("psum", [128, 512], F),
}
SEMAPHORES = (["cv", "ca", "cp", "cg", "ld0", "ld1", "ld2", "ld3", "ld4", "ld5", "dv", "dc", "dk", "dw", "dp", "dp2", "dr", "dr2", "dr3", "dy",
               "back", "sb", "rback", "rsb"]
              + ["a%d" % t for t in range(R)] + ["s%d" % t for t in range(R)]
              + ["ra%d" % t for t in range(R)] + ["rs%d" % t for t in range(R)])


def _bits(engines):
    m = 0
    for e in engines:
        m |= 1 << e
    return m


def _relay(src, dst, T, topo):
    if topo.may_write(src, dst):
        return None
    c = [k for k in topo.cores_of(src) if T.rank_of(k) is None and topo.may_write(k, dst)]
    c.sort(key=lambda k: (topo.die(k) != topo.die(src), k))
    return c[0]


def _relay_program(g, core, T, topo):
    n = len(T.cores)
    jobs = []
    for r in range(n):
        src = T.cores[r]
        for step in (1, 2):
            dst = T.cores[(r - step) % n]
            if _relay(src, dst, T, topo) == core:
                c0 = EW + 72 * (step - 1)
                jobs.append((1, dst, T.xx[:, c0:c0 + 72], T.rb[:, :], "rback", "back", "rsb"))
            dst = T.cores[(r + step) % n]
            if _relay(src, dst, T, topo) == core:
                for t in range(R):
                    c0 = 128 * t + 64 * (step - 1)
                    jobs.append((2 * t, dst, T.arr[:, c0:c0 + 64], T.rl[:, 64 * t:64 * t + 64], "ra%d" % t, "a%d" % t, "rs%d" % t))
    jobs.sort(key=lambda j: j[0])
    for turn, dst, there, here, came, lands, sent in jobs:
        rid, pid = topo.addr(dst, core)
        g.wait_ge(T.sem[came], 8)
        g.remote_dma(there, here, T.sem[lands], T.sem[sent], pid, rid, _bits(topo.engines(core, dst)[:8]))
    for job in jobs:
        g.wait_ge(T.sem[job[6]], 8)


def rank_program(g, core, T, topo):
    rank = T.rank_of(core)
    if rank is None:
        _relay_program(g, core, T, topo)
        return
    n = len(T.cores)
    Q = {"v": g.vector, "a": g.scalar, "p": g.tensor, "g": g, "s": g.sync}
    V, A, P = g.vector, g.scalar, g.tensor
    CS = {"v": "cv", "a": "ca", "p": "cp", "g": "cg"}
    cnt, know, lastw, readers, batch = {}, {q: {} for q in Q}, {}, {}, {}

    def need(q, ev, raw):
        sem, val, clock, eng = ev
        if eng == q == "p" and not raw:
            return
        if isinstance(val, list):
            if not val:
                val.append(cnt[sem])
            val = val[0]
        if know[q].get(sem, 0) < val:
            Q[q].wait_ge(T.sem[sem], val)
            know[q][sem] = val
        for s, v in clock.items():
            if know[q].get(s, 0) < v:
                know[q][s] = v

    def before(q, rd, wr, compute):
        for x in rd:
            if x in lastw:
                need(q, lastw[x], True)
        for x in wr:
            if x in lastw:
                need(q, lastw[x], not compute)
            for ev in readers.get(x, []):
                need(q, ev, not compute)

    def after(ev, rd, wr):
        for x in rd:
            readers.setdefault(x, []).append(ev)
        for x in wr:
            lastw[x] = ev
            readers[x] = []

    def op(q, fns, rd, wr):
        rd, wr = rd.split(), wr.split()
        before(q, rd, wr, True)
        ins = None
        for f in (fns if isinstance(fns, list) else [fns]):
            ins = f()
        s = CS[q]
        cnt[s] = cnt.get(s, 0) + 1
        ins.then_inc(T.sem[s], 1)
        after((s, cnt[s], dict(know[q]), q), rd, wr)

    def dma(q, out, in_, sem, rd, wr):
        rd, wr = rd.split(), wr.split()
        before(q, rd, wr, False)
        Q[q].dma_start(out, in_).then_inc(T.sem[sem], 16)
        cnt[sem] = cnt.get(sem, 0) + 16
        if batch.get(sem, [0]):
            batch[sem] = []
        after((sem, batch[sem], dict(know[q]), None), rd, wr)

    def landed(sem, regions):
        cnt[sem] = 16
        for x in regions.split():
            lastw[x] = (sem, 16, {}, None)

    def send(dsts, srcs, outs, relay_out, rsem, relay_sem, lsem, rd):
        rd = rd.split()
        before("g", rd, [], False)
        used, trs = [], []
        order = sorted(range(2), key=lambda j: _relay(core, dsts[j], T, topo) is not None)
        for j in order:
            rel = _relay(core, dsts[j], T, topo)
            to = dsts[j] if rel is None else rel
            eng = [e for e in topo.engines(core, to) if e not in used][:8]
            used += eng
            rid, pid = topo.addr(to, core)
            trs.append(RemoteDMATransfer(dst_ids=[DstId(rid=rid, pnc=pid)], dma_engine_mask=_bits(eng),
                                         remote_sem=T.sem[rsem if rel is None else relay_sem],
                                         src=srcs[j], dst=outs[j] if rel is None else relay_out))
        g.remote_dma_fused(trs, local_sem=T.sem[lsem])
        cnt[lsem] = 16
        after((lsem, 16, dict(know["g"]), None), rd, [])

    def tt(out, a, b, o, rd, wr):
        op("v", lambda: V.tensor_tensor(out, a, b, o), rd, wr)

    def ts(out, a, s1, o1, rd, wr, s2=None, o2=None):
        if o2 is None:
            op("v", lambda: V.tensor_scalar(out, a, s1, None, o1), rd, wr)
        else:
            op("v", lambda: V.tensor_scalar(out, a, s1, s2, o1, o2), rd, wr)

    def cp(q, out, in_, rd, wr):
        if q == "v":
            op("v", lambda: V.tensor_copy(out, in_), rd, wr)
        else:
            op("a", lambda: A.activation(out, in_, Act.Copy), rd, wr)

    def fill(ap, c, wr):
        op("v", lambda: V.memset(ap, c), "", wr)

    def iota(out, pattern, base, cm, wr):
        op("g", lambda: g.iota(out, pattern, base, cm, allow_small_or_imprecise_dtypes=True), "", wr)

    def spread(out, zt, src, s0, rd, wr):
        s1 = s0 + 16 * out.shape[1]
        op("p", [(lambda i=i: P.matmul(out, zt[:, 15 - i:143 - i], src[:, s0 + i:s1:16], i == 0, i == 15)) for i in range(16)], rd, wr)

    def col(j):
        return T.col[:, j:j + 1]

    def half(j):
        return T.h[:, 80 * j:80 * j + 80]

    def px(j):
        return T.sx[:, 80 * j:80 * j + 80]

    a_, b_ = slice(0, 80), slice(80, 160)


    def xr(t, c0, c1):
        return T.xx[:, XB[t] + c0:XB[t] + c1]
    fwd = [T.cores[(rank + 1) % n], T.cores[(rank + 2) % n]]
    bwd = [T.cores[(rank - 1) % n], T.cores[(rank - 2) % n]]
    landed("back", "ew")
    for t in range(R):
        landed("a%d" % t, "arr%d" % t)

    dma("s", xr(0, 2560, 2688), T.x[:, 2560:2688], "ld4", "", "x0o")
    dma("a", T.nui[:, 0:1], T.nu[:, :], "ld0", "", "nui")
    dma("a", T.aw[:, 128:256], T.x[:, 0:128], "ld0", "", "xo0")
    dma("s", T.nxi[:, :], T.nx[:, :], "ld1", "", "nxi")
    dma("a", T.voi[:, :], T.vol[:, :], "ld5", "", "voi")
    dma("s", T.xx[:, 0:2688], T.x[:, :], "ld2", "", "xn")

    def send_fwd(t):
        send(fwd, [xr(t, 2560, 2624), xr(t, 2624, 2688)], [T.arr[:, 128 * t:128 * t + 64], T.arr[:, 128 * t + 64:128 * t + 128]],
             T.rl[:, 64 * t:64 * t + 64], "a%d" % t, "ra%d" % t, "s%d" % t, "x%do" % t)

    op("g", lambda: g.iota(T.pci[:, 0:1], [[1, 1]], 0, 1), "", "pci0")
    iota(T.mg[:, :], [[1, 8], [0, 16]], 0, 0, "mg")
    iota(T.ci[:, :], [[1, PW]], 0, 0, "ci")
    send_fwd(0)
    fill(T.xx[:, VW:VW + QC // 2], 0.0, "vw")
    op("a", [(lambda j=j: A.activation(T.win[:, j:j + QC // 2], T.xx[:, VW:VW + QC // 2], Act.Copy)) for j in (0, QC // 2)], "vw", "win0")
    ts(T.pci[:, 1:2], T.pci[:, 0:1], 15, Op.bitwise_and, "pci0", "pci1")
    ts(T.pci[:, 2:3], T.pci[:, 0:1], 4, Op.logical_shift_right, "pci0", "pci2")
    ts(T.pci[:, 3:4], T.pci[:, 0:1], 16, Op.bitwise_and, "pci0", "pci3")
    ts(T.pci[:, 4:5], T.pci[:, 0:1], 31, Op.bitwise_and, "pci0", "pci4")
    fill(T.pk[:, :], 0.0, "pk")
    cP, cI, cG, cH16, cI32, cOD, cS0, cSG, cNU, cH, cNH, cPP, cPM, cPI, cHO, cND = range(16)
    cp("v", T.col[:, 0:5], T.pci[:, 0:5], "pci0 pci1 pci2 pci3 pci4", "c0")
    cp("v", col(cNU), T.nui[:, 0:1], "nui", "cnu")
    ts(col(cOD), col(cI), 1.0, Op.is_equal, "c0", "cod")
    ts(col(cS0), col(cI), 0.0, Op.is_equal, "c0", "cs0")

    ts(T.bnu[:, :], T.mg[:, :], col(cG), Op.is_equal, "mg c0 cnu", "bnu", col(cNU), Op.mult)
    tt(col(cSG), col(cS0), col(cOD), Op.subtract, "cod cs0", "csg")
    op("p", lambda: P.matmul(T.cnt[:, 0:128], T.bnu[:, :], T.aw[:, 128:256], True, True), "bnu xo0", "cnt")
    cp("v", T.pk[:, 0:1], col(cNU), "cnu pk", "pk0")
    cp("v", T.pk[:, 136:137], col(cNU), "cnu pk", "pk1")
    fill(T.vlb[:, :], 0.0, "vlb")
    ts(T.tb[:, :], T.cnt[:, 0:128], col(cSG), Op.mult, "cnt csg", "tb")
    ts(T.tf[:, :], T.cnt[:, 0:128], col(cOD), Op.mult, "cnt cod", "tf")
    fill(T.z[:, :], 0.0, "z")
    tt(T.pk[:, 8:136], T.tf[:, :], T.tb[:, :], Op.add, "tb tf pk", "pk2")
    send(bwd, [T.pk[:, 0:72], T.pk[:, 72:144]], [T.xx[:, EW:EW + 72], T.xx[:, EW + 72:EW + 144]], T.rb[:, :],
         "back", "rback", "sb", "pk pk0 pk1 pk2")
    am = [T.am[:, 128 * j:128 * j + 128] for j in range(9)]
    low, high, ones, full = (T.hm[:, 128 * j:128 * j + 128] for j in range(4))

    def diagonal(out, src, shift, rd, wr):
        op("g", lambda: g.affine_select(out, src, [[-1, 128]], Op.is_equal, 0.0, shift, 1), rd, wr)
    iota(T.hm[:, 256:512], [[127, 2], [0, 128]], 1, 0, "hm2")
    diagonal(am[4], ones, 0, "hm2", "am4")
    iota(T.rs[:, :], [[0, PW]], 0, 0, "rs0")
    iota(T.rz[:, :], [[0, PW]], 0, 0, "rz")
    iota(T.vh[:, 256:384], [[32, 4], [0, 2], [1, 16]], XP0 + CB + 256, 0, "vh3")
    iota(T.win[:, 4512:ROW], [[0, ROW - 4512]], 0, 0, "win2")
    iota(T.vh[:, 0:128], [[1, 128]], XP0 + CB + 128, 0, "vh1")
    iota(T.vs[:, :, 0:128], [[256, 11], [1, 128]], XP0 + CB + 384, 0, "vo")
    iota(low, [[0, 4], [-1, 2], [0, 16]], 1, 0, "hm0")
    iota(high, [[0, 4], [1, 2], [0, 16]], 0, 0, "hm1")
    iota(T.oti[:, :], [[0, 23], [16, 8]], 0, 0, "oti")
    for out, src, shift, nm in ((am[0], low, 0, "am0"), (am[1], high, 16, "am1"), (am[2], low, -16, "am2"), (am[3], high, 0, "am3"),
                                (T.ib[:, :], ones, 0, "ib"), (T.i128[:, :], full, 0, "i128")):
        diagonal(out, src, shift, "hm0 hm1 hm2", nm)
    iota(T.vh[:, 128:256], [[1, 128]], XP0 + 22 * 128, 0, "vh2")
    iota(T.one[:, :], [[0, 24]], 1, 0, "one")

    cp("v", T.nxu[:, :], T.nxi[:, :], "nxi", "nxu")
    cp("v", T.vlb[:, 0:160], T.voi[:, :], "voi vlb", "vlb")
    fill(T.xx[:, VW + QC // 2:EW], 0.0, "vw2")
    dma("s", T.xx[0::16, VW:EW], T.vlb[:, :], "dv", "vlb", "vw vw2")
    before("s", [], ["pk2"], False)
    dma("s", T.lei[:, :], T.le[:, :], "ld3", "", "lei")
    dma("s", T.lgi[:, :], T.lag[:, :], "ld3", "", "lgi")
    ts(T.z[:, 15:143:16], T.ci[:, 0:8], col(cG), Op.is_equal, "ci c0 z", "z")
    ts(T.ti1[:, :], T.nxi[:, :], 4, Op.logical_shift_right, "nxi", "ti1")
    ts(T.ti2[:, :], T.nxi[:, :], 15, Op.bitwise_and, "nxi", "ti2")
    ts(T.znu[:, :], T.z[:, :], col(cNU), Op.mult, "z cnu", "znu")
    AB, SCR = T.pt[:, 256:336], T.pt[:, 336:416]
    BS, DN, RR = T.pb[:, 0:160], T.pb[:, 160:240], T.pb[:, 240:320]
    DD = T.pb[:, 320:400], T.pb[:, 400:480], T.pb[:, 320:480]
    MU1, MU2 = T.mu1[:, 0:160], T.mu1[:, 256:416]
    ts(T.m2[:, :], T.nxi[:, :], 2560.0, Op.is_ge, "nxi", "m2s")
    ts(T.sx[:, 0:160], T.ti2[:, :], float(PW), Op.mult, "ti2", "px0 px1")
    ts(T.sx[:, 160:320], T.nxi[:, :], float(EW - VW + 8 - 2560), Op.add, "nxi", "px2 px3")
    spread(T.mu[:, 160:168], T.znu, T.aw, 128, "znu xo0", "mu")
    tt(T.p1[:, 0:160], T.sx[:, 0:160], T.ti1[:, :], Op.add, "px0 px1 ti1", "p1")
    tt(T.sx[:, 160:320], T.sx[:, 160:320], T.m2[:, :], Op.mult, "px2 px3 m2s", "px2 px3")
    ts(col(cHO), col(cH16), float(PW * PK), Op.mult, "c0", "cho", -float(QC * PK + SC), Op.add)
    tt(T.pm[:, 0:160], T.sx[:, 160:320], T.p1[:, 0:160], Op.max, "px2 px3 p1", "pm")
    ts(col(cPI), col(cI32), float(PW * PK), Op.mult, "c0", "cpi", -float(QC * PK), Op.add)
    cp("v", T.viu[:, :], T.pm[:, 0:160], "pm", "viu")

    def gathers(out, o0, name, window, offs, rd, cut, queues):
        for j in range(4):
            if cut[j] < cut[j + 1]:
                cp(queues[j], out[:, o0 + 16 * cut[j]:o0 + 16 * cut[j + 1]], window.indirect(offs[:, cut[j]:cut[j + 1]]), rd,
                   "%s%d" % (name, j))

    MUA, MUB = T.mu[:, a_], T.mu1[:, 160:240]

    def contents(t):
        spread(MUA, T.znu, T.xx, XB[t], "znu x%ds0 x%ds1" % (t, t), "mu")
        spread(MUB, T.znu, T.xx, XB[t] + 1280, "znu x%ds2 x%ds3" % (t, t), "mu1")

    def first_half(first):
        first()
        tt(half(2), MUA, T.d1[:, a_], Op.mult, "mu d1", "h2")
        tt(T.wv[:, a_], MUA, T.vp[:, a_], Op.mult, "mu vp", "wva")
        tt(half(1), half(2), RR, Op.subtract, "h2 pb", "h1")

    def act(out, in_, func, rd, wr, **how):
        op("a", lambda: A.activation(out, in_, func, **how), rd, wr)

    def sums(terms, rd, wr):
        op("p", [(lambda j=j: P.matmul(terms[j][0], terms[j][1], terms[j][2], j == 0, j == len(terms) - 1)) for j in range(len(terms))],
           rd + " am4 amx", wr)

    act(T.idn[:, :], T.ci[:, 0:160], Act.Identity, "ci c0", "idn", scale=16.0, bias=col(cI))
    gathers(T.xx, XB[0], "x0s", T.xx[:, 0:2688], T.nxu, "xn nxu", CUTX, "aava")
    contents(0)
    WALL = "win0 win1 win2 wf0 wf1 wf2 wf3"

    def reset(buf, nm, sem):
        dma("s", buf[0::32, :], (T.rs if nm == "pos" else T.rz)[:, :], sem, "rs0 rs1 rs2" if nm == "pos" else "rz", nm + "r0")
        dma("s", buf[16::32, :], T.rz[:, :], sem, "rz", nm + "r1")
    act(T.rs[:, 160:168], T.idn[:, 0:8], Act.Identity, "idn rs0", "rs1", bias=2560.0)
    act(T.rs[:, 0:8], T.idn[:, 0:8], Act.Identity, "idn rs0", "rs2", bias=float(XP0 + CB))
    reset(T.pos2, "pos2", "dr3")
    reset(T.pos, "pos", "dr")
    cp("a", T.wl[:, 160:PW], T.rz[:, 0:16], "rz", "wo")
    dma("s", T.win[:, QC:4512], T.win[:, 0:4512 - QC], "dr2", "win0 ew", "win1")
    gathers(T.gb, 0, "gb", T.xx[:, VW:EW + 144], T.viu, "vw vw2 ew viu", CUT, "vava")
    spread(T.mu1[:, a_], T.z, T.gb, 0, "z gb0 gb1", "mu1")
    spread(T.mu1[:, b_], T.z, T.gb, 1280, "z gb2 gb3", "mu1")
    act(T.m1[:, :], T.m2[:, :], Act.Identity, "m2s", "m1s", scale=-1.0, bias=1.0)
    act(T.pm[:, 0:160], T.p1[:, 0:160], Act.Identity, "p1 cho", "pm", scale=float(PK), bias=col(cHO))
    act(half(5), T.pm[:, b_], Act.Identity, "pm", "dv", bias=1280.0)
    op("v", [lambda: V.tensor_tensor(DD[0], T.lei[:, 160:240], T.lei[:, 0:80], Op.subtract),
             lambda: V.tensor_tensor(DD[1], T.lei[:, 240:320], T.lei[:, 80:160], Op.subtract)], "lei", "pb")
    act(T.nxl[:, 160:168], T.ci[:, 168:176], Act.Identity, "ci cpi", "nxo", scale=float(PK), bias=col(cPI))
    act(T.nxl[:, 168:176], T.ci[:, 160:168], Act.Identity, "ci cpi", "nxt", scale=float(PK), bias=col(cPI))
    tt(BS, T.pm[:, 0:160], T.idn[:, :], Op.add, "pm idn", "bs0")
    tt(T.c1[:, :], DD[2], T.m2[:, :], Op.mult, "pb m2s", "c1")
    tt(T.d1[:, :], DD[2], T.m1[:, :], Op.mult, "pb m1s", "d1")
    tt(DN, half(5), T.pm[:, a_], Op.subtract, "pm dv bs0", "dn0")
    tt(half(2), MUA, T.d1[:, a_], Op.mult, "mu d1", "h2")
    cp("a", T.dd[:, :], DD[2], "pb c1 d1 dn0", "dda ddb pbr")
    tt(T.u1[:, :], MU1, T.c1[:, :], Op.mult, "mu1 c1", "u1")
    tt(T.vp[:, :], MU1, T.m1[:, :], Op.mult, "mu1 m1s", "vp")
    tt(px(3), T.u1[:, b_], T.u1[:, a_], Op.subtract, "u1", "px3")
    tt(T.wv[:, a_], MUA, T.vp[:, a_], Op.mult, "mu vp", "wva")
    tt(half(1), half(2), px(3), Op.subtract, "h2 px3 pbr", "h1")
    op("a", [(lambda j=j, c=c: A.activation(am[j], am[4], Act.Identity, scale=c))
             for j, c in ((5, -1.0), (6, 1280.0), (7, -1280.0), (8, 2560.0))], "am4", "amx")
    act(T.idc[:, :], T.idn[:, :], Act.Identity, "idn", "idc", bias=float(CB))
    cp("a", col(cH), T.xx[:, EW:EW + 1], "ew", "ch")
    act(col(cND), T.xx[:, EW:EW + 1], Act.Identity, "ew", "cnd", scale=-2.0, bias=T.xx[:, EW + 136:EW + 137])
    act(T.z1[:, :], T.z[:, :], Act.Identity, "z ch", "z1", scale=col(cH))
    act(T.zd[:, :], T.z[:, :], Act.Identity, "z cnd", "zd", scale=col(cND))
    act(T.vh[:, 384:512], T.vh[:, 256:384], Act.Identity, "vh3 c0", "vs0", bias=col(cH16))
    op("a", [(lambda j=j: A.activation(T.vs[:, j, 128:256], T.vh[:, 384:512], Act.Identity, bias=256.0 * (j + 1))) for j in range(10)],
       "vs0", "vs")
    PF, PM = T.pg[:, 0:20, :, :], T.pg[:, 20:40, :, :]

    def later_constants():
        ts(T.sx[:, 320:480], T.nxi[:, :], 2624.0, Op.is_ge, "nxi", "px4 px5")
        tt(T.vv[:, :], T.vp[:, :], T.sx[:, 320:480], Op.subtract, "vp px4 px5", "va vb")
        tt(AB, T.dd[:, a_], T.dd[:, b_], Op.add, "dda ddb", "ab")
        cp("v", T.lgx[:, 0:8], T.lgi[:, :], "lgi", "lgx")

    def masks():
        act(T.m1[:, :], T.vv[:, :], Act.Relu, "va vb", "m1s", bias=1.0, scale=-1.0)
        act(T.m2[:, :], T.vv[:, :], Act.Relu, "va vb", "m2s", scale=-1.0)

    S = half(0)

    def rows(f, src, q2, rd):
        dma("s", T.win[f::32, :], src[:, :], "dw", rd, "wf%d" % (2 * f))
        dma(q2, T.win[16 + f::32, :], src[:, :], "dw", rd, "wf%d" % (2 * f + 1))

    def unpack(out, in_, rd, wr):
        ts(out, in_, 1.0 / PK, Op.mult, rd, wr, float(QC), Op.add)

    def slots(src, nm, x, k0, k1, rd):
        c = slice(8 * k0, 8 * k1)

        return [lambda: ts(T.sm[:, c], src, RND, Op.add, nm, "sm%d" % k0, RND, Op.subtract),
                lambda: tt(T.sm[:, c], src, T.sm[:, c], Op.subtract, nm + " sm%d" % k0, "sm%d" % k0),
                lambda: ts(T.xl[:, c], T.sm[:, c], float(SC), Op.add, "sm%d" % k0, "xl%d" % k0),
                lambda: cp("a", T.aw[:, 128 * (k0 + 1):128 * (k1 + 1)], x.indirect(T.xl[:, c]), rd + " xl%d" % k0, "xo%d" % k0)]

    def scatter(buf, nm, offs, vals, rd):
        op("a", lambda: A.activation(buf[:, :].indirect(offs), vals, Act.Silu), rd, nm + "r0 " + nm + "r1")

    def entry(k, u):
        j = (k - 2) // 2 * 2 + u
        return T.tte[:, 2 * j:2 * j + 2, :] if k % 2 == 0 else T.tto[:, 4 * j:4 * j + 4, :]

    def entry_q(k, u):
        j = (k - 2) // 2 * 2 + u
        return T.tte[:, 2 * j:2 * j + 2, 0::16] if k % 2 == 0 else T.tto[:, 4 * j:4 * j + 4, 0]

    def home(k0, k1):
        j0, j1 = (k0 - 2) // 2, (k1 - 2) // 2 + 1
        ks = slice(k0, k1 + 1, 2)
        rd = " ".join("tt%d tt%db" % (k, k) for k in range(k0, k1 + 1, 2)) + " am0 am1 am2 am3 am4"
        if k0 % 2 == 0:
            calls = [(lambda hc=hc, hh=hh: P.matmul(T.pf[:, ks, :, hc, :], am[2 * hc + hh], T.tte[:, 4 * j0:4 * j1, 16 * hh:16 * hh + 2],
                                                    hh == 0, hh == 1)) for hc in range(2) for hh in range(2)]
        else:
            calls = [lambda: P.matmul(T.pf[:, ks, :, :, :], am[4], T.tto[:, 8 * j0:8 * j1, 0:2], True, True)]
        op("p", calls, rd, "pf")

    for t in range(R):
        last = t == R - 1
        x, xn, yn = xr(t, 0, 2560), "x%d" % t, "x%d" % (t + 1)
        xs = " ".join("%ss%d" % (xn, j) for j in range(4))
        pos, pn, sv = T.pos, "pos", 8 * KA
        arrival = T.arr[:, 128 * t:128 * t + 128]
        tt(px(0), MUB, T.d1[:, b_], Op.mult, "mu1 d1", "px0")
        tt(px(2), MUB, T.vp[:, b_], Op.mult, "mu1 vp", "px2")
        tt(S, half(1), px(0), Op.is_lt, "h1 px0", "ss")
        tt(px(1), px(2), T.wv[:, a_], Op.subtract, "wva px2", "px1")
        tt(half(3), DN, S, Op.mult, "pb ss", "t5")
        tt(half(4), px(1), S, Op.mult, "px1 ss", "t6")
        tt(T.nxl[:, a_], T.pb[:, a_], half(3), Op.add, "pb t5", "nxa")
        tt(T.nxl[:, b_], T.pb[:, b_], half(3), Op.subtract, "pb t5", "nxb")
        rows(0, T.nxl, "a" if t else "s", "nxa nxb nxo nxt win0 win1 win2")
        tt(T.wl[:, b_], px(2), half(4), Op.subtract, "px2 t6", "wb")
        tt(T.wl[:, a_], T.wv[:, a_], half(4), Op.add, "wva t6", "wa")
        rows(1, T.wl, "a" if t else "s", "wa wb wo")
        if t > 0:
            before("g", WALL.split(), [], False)
            send_fwd(t)
        dma("s", T.aw[:, 0:128], arrival, "dc", "arr%d" % t, "aw")
        unpack(T.ql[:, 8:16], T.nxl[:, 0:8], "nxa", "ql1")
        tt(T.pf[:, 0, :, :, 1], T.mu[:, 160:168], T.voi[:, 0:8], Op.mult, "mu voi", "pf")
        if t == 0:
            later_constants()
        sums([(T.pg[:, 40:60, :, :], am[4], T.idc[:, :]), (T.pg[:, 40:50, :, :], am[6], S), (T.pg[:, 50:60, :, :], am[7], S)], "idc ss", "pg")
        if t == 0:
            masks()
        scatter(pos, pn, T.ql[:, 8:16], T.vh[:, 0:128], "ql1 vh1")
        cp("a", T.pf[:, 1, :, :, 1], T.wl[:, 0:8], "wa", "pf")
        if t == 0:
            cp("v", SCR, S, "ss", "sc")
        else:
            tt(SCR, SCR, S, Op.not_equal, "sc ss", "sc")
        if not last:
            tt(px(1), T.vv[:, b_], T.vv[:, a_], Op.subtract, "va vb", "px1")
            tt(px(3), AB, S, Op.mult, "ab ss", "px3")
            tt(px(0), px(1), S, Op.mult, "px1 ss", "px0")
            tt(px(4), px(3), T.dd[:, a_], Op.subtract, "px3 dda", "px4")
            tt(px(5), T.dd[:, b_], px(3), Op.subtract, "px3 ddb", "px5")
            tt(T.vv[:, a_], T.vv[:, a_], px(0), Op.add, "va px0", "va")
            tt(T.vv[:, b_], T.vv[:, b_], px(0), Op.subtract, "vb px0", "vb")
            act(T.vp[:, :], T.vv[:, :], Act.Relu, "va vb", "vp")
            act(T.m0[:, :], T.vp[:, :], Act.Sign, "vp", "m0")
            tt(T.c1[:, :], T.sx[:, 320:480], T.m1[:, :], Op.mult, "m1s px4 px5", "c1")
            tt(T.c2[:, :], T.sx[:, 320:480], T.m2[:, :], Op.mult, "m2s px4 px5", "c2")
        else:
            tt(half(5), T.nxi[:, b_], T.nxi[:, a_], Op.subtract, "nxi", "dv")
            tt(px(0), half(5), SCR, Op.mult, "dv sc", "px0")
            tt(T.yo[:, a_], T.nxi[:, a_], px(0), Op.add, "nxi px0", "yoa")
            tt(T.yo[:, b_], T.nxi[:, b_], px(0), Op.subtract, "nxi px0", "yob")
        ts(T.xl[:, 8:16], T.pg[:, 40, :, :], float(CB), Op.subtract, "pg", "xl1")
        cp("a", T.aw[:, 256:384], x.indirect(T.xl[:, 8:16]), xs + " xl1", "xo1")
        if t > 1:
            tt(T.aq[:, :], PF, T.aq[:, :], Op.max, "pg aq", "aq")
        if not last:
            cp("a", T.dfp[:, :], T.pg[:, 40:60, :, :], "pg xl1 aq", "dfp")
            spread(MU1, T.z1, T.xx, XB[t], "z1 " + xs, "mu1")
        else:
            ts(T.q3[:, 160:168], T.idn[:, 0:8], float(2560 + CB + 128), Op.add, "idn", "q3o")
        if not last:
            spread(MU2, T.zd, T.xx, XB[t], "zd " + xs, "mu1")
        early = {k1: slots(T.pf[:, k0:k1, :, :, 0], "pf", x, k0, k1, xs) for k0, k1 in zip(KS, KS[1:])}
        for k in range(1, 23):
            e = k + 1
            rp = [T.rep[:, 128 * (k % 2) + 64 * u:128 * (k % 2) + 64 * u + 64] for u in range(2)]
            nm = ["ql%d" % k, "ql%db" % k if k > 1 else "ql1"]
            for u in range(2):
                cp("v", rp[u], T.win[:, :].indirect(T.ql[:, 8 * k + 4 * u:8 * k + 4 * u + 4]), WALL + " " + nm[u], "rep%d%d" % (k % 2, u))
            for k1 in early:
                if e in (k1 + 1, k1 + 2):
                    early[k1][2 * (e - k1 - 1)]()
            for u in range(2):
                op("v", lambda: V.transpose(entry(e, u), rp[u]), "rep%d%d" % (k % 2, u), "tt%d%s" % (e, "b" * u))
            if e - 1 in early:
                early[e - 1][1]()
            if e == 23:
                if not last:
                    tt(T.u1[:, :], MU1, T.c1[:, :], Op.mult, "mu1 c1", "u1")
                unpack(T.ql[:, 184:192], T.tto[:, 80:88, 0], "tt23 tt23b", "ql23 ql23b")
            for u in range(2 * (e < 23)):
                unpack(T.ql[:, 8 * e + 4 * u:8 * e + 4 * u + 4], entry_q(e, u), "tt%d%s" % (e, "b" * u), "ql%d%s" % (e, "b" * u))
            if e in (2, 23):
                vals = T.vh[:, 384:512] if e == 2 else T.vs[:, 10, 0:128] if last else T.vh[:, 128:256]
                scatter(pos, pn, T.ql[:, 8 * e:8 * e + 8], vals, "ql%d ql%db vs0 vo vh2" % (e, e) if e > 2 else "ql2 ql2b vs0")
            elif e % 2 == 0:
                scatter(*((T.pos2, "pos2") if e in (4, 8, 12, 16) else (pos, pn)), T.ql[:, 8 * e - 8:8 * e + 8], T.vs[:, (e - 4) // 2, :],
                        "ql%d ql%db ql%d ql%db vs vo" % (e - 1, e - 1, e, e))
            if e - 2 in early:
                early[e - 2][3]()
            for k0, k1 in zip(KS, KS[1:]):
                if e in (k1 - 2, k1 - 1):
                    home(k0 + e % 2, e)
            if t == 0 and e == 3:
                act(T.ot[:, :], T.oti[:, :], Act.Identity, "oti c0", "ot", bias=col(cI))
            if t == 0 and e in (3, 5, 7, 9, 11):
                w0 = 8 << (e - 3) // 2
                cp("a", T.lgx[:, w0:min(2 * w0, 192)], T.lgx[:, 0:min(w0, 192 - w0)], "lgx", "lgx")
            if e == KS[1] and not last:
                sums([(BS, am[4], T.nxl[:, 0:160]), (T.pb[:, a_], am[7], S), (T.pb[:, b_], am[6], S)], "nxa nxb ss", "pb")
                sums([(DN, am[4], T.nxl[:, b_]), (DN, am[5], T.nxl[:, a_]), (DN, am[8], S)], "nxa nxb ss", "pb")
            if e == KS[1] and t > 0:
                sums([(PF, am[4], p[:, 0:160]) for p in (T.p1, T.p2, T.p3, T.p4)] + [(PF, am[5], T.ha[:, :])], "p1 p2 p3 p4 ha", "pg")
            if e == 16:
                dma("s", T.p3[:, :], T.pos2[0::32, :], "dp2", "pos2r0", "p3")
                dma("s", T.p4[:, :], T.pos2[16::32, :], "dp2", "pos2r1", "p4")
                if not last:
                    reset(T.pos2, "pos2", "dr3")
            if e == 17:
                if not last:
                    spread(T.mu[:, 160:168], T.znu, T.arr, 128 * t, "znu arr%d" % t, "mu")
                op("p", lambda: P.matmul(T.cnt[:, 8 + sv:192], T.ib[:, :], T.ot[:, sv:184], True, False), "ib ot", "cnt")
                op("p", lambda: P.matmul(T.mu[:, 264:264 + sv], T.ib[:, :], T.ot[:, 0:sv], True, False), "ib ot", "mu")
            if e in (21, 22):
                home(KS[-1] + e % 2, e)
            if e == 22:
                op("p", [lambda: P.matmul(PM, am[4], T.p3[:, 0:160], True, False), lambda: P.matmul(PM, am[4], T.p4[:, 0:160], False, False)],
                   "am4 p3 p4", "pg")
            if e == 3 and last:
                dma("s", T.yn[:, :], T.yo[:, :], "dy", "yoa yob", "")
                dma("s", T.y[:, 0:128], arrival, "dy", "arr%d" % t, "")
        dma("s", T.p1[:, :], pos[0::32, :], "dp", pn + "r0", "p1")
        dma("s", T.p2[:, :], pos[16::32, :], "dp", pn + "r1", "p2")
        tt(T.uu[:, 0:8], T.tto[:, 80:88, 1], T.lgx[:, 0:8], Op.subtract, "tt23 tt23b lgx", "wl23")
        late = slots(T.pf[:, KS[-1]:23, :, :, 0], "pf", x, KS[-1], 23, xs)
        AW = "aw xo0 xo1 " + " ".join("xo%d" % k0 for k0 in KS)
        for j, (c0, c1) in enumerate(((0, 2), (2, 4), (4, 8))):
            late[j]()
            if j == 2:
                late[3]()
            op("v", [(lambda c=c: V.tensor_tensor_scan(T.pt[:, c:184:8], T.one[:, 0:23], T.pf[:, 0:23, c // 2, c % 2, 1], 0.0,
                                                       Op.mult, Op.add)) for c in range(c0, c1)], "pf one", "ts%d" % j)
        if last:
            tt(T.q3[:, 0:160], PF, T.aq[:, :], Op.max, "pg aq", "q3")
        else:
            tt(T.u2[:, :], MU2, T.c2[:, :], Op.mult, "mu1 c2", "u2")
        tt(T.uu[:, 184:192], T.pt[:, 176:184], T.uu[:, 0:8], Op.add, "ts0 ts1 ts2 wl23", "ul")
        tt(T.uu[:, 8:184], T.pt[:, 8:184], T.lgx[:, 8:184], Op.subtract, "ts0 ts1 ts2 lgx", "uu")
        for d in [23] + list(range(1, 23)):
            cd = T.cnd[:, 184 * (d - 1):184 * (d - 1) + 192 - 8 * d]
            tt(cd, T.pt[:, 0:192 - 8 * d], T.uu[:, 8 * d:192], Op.is_le, "ts0 ts1 ts2 ul" + " uu" * (d < 23), "cd%d" % d)
            c0, cut = 184 * (d - 1), max(8 * (KA + 1 - d), 0)
            if cut:
                op("p", lambda: P.matmul(T.mu[:, 256 + 8 * d:264 + sv], T.i128[:, :], T.cnd[:, c0:c0 + cut], False, d == KA),
                   "i128 cd%d" % d, "mu")
            for b in ([d] if d < KA - 3 or d > KA else range(KA - 3, d + 1) if d == KA else []):
                c0, cut = 184 * (b - 1), max(8 * (KA + 1 - b), 0)
                op("p", lambda: P.matmul(T.cnt[:, 8 * b + cut:192], T.i128[:, :], T.cnd[:, c0 + cut:c0 + 192 - 8 * b], False, b == 22),
                   "i128 cd%d" % b, "cnt")
            if d == KA + 3:
                cp("v", T.sp[:, 0:sv], T.mu[:, 264:264 + sv], "mu", "spa")
                if t == 1:
                    for q in "va":
                        before(q, [], ["ew"], True)
                cp("a", xr(t, XP0, XP0 + 16 * sv), T.aw[:, 0:128 * (KA + 1)].indirect(T.sp[:, 0:sv]),
                   "aw xo0 xo1 spa " + " ".join("xo%d" % k0 for k0 in KS if k0 < KA), xn + "p1")
        if not last:
            tt(T.d1[:, :], DD[2], T.m0[:, :], Op.mult, "pb m0", "d1")
        cp("v", T.sp[:, sv:184], T.cnt[:, 8 + sv:192], "cnt", "spv")
        cp("a", xr(t, XP0 + 16 * sv, XP0 + 16 * SA), T.aw[:, :].indirect(T.sp[:, sv:SA]), AW + " spv", xn + "p4")

        def part(j, c0, c1):
            cp("v", xr(t, XP0 + 16 * c0, XP0 + 16 * c1), T.aw[:, :].indirect(T.sp[:, c0:c1]), AW + " spv", xn + "p%d" % j)
        op("p", [lambda: P.matmul(PM, am[4], T.p1[:, 0:160], False, False), lambda: P.matmul(PM, am[4], T.p2[:, 0:160], False, True)],
           "am4 p1 p2", "pg")
        if not last:
            reset(pos, pn, "dr")
            sums([(RR, am[4], u[:, s]) for u in (T.u1, T.u2) for s in (a_, b_)], "u1 u2", "pb")
            tt(T.oi[:, 0:8], T.p1[:, 160:168], T.p2[:, 160:168], Op.max, "p1 p2", "oi0")
            part(0, SA, 168)
            tt(T.pm[:, 0:160], PM, T.dfp[:, :], Op.max, "pg dfp", "pm")
            part(2, 168, 176)
            ts(T.piu[:, 0:160], T.pm[:, 0:160], float(CB), Op.subtract, "pm", "piu", 0.25, Op.add)
            part(3, 176, 184)
            ts(T.oi[:, 8:16], T.oi[:, 0:8], CB - 1, Op.bitwise_and, "oi0", "oi1")
        else:
            tt(T.sx[:, 0:8], T.p1[:, 160:168], T.p2[:, 160:168], Op.max, "p1 p2", "px0")
            part(0, SA, 168)
            tt(T.pm[:, 0:160], PM, T.q3[:, 0:160], Op.max, "pg q3", "pm")
            tt(T.pm[:, 160:168], T.sx[:, 0:8], T.q3[:, 160:168], Op.max, "px0 q3o", "pmo")
            part(2, 168, 176)
            ts(T.piu[:, 8:168], T.pm[:, 8:168], XB[t] - CB - 128 + 0.25, Op.add, "pm pmo", "piu")
            part(3, 176, 184)
        xall = "%s %so %sp0 %sp1 %sp2 %sp3 %sp4 piu" % (xs, xn, xn, xn, xn, xn, xn)
        if not last:
            dma("s", T.aw[:, 128:256], arrival, "dk", "arr%d" % t, "xo0")
            if t == 0:
                for q in "va":
                    before(q, [], ["vw", "vw2"], True)
            gathers(T.xx, XB[t + 1], yn + "s", xr(t, 0, XW), T.piu, xall, CUT, "vava")
            contents(t + 1)
            act(T.ha[:, :], PM, Act.Abs, "pg pm", "ha", bias=-float(XW - 64))
            first_half(lambda: cp("v", T.piu[:, 160:168], T.oi[:, 8:16], "oi1", "pio"))
            act(T.hb[:, :], T.ha[:, :], Act.Relu, "ha", "hb", bias=200000.0, scale=-1000.0)
            if t == 0:
                act(T.aq[:, :], T.idn[:, :], Act.Identity, "idn", "aq", bias=float(CB + 128 - XB[R - 1]))
            act(T.ha[:, :], T.hb[:, :], Act.Relu, "hb", "ha", bias=float(CB + 128), scale=-1.0)
            cp("a", xr(t + 1, 2560, 2688), xr(t, 0, XW).indirect(T.piu[:, 160:168]), xall + " pio", yn + "o")
            act(T.ha[:, :], T.ha[:, :], Act.Identity, "ha", "ha", bias=float(XB[R - 1] - XB[t] - CB - 128))
            if t < R - 2:
                masks()
        else:
            for j in range(len(YC) - 1):
                cp("va"[j % 2], T.gb[:, 16 * YC[j]:16 * YC[j + 1]], T.xx[:, :].indirect(T.piu[:, YC[j]:YC[j + 1]]), xall, "y%d" % j)
                if j % 2:
                    c = slice(16 * YC[j - 1], 16 * YC[j + 1])
                    dma("s", T.y[:, c], T.gb[:, c], "dy", "y%d y%d" % (j - 1, j), "")
    for s in sorted(cnt):
        need("g", (s, cnt[s], {}, None), True)
